import numpy as np
import ml_dtypes


def mxq(x, axis, fmt="e4m3"):
    dtype, down = {"e4m3": (ml_dtypes.float8_e4m3fn, 7), "e5m2": (ml_dtypes.float8_e5m2, 14)}[fmt]
    v = np.moveaxis(np.asarray(x, np.float32).astype(ml_dtypes.bfloat16).astype(np.float64), axis, -1)
    blocks = v.reshape(v.shape[:-1] + (-1, 32))
    amax = np.abs(blocks).max(-1, keepdims=True)
    byte = np.maximum(np.where(amax > 0, np.frexp(amax)[1] - 1 + 127, 0) - down, 1)
    scale = np.exp2(byte - 127.0)
    codes = (blocks / scale).astype(np.float32).astype(dtype).astype(np.float64)
    return np.moveaxis((codes * scale).reshape(v.shape), -1, axis)


WIDE = False


def mx_kscale(k):
    if not WIDE:
        return np.ones(k)
    levels = np.array([10, -10, 5, -5, 0])
    if k % 512:
        return np.exp2(np.random.permutation(np.resize(levels, k // 32))).repeat(32)
    a = np.empty((k // 512, 16))
    for p in range(k // 512):
        a[p, :8] = np.random.permutation(np.resize(levels, 8))
        for g in range(8):
            far = levels[np.abs(levels - a[p, g]) >= 10]
            a[p, g + 8] = far[np.random.randint(len(far))]
    return np.exp2(a.ravel()).repeat(32)


def f64(x):
    return np.asarray(x).astype(np.float64)


def striped(idx):
    return np.tile(idx.reshape(-1, 16).T, (8, 1)).astype(np.uint16)


def unstriped(offs):
    return offs[:16].T.reshape(-1).astype(np.int64)


E2M1 = np.array([0.0, 0.5, 1.0, 1.5, 2.0, 3.0, 4.0, 6.0, -0.0, -0.5, -1.0, -1.5, -2.0, -3.0, -4.0, -6.0])


def pack_weight(w, fmt):
    k, n = w.shape
    w = f64(np.asarray(w, np.float32).astype(ml_dtypes.bfloat16)).reshape(k // 32, 32, n)
    amax = np.abs(w).max(1)
    if fmt == "e4m3":
        byte = np.frexp(amax)[1] - 1 + 127 - 7
    else:
        mant, ex = np.frexp(amax / 6.0)
        byte = np.where(mant > 0.5, ex, ex - 1) + 127
    byte = np.clip(np.where(amax > 0, byte, 1), 1, 254)
    scaled = (w * np.exp2(127.0 - byte)[:, None, :]).reshape(k, n).astype(np.float32)
    by_word = np.ascontiguousarray(scaled.reshape(k // 512, 128, 4, n).transpose(0, 1, 3, 2))
    if fmt == "e4m3":
        words = by_word.astype(ml_dtypes.float8_e4m3fn).view(np.uint8)
    else:
        c = by_word.astype(ml_dtypes.float4_e2m1fn).view(np.uint8) & 0xF
        words = (c[..., 0::2] | (c[..., 1::2] << 4)).reshape(k // 512, 128, 2 * n)
    return np.ascontiguousarray(words), np.ascontiguousarray(byte.astype(np.uint8).reshape(k // 512, 16, n))


def unpack_weight(words, scales, fmt):
    g, _, n = scales.shape
    words = np.ascontiguousarray(words).reshape(g, 128, n, -1)
    if fmt == "e4m3":
        vals = words.view(ml_dtypes.float8_e4m3fn).astype(np.float64)
    else:
        nib = np.empty((g, 128, n, 4), np.uint8)
        nib[..., 0::2] = words & 0xF
        nib[..., 1::2] = words >> 4
        vals = E2M1[nib]
    vals = vals * np.repeat(np.exp2(scales.astype(np.float64) - 127.0), 8, axis=1)[..., None]
    return vals.transpose(0, 1, 3, 2).reshape(g * 512, n)


def d_sigmoid(v):
    s = 1.0 / (1.0 + np.exp(-np.maximum(v, -700.0)))
    return s * (1.0 - s)


def sigmoid(v):
    return 1.0 / (1.0 + np.exp(-np.maximum(v, -700.0)))


K, T, E, C, H, N = 512, 512, 4, 128, 512, 1024


def by_expert(wq, xq):
    return np.concatenate([wq[e].T @ xq[:, e * C:(e + 1) * C] for e in range(E)], axis=1)


def setup_inputs():
    n = np.random.standard_normal
    s = mx_kscale(K)
    v = mx_kscale(N)
    u = mx_kscale(H)
    slot_token = np.random.permutation(T)[:E * C]
    w_slot = np.random.uniform(0.2, 1.0, E * C)
    x = pack_weight(n((K, T)) * s[:, None], "e4m3")
    dy = pack_weight(n((N, T)) * v[:, None], "e4m3")
    m1 = n((E, K, H))
    m3 = n((E, K, H))
    w1 = [pack_weight(m, "e4m3") for m in m1 / np.sqrt(K) / s[None, :, None]]
    w3 = [pack_weight(m, "e4m3") for m in m3 / np.sqrt(K) / s[None, :, None]]
    w2t = [pack_weight(m, "e4m3") for m in n((E, N, H)) / np.sqrt(N) / v[None, :, None] * u]
    w1t = [pack_weight(m, "e4m3") for m in m1.transpose(0, 2, 1) / np.sqrt(H) / u[None, :, None]]
    w3t = [pack_weight(m, "e4m3") for m in m3.transpose(0, 2, 1) / np.sqrt(H) / u[None, :, None]]
    return {
        "x_words": x[0],
        "x_scales": x[1],
        "dy_words": dy[0],
        "dy_scales": dy[1],
        "w1_words": np.stack([m[0] for m in w1]),
        "w1_scales": np.stack([m[1] for m in w1]),
        "w3_words": np.stack([m[0] for m in w3]),
        "w3_scales": np.stack([m[1] for m in w3]),
        "w2t_words": np.stack([m[0] for m in w2t]),
        "w2t_scales": np.stack([m[1] for m in w2t]),
        "w1t_words": np.stack([m[0] for m in w1t]),
        "w1t_scales": np.stack([m[1] for m in w1t]),
        "w3t_words": np.stack([m[0] for m in w3t]),
        "w3t_scales": np.stack([m[1] for m in w3t]),
        "gate": (np.tile(w_slot, (128, 1))).astype(np.float32),
        "offs": striped(slot_token),
    }


def reference(x_words, x_scales, dy_words, dy_scales, w1_words, w1_scales, w3_words, w3_scales, w2t_words, w2t_scales, w1t_words, w1t_scales, w3t_words, w3t_scales, gate, offs):
    w1 = np.stack([unpack_weight(w1_words[e], w1_scales[e], "e4m3") for e in range(E)])
    w3 = np.stack([unpack_weight(w3_words[e], w3_scales[e], "e4m3") for e in range(E)])
    w2t = np.stack([unpack_weight(w2t_words[e], w2t_scales[e], "e4m3") for e in range(E)])
    w1t = np.stack([unpack_weight(w1t_words[e], w1t_scales[e], "e4m3") for e in range(E)])
    w3t = np.stack([unpack_weight(w3t_words[e], w3t_scales[e], "e4m3") for e in range(E)])
    idx = unstriped(offs)
    xq = unpack_weight(x_words, x_scales, "e4m3")[:, idx]
    gq = unpack_weight(dy_words, dy_scales, "e4m3")[:, idx]
    dh = f64(gate[:1]) * by_expert(w2t, gq)
    a1, a3 = by_expert(w1, xq), by_expert(w3, xq)
    dx = by_expert(w1t, mxq(dh * a3 * d_sigmoid(a1), 0, "e4m3")) + by_expert(w3t, mxq(dh * sigmoid(a1), 0, "e4m3"))
    out = np.zeros((K, T))
    out[:, idx] = dx
    return out

@@ -1,0 +1,198 @@
+from contextlib import ExitStack
+
+import concourse.mybir as mybir
+from concourse.masks import make_identity
+
+K, T, E, C, H, N = 512, 512, 4, 128, 512, 1024
+FLOPS = 1610612736
+
+F32 = mybir.dt.float32
+BF16 = mybir.dt.bfloat16
+I32 = mybir.dt.int32
+U32 = mybir.dt.uint32
+U16 = mybir.dt.uint16
+U8 = mybir.dt.uint8
+X4 = mybir.dt.float8_e4m3fn_x4
+ACT = mybir.ActivationFunctionType
+MULT = mybir.AluOpType.mult
+
+P = 128
+W2_ROW = 12
+VECTOR_EXPERTS = (0, 1)
+GATHER_CUTS = ((0, 1), (1, 2), (2, 4))
+
+
+def tile_moe_rec_glu_sigmoid_kernel(
+    tc, x_words, x_scales, dy_words, dy_scales, w1_words, w1_scales, w3_words, w3_scales,
+    w2t_words, w2t_scales, w1t_words, w1t_scales, w3t_words, w3t_scales, gate, offs, out,
+):
+    nc = tc.nc
+    with ExitStack() as ctx:
+        keep = ctx.enter_context(tc.tile_pool(name="keep", bufs=1))
+        work = ctx.enter_context(tc.tile_pool(name="work", bufs=2))
+        ps1 = ctx.enter_context(tc.psum_pool(name="ps1", bufs=1))
+        ps2 = ctx.enter_context(tc.psum_pool(name="ps2", bufs=2))
+
+        offsets = keep.tile([P, T // 16], U16, name="offsets")
+        xw = keep.tile([P, T], I32, name="xw", align_bytes=64)
+        dyw = keep.tile([P, 2, T], I32, name="dyw", align_bytes=64)
+        xs = keep.tile([P, T], U8, name="xs", align_bytes=64)
+        dys = keep.tile([P, T], U8, name="dys", align_bytes=64)
+        w2s = keep.tile([P, 2 * E, H], U8, name="w2s", align_bytes=64)
+        ws = keep.tile([P, 4, H], U8, name="ws", align_bytes=64)
+        gcol = keep.tile([P, E], F32, name="gcol")
+        ident = keep.tile([P, P], F32, name="ident", align_bytes=64)
+        w1 = [keep.tile([P, H], I32, name="w1_%d" % e, align_bytes=64) for e in range(E)]
+        w3 = [keep.tile([P, H], I32, name="w3_%d" % e, align_bytes=64) for e in range(E)]
+        w2 = [keep.tile([P, 2, H], I32, name="w2_%d" % e, align_bytes=64) for e in range(E)]
+        w1t = [keep.tile([P, K], I32, name="w1t_%d" % e, align_bytes=64) for e in range(E)]
+        w3t = [keep.tile([P, K], I32, name="w3t_%d" % e, align_bytes=64) for e in range(E)]
+        xg = keep.tile([P, T], U32, name="xg", align_bytes=64)
+        dyg = [keep.tile([P, T], U32, name="dyg%d" % s, align_bytes=64) for s in range(2)]
+        xsg = keep.tile([P, T], U8, name="xsg", align_bytes=64)
+        dysg = keep.tile([P, T], U8, name="dysg", align_bytes=64)
+        dx = keep.tile([P, 4, T], F32, name="dx", align_bytes=64)
+        win = [keep.tile([P, T], F32, name="win%d" % j, align_bytes=64) for j in range(4)]
+
+        def words(ap):
+            return ap.rearrange("p n d -> p (n d)").bitcast(I32)
+
+        def load_one(dst, src, e):
+            nc.sync.dma_start(dst[e][:], words(src[e, 0]))
+
+        def load_w2(e):
+            nc.sync.dma_start(w2[e][:], w2t_words[e].rearrange("s p n d -> p s (n d)").bitcast(I32))
+
+        def load_packed(eng, j, scales):
+            for q in range(4):
+                eng.dma_start(
+                    ws[32 * q : 32 * q + 16, j, :].bitcast(I32),
+                    scales[:, 0, 4 * q : 4 * q + 4, :].bitcast(I32),
+                )
+
+        nc.vector.memset(xs[:].bitcast(I32), 0)
+        nc.vector.memset(dys[:].bitcast(I32), 0)
+        nc.vector.memset(w2s[:].rearrange("p a n -> p (a n)").bitcast(I32), 0)
+        nc.vector.memset(ws[:].rearrange("p a n -> p (a n)").bitcast(I32), 0)
+
+        nc.sync.dma_start(offsets[:], offs)
+        nc.sync.dma_start(xw[:], words(x_words[0]))
+        for q in range(4):
+            nc.sync.dma_start(xs[32 * q : 32 * q + 4, :].bitcast(I32), x_scales[0, 4 * q : 4 * q + 4, :].bitcast(I32))
+        nc.sync.dma_start(dyw[:], dy_words.rearrange("s p n d -> p s (n d)").bitcast(I32))
+        load_one(w1, w1_words, 0)
+        w2rows = w2t_scales.rearrange("e s (q r) n -> r q (e s) n", r=4)
+        for r in range(4):
+            nc.gpsimd.dma_start(w2s[W2_ROW + r : P : 32, :, :].bitcast(I32), w2rows[r].bitcast(I32))
+        make_identity(nc, ident[:])
+        for q in range(4):
+            nc.sync.dma_start(dys[32 * q : 32 * q + 8, :].bitcast(I32), dy_scales[:, 4 * q : 4 * q + 4, :].bitcast(I32))
+        load_w2(0)
+        load_packed(nc.sync, 0, w1_scales)
+        load_one(w3, w3_words, 0)
+        with nc.allow_non_contiguous_dma(reason="one gate value a partition"):
+            nc.sync.dma_start(
+                gcol[:],
+                gate.rearrange("r c -> (r c)")[0 : E * (T + C)].rearrange("(e x) -> x e", x=T + C)[0:P, :],
+            )
+        load_packed(nc.sync, 1, w3_scales)
+        load_one(w1, w1_words, 1)
+        load_one(w3t, w3t_words, 0)
+        load_packed(nc.sync, 3, w3t_scales)
+        load_one(w1t, w1t_words, 0)
+        load_w2(1)
+        load_packed(nc.sync, 2, w1t_scales)
+        load_one(w3, w3_words, 1)
+
+        def load_first(e):
+            load_one(w1, w1_words, e)
+            load_w2(e)
+            load_one(w3, w3_words, e)
+
+        def load_second(e):
+            load_one(w3t, w3t_words, e)
+            load_one(w1t, w1t_words, e)
+
+        load_first(2)
+        load_second(1)
+        load_first(3)
+        load_second(2)
+        load_second(3)
+
+        def gather(e0, e1):
+            lst = offsets[:, e0 * C // 16 : e1 * C // 16]
+            cols = slice(e0 * C, e1 * C)
+            nc.vector.tensor_copy(xg[:, cols], xw[:].bitcast(U32).indirect(lst))
+            nc.vector.tensor_copy(xsg[:, cols], xs[:].indirect(lst))
+            for s in range(2):
+                nc.vector.tensor_copy(dyg[s][:, cols], dyw[:, s, :].bitcast(U32).indirect(lst))
+            nc.vector.tensor_copy(dysg[:, cols], dys[:].indirect(lst))
+
+        def by_byte(bank):
+            return bank[:].rearrange("p (m d) -> p d m", d=4)
+
+        def expert(e):
+            cols = slice(e * C, (e + 1) * C)
+            a1 = ps1.tile([P, H], F32, name="a1")
+            dh = ps2.tile([P, H], F32, name="dh")
+            a3 = ps2.tile([P, H], F32, name="a3")
+            nc.tensor.matmul_mx(a1[:], lhsT=xg[:, cols].bitcast(X4), lhsT_scale=xsg[:, cols],
+                                rhs=w1[e][:].bitcast(X4), rhs_scale=ws[4 * e : P, 0, :], start=True, stop=True)
+            for s in range(2):
+                nc.tensor.matmul_mx(dh[:], lhsT=dyg[s][:, cols].bitcast(X4), lhsT_scale=dysg[4 * s : P, cols],
+                                    rhs=w2[e][:, s, :].bitcast(X4), rhs_scale=w2s[W2_ROW:P, 2 * e + s, :],
+                                    start=(s == 0), stop=(s == 1))
+            nc.tensor.matmul_mx(a3[:], lhsT=xg[:, cols].bitcast(X4), lhsT_scale=xsg[:, cols],
+                                rhs=w3[e][:].bitcast(X4), rhs_scale=ws[4 * e : P, 1, :], start=True, stop=True)
+
+            sig = work.tile([P, 4, C], F32, name="sig")
+            nsig = work.tile([P, 4, C], F32, name="nsig")
+            da3 = work.tile([P, 4, C], F32, name="da3")
+            u = work.tile([P, 4, C], F32, name="u")
+            da1 = work.tile([P, 4, C], F32, name="da1")
+            nc.scalar.activation(sig[:], by_byte(a1), ACT.Sigmoid)
+            if e in VECTOR_EXPERTS:
+                nc.scalar.activation(nsig[:], by_byte(a1), ACT.Sigmoid, scale=-1.0)
+                nc.vector.scalar_tensor_tensor(da3[:], by_byte(dh), gcol[:, e : e + 1], sig[:], MULT, MULT)
+                nc.vector.tensor_tensor(u[:], by_byte(a3), nsig[:], MULT)
+                nc.vector.tensor_tensor(da1[:], da3[:], u[:], MULT)
+            else:
+                dhg = work.tile([P, 4, C], F32, name="dhg")
+                a3s = work.tile([P, 4, C], F32, name="a3s")
+                nc.scalar.activation(dhg[:], by_byte(dh), ACT.Copy, scale=gcol[:, e : e + 1])
+                nc.scalar.activation(nsig[:], by_byte(a1), ACT.Sigmoid, scale=-1.0)
+                nc.scalar.copy(a3s[:], by_byte(a3))
+                nc.gpsimd.tensor_tensor(da3[:], dhg[:], sig[:], MULT)
+                nc.gpsimd.tensor_tensor(u[:], a3s[:], nsig[:], MULT)
+                nc.gpsimd.tensor_tensor(da1[:], da3[:], u[:], MULT)
+
+            dab = work.tile([P, 2, C, 4], BF16, name="dab", align_bytes=64)
+            for j, src in enumerate((da3, da1)):
+                turned = ps1.tile([P, 4, C], F32, name="turned%d" % j)
+                for d in range(4):
+                    nc.tensor.transpose(turned[:, d, :], src[:, d, :], ident[:])
+                nc.scalar.copy(dab[:, j, :, :], turned[:].rearrange("p d c -> p c d"))
+            daw = work.tile([P, 2 * C], U32, name="daw", align_bytes=64)
+            das = work.tile([P, 2 * C], U8, name="das", align_bytes=64)
+            nc.vector.quantize_mx(daw[:].bitcast(X4), das[:], dab[:].rearrange("p j c d -> p (j c d)"))
+
+            acc = ps1.tile([P, 4, C], F32, name="acc")
+            for kt in range(4):
+                kc = slice(kt * P, (kt + 1) * P)
+                for j, (w, plane) in enumerate(((w3t, 3), (w1t, 2))):
+                    dc = slice(j * C, (j + 1) * C)
+                    nc.tensor.matmul_mx(acc[:, kt, :], lhsT=w[e][:, kc].bitcast(X4), lhsT_scale=ws[4 * e : P, plane, kc],
+                                        rhs=daw[:, dc].bitcast(X4), rhs_scale=das[:, dc], start=(j == 0), stop=(j == 1))
+            nc.scalar.copy(dx[:, :, cols], acc[:])
+
+        for e0, e1 in GATHER_CUTS:
+            gather(e0, e1)
+            for e in range(e0, e1):
+                expert(e)
+
+        for e in range(E):
+            lst = offsets[:, e * C // 16 : (e + 1) * C // 16]
+            for kt in range(4):
+                nc.vector.tensor_copy(win[kt][:].indirect(lst), dx[:, kt, e * C : (e + 1) * C])
+                if e == E - 1:
+                    nc.sync.dma_start(out[kt * P : (kt + 1) * P, :], win[kt][:])

@@ -17,9 +17,11 @@ ACT = mybir.ActivationFunctionType
 MULT = mybir.AluOpType.mult
 
 P = 128
-W2_ROW = 12
-VECTOR_EXPERTS = (0, 1)
-GATHER_CUTS = ((0, 1), (1, 2), (2, 4))
+PATHS = 'VWVH'
+RING = 4
+A1B, DHB, A3B = (0, 0, 0, 0), (1, 2, 1, 2), (3, 4, 3, 4)
+T3B, T1B, ACCB = (5, 5, 5, 5), (6, 6, 6, 6), ((7, 7), (7, 7), (7, 7), (7, 7))
+SUB = mybir.AluOpType.subtract
 
 
 def tile_moe_rec_glu_sigmoid_kernel(
@@ -29,39 +31,33 @@ def tile_moe_rec_glu_sigmoid_kernel(
     nc = tc.nc
     with ExitStack() as ctx:
         keep = ctx.enter_context(tc.tile_pool(name="keep", bufs=1))
-        work = ctx.enter_context(tc.tile_pool(name="work", bufs=2))
-        ps1 = ctx.enter_context(tc.psum_pool(name="ps1", bufs=1))
-        ps2 = ctx.enter_context(tc.psum_pool(name="ps2", bufs=2))
+        work = ctx.enter_context(tc.tile_pool(name="work", bufs=3))
+        psum = ctx.enter_context(tc.psum_pool(name="psum", bufs=1))
+        bank = [psum.tile([P, H], F32, name="bank%d" % b) for b in range(8)]
 
         offsets = keep.tile([P, T // 16], U16, name="offsets")
         xw = keep.tile([P, T], I32, name="xw", align_bytes=64)
         dyw = keep.tile([P, 2, T], I32, name="dyw", align_bytes=64)
         xs = keep.tile([P, T], U8, name="xs", align_bytes=64)
         dys = keep.tile([P, T], U8, name="dys", align_bytes=64)
-        w2s = keep.tile([P, 2 * E, H], U8, name="w2s", align_bytes=64)
+        w2s = keep.tile([P, 2, H], U8, name="w2s", align_bytes=64)
         ws = keep.tile([P, 4, H], U8, name="ws", align_bytes=64)
         gcol = keep.tile([P, E], F32, name="gcol")
         ident = keep.tile([P, P], F32, name="ident", align_bytes=64)
-        w1 = [keep.tile([P, H], I32, name="w1_%d" % e, align_bytes=64) for e in range(E)]
-        w3 = [keep.tile([P, H], I32, name="w3_%d" % e, align_bytes=64) for e in range(E)]
-        w2 = [keep.tile([P, 2, H], I32, name="w2_%d" % e, align_bytes=64) for e in range(E)]
-        w1t = [keep.tile([P, K], I32, name="w1t_%d" % e, align_bytes=64) for e in range(E)]
-        w3t = [keep.tile([P, K], I32, name="w3t_%d" % e, align_bytes=64) for e in range(E)]
-        xg = keep.tile([P, T], U32, name="xg", align_bytes=64)
-        dyg = [keep.tile([P, T], U32, name="dyg%d" % s, align_bytes=64) for s in range(2)]
-        xsg = keep.tile([P, T], U8, name="xsg", align_bytes=64)
-        dysg = keep.tile([P, T], U8, name="dysg", align_bytes=64)
-        dx = keep.tile([P, 4, T], F32, name="dx", align_bytes=64)
+        w1 = keep.tile([P, E, H], I32, name="w1", align_bytes=64)
+        w3 = keep.tile([P, E, H], I32, name="w3", align_bytes=64)
+        w2 = keep.tile([P, 2 * E, H], I32, name="w2", align_bytes=64)
+        w1t = keep.tile([P, E, K], I32, name="w1t", align_bytes=64)
+        w3t = keep.tile([P, E, K], I32, name="w3t", align_bytes=64)
+        xg = keep.tile([P, 4 * C], U32, name="xg", align_bytes=64)
+        dyg = [keep.tile([P, 4 * C], U32, name="dyg%d" % s, align_bytes=64) for s in range(2)]
+        xsg = keep.tile([P, 4 * C], U8, name="xsg", align_bytes=64)
+        dysg = keep.tile([P, 4 * C], U8, name="dysg", align_bytes=64)
+        dx = [keep.tile([P, 4, C], F32, name="dx%d" % e, align_bytes=64) for e in range(E)]
         win = [keep.tile([P, T], F32, name="win%d" % j, align_bytes=64) for j in range(4)]
 
-        def words(ap):
-            return ap.rearrange("p n d -> p (n d)").bitcast(I32)
-
-        def load_one(dst, src, e):
-            nc.sync.dma_start(dst[e][:], words(src[e, 0]))
-
-        def load_w2(e):
-            nc.sync.dma_start(w2[e][:], w2t_words[e].rearrange("s p n d -> p s (n d)").bitcast(I32))
+        def load_words(eng, dst, src, a0, a1):
+            eng.dma_start(dst[:, a0:a1, :], src.rearrange("e s p n d -> p (e s) (n d)").bitcast(I32)[:, a0:a1, :])
 
         def load_packed(eng, j, scales):
             for q in range(4):
@@ -70,129 +66,184 @@ def tile_moe_rec_glu_sigmoid_kernel(
                     scales[:, 0, 4 * q : 4 * q + 4, :].bitcast(I32),
                 )
 
-        nc.vector.memset(xs[:].bitcast(I32), 0)
-        nc.vector.memset(dys[:].bitcast(I32), 0)
-        nc.vector.memset(w2s[:].rearrange("p a n -> p (a n)").bitcast(I32), 0)
-        nc.vector.memset(ws[:].rearrange("p a n -> p (a n)").bitcast(I32), 0)
+        nc.vector.memset(ws[:, 0:2, :].rearrange("p a n -> p (a n)").bitcast(I32), 0)
+        nc.gpsimd.memset(dys[:].bitcast(I32), 0)
+        nc.gpsimd.memset(xs[:].bitcast(I32), 0)
+        nc.gpsimd.memset(w2s[:].rearrange("p a n -> p (a n)").bitcast(I32), 0)
+        nc.gpsimd.memset(ws[:, 2:4, :].rearrange("p a n -> p (a n)").bitcast(I32), 0)
 
         nc.sync.dma_start(offsets[:], offs)
-        nc.sync.dma_start(xw[:], words(x_words[0]))
-        for q in range(4):
-            nc.sync.dma_start(xs[32 * q : 32 * q + 4, :].bitcast(I32), x_scales[0, 4 * q : 4 * q + 4, :].bitcast(I32))
+        nc.sync.dma_start(xw[:], x_words[0].rearrange("p n d -> p (n d)").bitcast(I32))
+        nc.sync.dma_start(dys[32 * 2 : 32 * 2 + 8, :].bitcast(I32), dy_scales[:, 4 * 2 : 4 * 2 + 4, :].bitcast(I32))
+        nc.sync.dma_start(dys[32 * 1 : 32 * 1 + 8, :].bitcast(I32), dy_scales[:, 4 * 1 : 4 * 1 + 4, :].bitcast(I32))
+        nc.sync.dma_start(dys[32 * 0 : 32 * 0 + 8, :].bitcast(I32), dy_scales[:, 4 * 0 : 4 * 0 + 4, :].bitcast(I32))
+        nc.sync.dma_start(xs[32 * 2 : 32 * 2 + 4, :].bitcast(I32), x_scales[0, 4 * 2 : 4 * 2 + 4, :].bitcast(I32))
         nc.sync.dma_start(dyw[:], dy_words.rearrange("s p n d -> p s (n d)").bitcast(I32))
-        load_one(w1, w1_words, 0)
-        w2rows = w2t_scales.rearrange("e s (q r) n -> r q (e s) n", r=4)
-        for r in range(4):
-            nc.gpsimd.dma_start(w2s[W2_ROW + r : P : 32, :, :].bitcast(I32), w2rows[r].bitcast(I32))
-        make_identity(nc, ident[:])
-        for q in range(4):
-            nc.sync.dma_start(dys[32 * q : 32 * q + 8, :].bitcast(I32), dy_scales[:, 4 * q : 4 * q + 4, :].bitcast(I32))
-        load_w2(0)
-        load_packed(nc.sync, 0, w1_scales)
-        load_one(w3, w3_words, 0)
+        nc.sync.dma_start(ws[32 * 0 : 32 * 0 + 16, 1, :].bitcast(I32), w3_scales[:, 0, 4 * 0 : 4 * 0 + 4, :].bitcast(I32))
+        nc.sync.dma_start(xs[32 * 1 : 32 * 1 + 4, :].bitcast(I32), x_scales[0, 4 * 1 : 4 * 1 + 4, :].bitcast(I32))
+        nc.sync.dma_start(ws[32 * 3 : 32 * 3 + 16, 0, :].bitcast(I32), w1_scales[:, 0, 4 * 3 : 4 * 3 + 4, :].bitcast(I32))
         with nc.allow_non_contiguous_dma(reason="one gate value a partition"):
-            nc.sync.dma_start(
+            nc.scalar.dma_start(
                 gcol[:],
                 gate.rearrange("r c -> (r c)")[0 : E * (T + C)].rearrange("(e x) -> x e", x=T + C)[0:P, :],
             )
-        load_packed(nc.sync, 1, w3_scales)
-        load_one(w1, w1_words, 1)
-        load_one(w3t, w3t_words, 0)
-        load_packed(nc.sync, 3, w3t_scales)
-        load_one(w1t, w1t_words, 0)
-        load_w2(1)
-        load_packed(nc.sync, 2, w1t_scales)
-        load_one(w3, w3_words, 1)
+        nc.sync.dma_start(w2s[32 * 2 : 32 * 2 + 16, 0, :].bitcast(I32), w2t_scales.rearrange("e s b n -> (e s) b n")[0:4, 4 * 2 : 4 * 2 + 4, :].bitcast(I32))
+        nc.sync.dma_start(xs[32 * 0 : 32 * 0 + 4, :].bitcast(I32), x_scales[0, 4 * 0 : 4 * 0 + 4, :].bitcast(I32))
+        nc.sync.dma_start(ws[32 * 3 : 32 * 3 + 16, 1, :].bitcast(I32), w3_scales[:, 0, 4 * 3 : 4 * 3 + 4, :].bitcast(I32))
+        load_words(nc.sync, w3, w3_words, 0, 1)
+        nc.sync.dma_start(ws[32 * 0 : 32 * 0 + 16, 0, :].bitcast(I32), w1_scales[:, 0, 4 * 0 : 4 * 0 + 4, :].bitcast(I32))
+        load_words(nc.sync, w1, w1_words, 0, 1)
+        nc.sync.dma_start(ws[32 * 1 : 32 * 1 + 16, 1, :].bitcast(I32), w3_scales[:, 0, 4 * 1 : 4 * 1 + 4, :].bitcast(I32))
+        nc.gpsimd.dma_start(w2s[32 * 0 : 32 * 0 + 16, 0, :].bitcast(I32), w2t_scales.rearrange("e s b n -> (e s) b n")[0:4, 4 * 0 : 4 * 0 + 4, :].bitcast(I32))
+        nc.gpsimd.dma_start(ws[32 * 1 : 32 * 1 + 16, 0, :].bitcast(I32), w1_scales[:, 0, 4 * 1 : 4 * 1 + 4, :].bitcast(I32))
+        nc.sync.dma_start(ws[32 * 2 : 32 * 2 + 16, 0, :].bitcast(I32), w1_scales[:, 0, 4 * 2 : 4 * 2 + 4, :].bitcast(I32))
+        nc.sync.dma_start(xs[32 * 3 : 32 * 3 + 4, :].bitcast(I32), x_scales[0, 4 * 3 : 4 * 3 + 4, :].bitcast(I32))
+        load_words(nc.sync, w2, w2t_words, 0, 2)
+        nc.sync.dma_start(dys[32 * 3 : 32 * 3 + 8, :].bitcast(I32), dy_scales[:, 4 * 3 : 4 * 3 + 4, :].bitcast(I32))
+        nc.sync.dma_start(ws[32 * 2 : 32 * 2 + 16, 1, :].bitcast(I32), w3_scales[:, 0, 4 * 2 : 4 * 2 + 4, :].bitcast(I32))
+        nc.sync.dma_start(w2s[32 * 1 : 32 * 1 + 16, 0, :].bitcast(I32), w2t_scales.rearrange("e s b n -> (e s) b n")[0:4, 4 * 1 : 4 * 1 + 4, :].bitcast(I32))
+        nc.sync.dma_start(w2s[32 * 3 : 32 * 3 + 16, 0, :].bitcast(I32), w2t_scales.rearrange("e s b n -> (e s) b n")[0:4, 4 * 3 : 4 * 3 + 4, :].bitcast(I32))
+        nc.gpsimd.dma_start(ws[32 * 0 : 32 * 0 + 16, 3, :].bitcast(I32), w3t_scales[:, 0, 4 * 0 : 4 * 0 + 4, :].bitcast(I32))
+        load_words(nc.sync, w1, w1_words, 1, 2)
+        load_words(nc.sync, w3, w3_words, 1, 2)
+        load_words(nc.sync, w1, w1_words, 2, 3)
+        nc.gpsimd.dma_start(ws[32 * 3 : 32 * 3 + 16, 3, :].bitcast(I32), w3t_scales[:, 0, 4 * 3 : 4 * 3 + 4, :].bitcast(I32))
+        load_words(nc.sync, w1t, w1t_words, 0, 1)
+        make_identity(nc, ident[:])
+        load_words(nc.sync, w3, w3_words, 3, 4)
+        nc.sync.dma_start(ws[32 * 0 : 32 * 0 + 16, 2, :].bitcast(I32), w1t_scales[:, 0, 4 * 0 : 4 * 0 + 4, :].bitcast(I32))
+        nc.sync.dma_start(ws[32 * 2 : 32 * 2 + 16, 2, :].bitcast(I32), w1t_scales[:, 0, 4 * 2 : 4 * 2 + 4, :].bitcast(I32))
+        nc.sync.dma_start(ws[32 * 3 : 32 * 3 + 16, 2, :].bitcast(I32), w1t_scales[:, 0, 4 * 3 : 4 * 3 + 4, :].bitcast(I32))
+        nc.gpsimd.dma_start(ws[32 * 1 : 32 * 1 + 16, 3, :].bitcast(I32), w3t_scales[:, 0, 4 * 1 : 4 * 1 + 4, :].bitcast(I32))
+        load_words(nc.sync, w2, w2t_words, 2, 4)
+        load_words(nc.sync, w3, w3_words, 2, 3)
+        load_words(nc.sync, w3t, w3t_words, 0, 1)
+        nc.sync.dma_start(w2s[32 * 0 : 32 * 0 + 16, 1, :].bitcast(I32), w2t_scales.rearrange("e s b n -> (e s) b n")[4:8, 4 * 0 : 4 * 0 + 4, :].bitcast(I32))
+        nc.sync.dma_start(w2s[32 * 3 : 32 * 3 + 16, 1, :].bitcast(I32), w2t_scales.rearrange("e s b n -> (e s) b n")[4:8, 4 * 3 : 4 * 3 + 4, :].bitcast(I32))
+        nc.gpsimd.dma_start(ws[32 * 2 : 32 * 2 + 16, 3, :].bitcast(I32), w3t_scales[:, 0, 4 * 2 : 4 * 2 + 4, :].bitcast(I32))
+        nc.sync.dma_start(w2s[32 * 1 : 32 * 1 + 16, 1, :].bitcast(I32), w2t_scales.rearrange("e s b n -> (e s) b n")[4:8, 4 * 1 : 4 * 1 + 4, :].bitcast(I32))
+        load_words(nc.sync, w2, w2t_words, 4, 6)
+        load_words(nc.sync, w2, w2t_words, 6, 8)
+        load_words(nc.sync, w1t, w1t_words, 1, 2)
+        nc.sync.dma_start(w2s[32 * 2 : 32 * 2 + 16, 1, :].bitcast(I32), w2t_scales.rearrange("e s b n -> (e s) b n")[4:8, 4 * 2 : 4 * 2 + 4, :].bitcast(I32))
+        load_words(nc.sync, w1, w1_words, 3, 4)
+        load_words(nc.sync, w3t, w3t_words, 1, 2)
+        load_words(nc.sync, w1t, w1t_words, 2, 3)
+        load_words(nc.sync, w3t, w3t_words, 3, 4)
+        load_words(nc.sync, w3t, w3t_words, 2, 3)
+        load_words(nc.sync, w1t, w1t_words, 3, 4)
+        nc.gpsimd.dma_start(ws[32 * 1 : 32 * 1 + 16, 2, :].bitcast(I32), w1t_scales[:, 0, 4 * 1 : 4 * 1 + 4, :].bitcast(I32))
 
-        def load_first(e):
-            load_one(w1, w1_words, e)
-            load_w2(e)
-            load_one(w3, w3_words, e)
+        def ring(e0, e1):
+            return slice(e0 % RING * C, ((e1 - 1) % RING + 1) * C)
 
-        def load_second(e):
-            load_one(w3t, w3t_words, e)
-            load_one(w1t, w1t_words, e)
-
-        load_first(2)
-        load_second(1)
-        load_first(3)
-        load_second(2)
-        load_second(3)
-
-        def gather(e0, e1):
+        def gather_x(e0, e1):
             lst = offsets[:, e0 * C // 16 : e1 * C // 16]
-            cols = slice(e0 * C, e1 * C)
-            nc.vector.tensor_copy(xg[:, cols], xw[:].bitcast(U32).indirect(lst))
-            nc.vector.tensor_copy(xsg[:, cols], xs[:].indirect(lst))
+            nc.vector.tensor_copy(xg[:, ring(e0, e1)], xw[:].bitcast(U32).indirect(lst))
+            nc.vector.tensor_copy(xsg[:, ring(e0, e1)], xs[:].indirect(lst))
+
+        def gather_dy(e0, e1):
+            lst = offsets[:, e0 * C // 16 : e1 * C // 16]
             for s in range(2):
-                nc.vector.tensor_copy(dyg[s][:, cols], dyw[:, s, :].bitcast(U32).indirect(lst))
-            nc.vector.tensor_copy(dysg[:, cols], dys[:].indirect(lst))
+                nc.vector.tensor_copy(dyg[s][:, ring(e0, e1)], dyw[:, s, :].bitcast(U32).indirect(lst))
+            nc.vector.tensor_copy(dysg[:, ring(e0, e1)], dys[:].indirect(lst))
 
-        def by_byte(bank):
-            return bank[:].rearrange("p (m d) -> p d m", d=4)
+        def by_byte(sums):
+            return sums[:].rearrange("p (m d) -> p d m", d=4)
 
-        def expert(e):
-            cols = slice(e * C, (e + 1) * C)
-            a1 = ps1.tile([P, H], F32, name="a1")
-            dh = ps2.tile([P, H], F32, name="dh")
-            a3 = ps2.tile([P, H], F32, name="a3")
+        def first(e):
+            cols = ring(e, e + 1)
+            a1, dh, a3 = bank[A1B[e]], bank[DHB[e]], bank[A3B[e]]
             nc.tensor.matmul_mx(a1[:], lhsT=xg[:, cols].bitcast(X4), lhsT_scale=xsg[:, cols],
-                                rhs=w1[e][:].bitcast(X4), rhs_scale=ws[4 * e : P, 0, :], start=True, stop=True)
+                                rhs=w1[:, e, :].bitcast(X4), rhs_scale=ws[4 * e : P, 0, :], start=True, stop=True)
+            nc.tensor.matmul_mx(a3[:], lhsT=xg[:, cols].bitcast(X4), lhsT_scale=xsg[:, cols],
+                                rhs=w3[:, e, :].bitcast(X4), rhs_scale=ws[4 * e : P, 1, :], start=True, stop=True)
             for s in range(2):
                 nc.tensor.matmul_mx(dh[:], lhsT=dyg[s][:, cols].bitcast(X4), lhsT_scale=dysg[4 * s : P, cols],
-                                    rhs=w2[e][:, s, :].bitcast(X4), rhs_scale=w2s[W2_ROW:P, 2 * e + s, :],
+                                    rhs=w2[:, 2 * e + s, :].bitcast(X4), rhs_scale=w2s[4 * ((2 * e + s) % 4) : P, e // 2, :],
                                     start=(s == 0), stop=(s == 1))
-            nc.tensor.matmul_mx(a3[:], lhsT=xg[:, cols].bitcast(X4), lhsT_scale=xsg[:, cols],
-                                rhs=w3[e][:].bitcast(X4), rhs_scale=ws[4 * e : P, 1, :], start=True, stop=True)
 
+        def products(e):
+            a1, dh, a3 = bank[A1B[e]], bank[DHB[e]], bank[A3B[e]]
             sig = work.tile([P, 4, C], F32, name="sig")
-            nsig = work.tile([P, 4, C], F32, name="nsig")
             da3 = work.tile([P, 4, C], F32, name="da3")
             u = work.tile([P, 4, C], F32, name="u")
-            da1 = work.tile([P, 4, C], F32, name="da1")
+            nda1 = work.tile([P, 4, C], F32, name="nda1")
             nc.scalar.activation(sig[:], by_byte(a1), ACT.Sigmoid)
-            if e in VECTOR_EXPERTS:
+            if PATHS[e] == "P":
+                nsig = work.tile([P, 4, C], F32, name="nsig")
+                na3 = work.tile([P, 4, C], F32, name="na3")
                 nc.scalar.activation(nsig[:], by_byte(a1), ACT.Sigmoid, scale=-1.0)
+                nc.scalar.activation(na3[:], by_byte(a3), ACT.Copy, scale=-1.0)
+                nc.gpsimd.tensor_tensor(u[:], na3[:], nsig[:], MULT)
+            else:
+                nc.vector.scalar_tensor_tensor(u[:], sig[:], 1.0, by_byte(a3), SUB, MULT)
+            if PATHS[e] in "VW":
                 nc.vector.scalar_tensor_tensor(da3[:], by_byte(dh), gcol[:, e : e + 1], sig[:], MULT, MULT)
-                nc.vector.tensor_tensor(u[:], by_byte(a3), nsig[:], MULT)
-                nc.vector.tensor_tensor(da1[:], da3[:], u[:], MULT)
             else:
                 dhg = work.tile([P, 4, C], F32, name="dhg")
-                a3s = work.tile([P, 4, C], F32, name="a3s")
                 nc.scalar.activation(dhg[:], by_byte(dh), ACT.Copy, scale=gcol[:, e : e + 1])
-                nc.scalar.activation(nsig[:], by_byte(a1), ACT.Sigmoid, scale=-1.0)
-                nc.scalar.copy(a3s[:], by_byte(a3))
                 nc.gpsimd.tensor_tensor(da3[:], dhg[:], sig[:], MULT)
-                nc.gpsimd.tensor_tensor(u[:], a3s[:], nsig[:], MULT)
-                nc.gpsimd.tensor_tensor(da1[:], da3[:], u[:], MULT)
+            last = nc.vector if PATHS[e] == "V" else nc.gpsimd
+            last.tensor_tensor(nda1[:], da3[:], u[:], MULT)
+            made[e] = (da3, nda1)
 
+        def turn(e):
+            da3, nda1 = made[e]
             dab = work.tile([P, 2, C, 4], BF16, name="dab", align_bytes=64)
-            for j, src in enumerate((da3, da1)):
-                turned = ps1.tile([P, 4, C], F32, name="turned%d" % j)
+            for j, (src, turned, sign) in enumerate(((da3, bank[T3B[e]], 1.0), (nda1, bank[T1B[e]], -1.0))):
                 for d in range(4):
-                    nc.tensor.transpose(turned[:, d, :], src[:, d, :], ident[:])
-                nc.scalar.copy(dab[:, j, :, :], turned[:].rearrange("p d c -> p c d"))
+                    nc.tensor.transpose(turned[:, d * C : (d + 1) * C], src[:, d, :], ident[:])
+                nc.scalar.activation(dab[:, j, :, :], turned[:].rearrange("p (d c) -> p c d", d=4), ACT.Copy, scale=sign)
             daw = work.tile([P, 2 * C], U32, name="daw", align_bytes=64)
             das = work.tile([P, 2 * C], U8, name="das", align_bytes=64)
             nc.vector.quantize_mx(daw[:].bitcast(X4), das[:], dab[:].rearrange("p j c d -> p (j c d)"))
+            packed[e] = (daw, das)
 
-            acc = ps1.tile([P, 4, C], F32, name="acc")
-            for kt in range(4):
+        def back(e, half):
+            daw, das = packed[e]
+            acc = bank[ACCB[e][half]]
+            for h in range(2):
+                kt = 2 * half + h
                 kc = slice(kt * P, (kt + 1) * P)
                 for j, (w, plane) in enumerate(((w3t, 3), (w1t, 2))):
                     dc = slice(j * C, (j + 1) * C)
-                    nc.tensor.matmul_mx(acc[:, kt, :], lhsT=w[e][:, kc].bitcast(X4), lhsT_scale=ws[4 * e : P, plane, kc],
+                    nc.tensor.matmul_mx(acc[:, h * C : (h + 1) * C], lhsT=w[:, e, kc].bitcast(X4),
+                                        lhsT_scale=ws[4 * e : P, plane, kc],
                                         rhs=daw[:, dc].bitcast(X4), rhs_scale=das[:, dc], start=(j == 0), stop=(j == 1))
-            nc.scalar.copy(dx[:, :, cols], acc[:])
+            nc.scalar.copy(dx[e][:, 2 * half : 2 * half + 2, :].rearrange("p h c -> p (h c)"), acc[:, 0 : 2 * C])
 
-        for e0, e1 in GATHER_CUTS:
-            gather(e0, e1)
-            for e in range(e0, e1):
-                expert(e)
+        made, packed = {}, {}
+        gather_x(0, 0 + 1)
+        gather_dy(0, 0 + 1)
+        first(0)
+        products(0)
+        gather_x(1, 1 + 1)
+        gather_dy(1, 1 + 1)
+        first(1)
+        products(1)
+        gather_x(2, 3 + 1)
+        gather_dy(2, 3 + 1)
+        turn(0)
+        back(0, 0)
+        back(0, 1)
+        first(2)
+        products(2)
+        turn(1)
+        back(1, 0)
+        back(1, 1)
+        first(3)
+        products(3)
+        turn(2)
+        back(2, 0)
+        back(2, 1)
+        turn(3)
+        back(3, 0)
+        back(3, 1)
 
         for e in range(E):
             lst = offsets[:, e * C // 16 : (e + 1) * C // 16]
             for kt in range(4):
-                nc.vector.tensor_copy(win[kt][:].indirect(lst), dx[:, kt, e * C : (e + 1) * C])
+                nc.vector.tensor_copy(win[kt][:].indirect(lst), dx[e][:, kt, :])
                 if e == E - 1:
                     nc.sync.dma_start(out[kt * P : (kt + 1) * P, :], win[kt][:])

@@ -31,7 +31,7 @@ def tile_moe_rec_glu_sigmoid_kernel(
     nc = tc.nc
     with ExitStack() as ctx:
         keep = ctx.enter_context(tc.tile_pool(name="keep", bufs=1))
-        work = ctx.enter_context(tc.tile_pool(name="work", bufs=3))
+        work = ctx.enter_context(tc.tile_pool(name="work", bufs=4))
         psum = ctx.enter_context(tc.psum_pool(name="psum", bufs=1))
         bank = [psum.tile([P, H], F32, name="bank%d" % b) for b in range(8)]
 
@@ -66,73 +66,70 @@ def tile_moe_rec_glu_sigmoid_kernel(
                     scales[:, 0, 4 * q : 4 * q + 4, :].bitcast(I32),
                 )
 
+        nc.vector.memset(xs[:].bitcast(I32), 0)
         nc.vector.memset(ws[:, 0:2, :].rearrange("p a n -> p (a n)").bitcast(I32), 0)
-        nc.gpsimd.memset(dys[:].bitcast(I32), 0)
-        nc.gpsimd.memset(xs[:].bitcast(I32), 0)
-        nc.gpsimd.memset(w2s[:].rearrange("p a n -> p (a n)").bitcast(I32), 0)
+        nc.vector.memset(w2s[:].rearrange("p a n -> p (a n)").bitcast(I32), 0)
+        nc.vector.memset(dys[:].bitcast(I32), 0)
         nc.gpsimd.memset(ws[:, 2:4, :].rearrange("p a n -> p (a n)").bitcast(I32), 0)
 
         nc.sync.dma_start(offsets[:], offs)
         nc.sync.dma_start(xw[:], x_words[0].rearrange("p n d -> p (n d)").bitcast(I32))
-        nc.sync.dma_start(dys[32 * 2 : 32 * 2 + 8, :].bitcast(I32), dy_scales[:, 4 * 2 : 4 * 2 + 4, :].bitcast(I32))
-        nc.sync.dma_start(dys[32 * 1 : 32 * 1 + 8, :].bitcast(I32), dy_scales[:, 4 * 1 : 4 * 1 + 4, :].bitcast(I32))
-        nc.sync.dma_start(dys[32 * 0 : 32 * 0 + 8, :].bitcast(I32), dy_scales[:, 4 * 0 : 4 * 0 + 4, :].bitcast(I32))
-        nc.sync.dma_start(xs[32 * 2 : 32 * 2 + 4, :].bitcast(I32), x_scales[0, 4 * 2 : 4 * 2 + 4, :].bitcast(I32))
-        nc.sync.dma_start(dyw[:], dy_words.rearrange("s p n d -> p s (n d)").bitcast(I32))
-        nc.sync.dma_start(ws[32 * 0 : 32 * 0 + 16, 1, :].bitcast(I32), w3_scales[:, 0, 4 * 0 : 4 * 0 + 4, :].bitcast(I32))
+        nc.gpsimd.dma_start(xs[32 * 3 : 32 * 3 + 4, :].bitcast(I32), x_scales[0, 4 * 3 : 4 * 3 + 4, :].bitcast(I32))
+        nc.gpsimd.dma_start(ws[32 * 2 : 32 * 2 + 16, 0, :].bitcast(I32), w1_scales[:, 0, 4 * 2 : 4 * 2 + 4, :].bitcast(I32))
+        nc.gpsimd.dma_start(ws[32 * 1 : 32 * 1 + 16, 0, :].bitcast(I32), w1_scales[:, 0, 4 * 1 : 4 * 1 + 4, :].bitcast(I32))
         nc.sync.dma_start(xs[32 * 1 : 32 * 1 + 4, :].bitcast(I32), x_scales[0, 4 * 1 : 4 * 1 + 4, :].bitcast(I32))
+        nc.sync.dma_start(xs[32 * 2 : 32 * 2 + 4, :].bitcast(I32), x_scales[0, 4 * 2 : 4 * 2 + 4, :].bitcast(I32))
+        nc.gpsimd.dma_start(w2s[32 * 3 : 32 * 3 + 16, 0, :].bitcast(I32), w2t_scales.rearrange("e s b n -> (e s) b n")[0:4, 4 * 3 : 4 * 3 + 4, :].bitcast(I32))
+        nc.gpsimd.dma_start(dys[32 * 0 : 32 * 0 + 8, :].bitcast(I32), dy_scales[:, 4 * 0 : 4 * 0 + 4, :].bitcast(I32))
+        nc.sync.dma_start(xs[32 * 0 : 32 * 0 + 4, :].bitcast(I32), x_scales[0, 4 * 0 : 4 * 0 + 4, :].bitcast(I32))
+        nc.gpsimd.dma_start(ws[32 * 3 : 32 * 3 + 16, 1, :].bitcast(I32), w3_scales[:, 0, 4 * 3 : 4 * 3 + 4, :].bitcast(I32))
         nc.sync.dma_start(ws[32 * 3 : 32 * 3 + 16, 0, :].bitcast(I32), w1_scales[:, 0, 4 * 3 : 4 * 3 + 4, :].bitcast(I32))
+        nc.sync.dma_start(dyw[:], dy_words.rearrange("s p n d -> p s (n d)").bitcast(I32))
+        load_words(nc.sync, w3, w3_words, 0, 1)
+        nc.sync.dma_start(ws[32 * 0 : 32 * 0 + 16, 0, :].bitcast(I32), w1_scales[:, 0, 4 * 0 : 4 * 0 + 4, :].bitcast(I32))
+        nc.sync.dma_start(dys[32 * 1 : 32 * 1 + 8, :].bitcast(I32), dy_scales[:, 4 * 1 : 4 * 1 + 4, :].bitcast(I32))
+        nc.sync.dma_start(ws[32 * 2 : 32 * 2 + 16, 2, :].bitcast(I32), w1t_scales[:, 0, 4 * 2 : 4 * 2 + 4, :].bitcast(I32))
+        nc.sync.dma_start(w2s[32 * 1 : 32 * 1 + 16, 0, :].bitcast(I32), w2t_scales.rearrange("e s b n -> (e s) b n")[0:4, 4 * 1 : 4 * 1 + 4, :].bitcast(I32))
+        nc.sync.dma_start(w2s[32 * 0 : 32 * 0 + 16, 0, :].bitcast(I32), w2t_scales.rearrange("e s b n -> (e s) b n")[0:4, 4 * 0 : 4 * 0 + 4, :].bitcast(I32))
+        load_words(nc.sync, w1, w1_words, 0, 2)
+        nc.sync.dma_start(ws[32 * 2 : 32 * 2 + 16, 1, :].bitcast(I32), w3_scales[:, 0, 4 * 2 : 4 * 2 + 4, :].bitcast(I32))
+        nc.sync.dma_start(dys[32 * 3 : 32 * 3 + 8, :].bitcast(I32), dy_scales[:, 4 * 3 : 4 * 3 + 4, :].bitcast(I32))
+        nc.sync.dma_start(ws[32 * 0 : 32 * 0 + 16, 1, :].bitcast(I32), w3_scales[:, 0, 4 * 0 : 4 * 0 + 4, :].bitcast(I32))
+        make_identity(nc, ident[:])
+        nc.sync.dma_start(w2s[32 * 2 : 32 * 2 + 16, 0, :].bitcast(I32), w2t_scales.rearrange("e s b n -> (e s) b n")[0:4, 4 * 2 : 4 * 2 + 4, :].bitcast(I32))
+        nc.sync.dma_start(dys[32 * 2 : 32 * 2 + 8, :].bitcast(I32), dy_scales[:, 4 * 2 : 4 * 2 + 4, :].bitcast(I32))
+        nc.sync.dma_start(ws[32 * 1 : 32 * 1 + 16, 1, :].bitcast(I32), w3_scales[:, 0, 4 * 1 : 4 * 1 + 4, :].bitcast(I32))
+        load_words(nc.sync, w2, w2t_words, 0, 2)
+        nc.gpsimd.dma_start(ws[32 * 1 : 32 * 1 + 16, 3, :].bitcast(I32), w3t_scales[:, 0, 4 * 1 : 4 * 1 + 4, :].bitcast(I32))
+        nc.gpsimd.dma_start(ws[32 * 0 : 32 * 0 + 16, 3, :].bitcast(I32), w3t_scales[:, 0, 4 * 0 : 4 * 0 + 4, :].bitcast(I32))
+        load_words(nc.sync, w1, w1_words, 2, 3)
+        load_words(nc.sync, w3, w3_words, 1, 2)
+        load_words(nc.sync, w1t, w1t_words, 0, 1)
+        load_words(nc.sync, w3, w3_words, 2, 4)
+        nc.sync.dma_start(ws[32 * 2 : 32 * 2 + 16, 3, :].bitcast(I32), w3t_scales[:, 0, 4 * 2 : 4 * 2 + 4, :].bitcast(I32))
+        nc.sync.dma_start(ws[32 * 1 : 32 * 1 + 16, 2, :].bitcast(I32), w1t_scales[:, 0, 4 * 1 : 4 * 1 + 4, :].bitcast(I32))
+        load_words(nc.sync, w2, w2t_words, 2, 4)
         with nc.allow_non_contiguous_dma(reason="one gate value a partition"):
             nc.scalar.dma_start(
                 gcol[:],
                 gate.rearrange("r c -> (r c)")[0 : E * (T + C)].rearrange("(e x) -> x e", x=T + C)[0:P, :],
             )
-        nc.sync.dma_start(w2s[32 * 2 : 32 * 2 + 16, 0, :].bitcast(I32), w2t_scales.rearrange("e s b n -> (e s) b n")[0:4, 4 * 2 : 4 * 2 + 4, :].bitcast(I32))
-        nc.sync.dma_start(xs[32 * 0 : 32 * 0 + 4, :].bitcast(I32), x_scales[0, 4 * 0 : 4 * 0 + 4, :].bitcast(I32))
-        nc.sync.dma_start(ws[32 * 3 : 32 * 3 + 16, 1, :].bitcast(I32), w3_scales[:, 0, 4 * 3 : 4 * 3 + 4, :].bitcast(I32))
-        load_words(nc.sync, w3, w3_words, 0, 1)
-        nc.sync.dma_start(ws[32 * 0 : 32 * 0 + 16, 0, :].bitcast(I32), w1_scales[:, 0, 4 * 0 : 4 * 0 + 4, :].bitcast(I32))
-        load_words(nc.sync, w1, w1_words, 0, 1)
-        nc.sync.dma_start(ws[32 * 1 : 32 * 1 + 16, 1, :].bitcast(I32), w3_scales[:, 0, 4 * 1 : 4 * 1 + 4, :].bitcast(I32))
-        nc.gpsimd.dma_start(w2s[32 * 0 : 32 * 0 + 16, 0, :].bitcast(I32), w2t_scales.rearrange("e s b n -> (e s) b n")[0:4, 4 * 0 : 4 * 0 + 4, :].bitcast(I32))
-        nc.gpsimd.dma_start(ws[32 * 1 : 32 * 1 + 16, 0, :].bitcast(I32), w1_scales[:, 0, 4 * 1 : 4 * 1 + 4, :].bitcast(I32))
-        nc.sync.dma_start(ws[32 * 2 : 32 * 2 + 16, 0, :].bitcast(I32), w1_scales[:, 0, 4 * 2 : 4 * 2 + 4, :].bitcast(I32))
-        nc.sync.dma_start(xs[32 * 3 : 32 * 3 + 4, :].bitcast(I32), x_scales[0, 4 * 3 : 4 * 3 + 4, :].bitcast(I32))
-        load_words(nc.sync, w2, w2t_words, 0, 2)
-        nc.sync.dma_start(dys[32 * 3 : 32 * 3 + 8, :].bitcast(I32), dy_scales[:, 4 * 3 : 4 * 3 + 4, :].bitcast(I32))
-        nc.sync.dma_start(ws[32 * 2 : 32 * 2 + 16, 1, :].bitcast(I32), w3_scales[:, 0, 4 * 2 : 4 * 2 + 4, :].bitcast(I32))
-        nc.sync.dma_start(w2s[32 * 1 : 32 * 1 + 16, 0, :].bitcast(I32), w2t_scales.rearrange("e s b n -> (e s) b n")[0:4, 4 * 1 : 4 * 1 + 4, :].bitcast(I32))
-        nc.sync.dma_start(w2s[32 * 3 : 32 * 3 + 16, 0, :].bitcast(I32), w2t_scales.rearrange("e s b n -> (e s) b n")[0:4, 4 * 3 : 4 * 3 + 4, :].bitcast(I32))
-        nc.gpsimd.dma_start(ws[32 * 0 : 32 * 0 + 16, 3, :].bitcast(I32), w3t_scales[:, 0, 4 * 0 : 4 * 0 + 4, :].bitcast(I32))
-        load_words(nc.sync, w1, w1_words, 1, 2)
-        load_words(nc.sync, w3, w3_words, 1, 2)
-        load_words(nc.sync, w1, w1_words, 2, 3)
-        nc.gpsimd.dma_start(ws[32 * 3 : 32 * 3 + 16, 3, :].bitcast(I32), w3t_scales[:, 0, 4 * 3 : 4 * 3 + 4, :].bitcast(I32))
-        load_words(nc.sync, w1t, w1t_words, 0, 1)
-        make_identity(nc, ident[:])
-        load_words(nc.sync, w3, w3_words, 3, 4)
-        nc.sync.dma_start(ws[32 * 0 : 32 * 0 + 16, 2, :].bitcast(I32), w1t_scales[:, 0, 4 * 0 : 4 * 0 + 4, :].bitcast(I32))
-        nc.sync.dma_start(ws[32 * 2 : 32 * 2 + 16, 2, :].bitcast(I32), w1t_scales[:, 0, 4 * 2 : 4 * 2 + 4, :].bitcast(I32))
-        nc.sync.dma_start(ws[32 * 3 : 32 * 3 + 16, 2, :].bitcast(I32), w1t_scales[:, 0, 4 * 3 : 4 * 3 + 4, :].bitcast(I32))
-        nc.gpsimd.dma_start(ws[32 * 1 : 32 * 1 + 16, 3, :].bitcast(I32), w3t_scales[:, 0, 4 * 1 : 4 * 1 + 4, :].bitcast(I32))
-        load_words(nc.sync, w2, w2t_words, 2, 4)
-        load_words(nc.sync, w3, w3_words, 2, 3)
         load_words(nc.sync, w3t, w3t_words, 0, 1)
-        nc.sync.dma_start(w2s[32 * 0 : 32 * 0 + 16, 1, :].bitcast(I32), w2t_scales.rearrange("e s b n -> (e s) b n")[4:8, 4 * 0 : 4 * 0 + 4, :].bitcast(I32))
-        nc.sync.dma_start(w2s[32 * 3 : 32 * 3 + 16, 1, :].bitcast(I32), w2t_scales.rearrange("e s b n -> (e s) b n")[4:8, 4 * 3 : 4 * 3 + 4, :].bitcast(I32))
-        nc.gpsimd.dma_start(ws[32 * 2 : 32 * 2 + 16, 3, :].bitcast(I32), w3t_scales[:, 0, 4 * 2 : 4 * 2 + 4, :].bitcast(I32))
+        nc.sync.dma_start(ws[32 * 0 : 32 * 0 + 16, 2, :].bitcast(I32), w1t_scales[:, 0, 4 * 0 : 4 * 0 + 4, :].bitcast(I32))
         nc.sync.dma_start(w2s[32 * 1 : 32 * 1 + 16, 1, :].bitcast(I32), w2t_scales.rearrange("e s b n -> (e s) b n")[4:8, 4 * 1 : 4 * 1 + 4, :].bitcast(I32))
         load_words(nc.sync, w2, w2t_words, 4, 6)
         load_words(nc.sync, w2, w2t_words, 6, 8)
-        load_words(nc.sync, w1t, w1t_words, 1, 2)
-        nc.sync.dma_start(w2s[32 * 2 : 32 * 2 + 16, 1, :].bitcast(I32), w2t_scales.rearrange("e s b n -> (e s) b n")[4:8, 4 * 2 : 4 * 2 + 4, :].bitcast(I32))
+        nc.sync.dma_start(w2s[32 * 3 : 32 * 3 + 16, 1, :].bitcast(I32), w2t_scales.rearrange("e s b n -> (e s) b n")[4:8, 4 * 3 : 4 * 3 + 4, :].bitcast(I32))
         load_words(nc.sync, w1, w1_words, 3, 4)
         load_words(nc.sync, w3t, w3t_words, 1, 2)
-        load_words(nc.sync, w1t, w1t_words, 2, 3)
+        load_words(nc.sync, w1t, w1t_words, 1, 2)
+        load_words(nc.sync, w1t, w1t_words, 2, 4)
+        nc.gpsimd.dma_start(ws[32 * 3 : 32 * 3 + 16, 3, :].bitcast(I32), w3t_scales[:, 0, 4 * 3 : 4 * 3 + 4, :].bitcast(I32))
+        nc.gpsimd.dma_start(ws[32 * 3 : 32 * 3 + 16, 2, :].bitcast(I32), w1t_scales[:, 0, 4 * 3 : 4 * 3 + 4, :].bitcast(I32))
         load_words(nc.sync, w3t, w3t_words, 3, 4)
+        nc.gpsimd.dma_start(w2s[32 * 0 : 32 * 0 + 16, 1, :].bitcast(I32), w2t_scales.rearrange("e s b n -> (e s) b n")[4:8, 4 * 0 : 4 * 0 + 4, :].bitcast(I32))
         load_words(nc.sync, w3t, w3t_words, 2, 3)
-        load_words(nc.sync, w1t, w1t_words, 3, 4)
-        nc.gpsimd.dma_start(ws[32 * 1 : 32 * 1 + 16, 2, :].bitcast(I32), w1t_scales[:, 0, 4 * 1 : 4 * 1 + 4, :].bitcast(I32))
+        nc.gpsimd.dma_start(w2s[32 * 2 : 32 * 2 + 16, 1, :].bitcast(I32), w2t_scales.rearrange("e s b n -> (e s) b n")[4:8, 4 * 2 : 4 * 2 + 4, :].bitcast(I32))
 
         def ring(e0, e1):
             return slice(e0 % RING * C, ((e1 - 1) % RING + 1) * C)

@@ -15,13 +15,9 @@ U8 = mybir.dt.uint8
 X4 = mybir.dt.float8_e4m3fn_x4
 ACT = mybir.ActivationFunctionType
 MULT = mybir.AluOpType.mult
+SUB = mybir.AluOpType.subtract
 
 P = 128
-PATHS = 'VWVH'
-RING = 4
-A1B, DHB, A3B = (0, 0, 0, 0), (1, 2, 1, 2), (3, 4, 3, 4)
-T3B, T1B, ACCB = (5, 5, 5, 5), (6, 6, 6, 6), ((7, 7), (7, 7), (7, 7), (7, 7))
-SUB = mybir.AluOpType.subtract
 
 
 def tile_moe_rec_glu_sigmoid_kernel(
@@ -34,161 +30,130 @@ def tile_moe_rec_glu_sigmoid_kernel(
         work = ctx.enter_context(tc.tile_pool(name="work", bufs=4))
         psum = ctx.enter_context(tc.psum_pool(name="psum", bufs=1))
         bank = [psum.tile([P, H], F32, name="bank%d" % b) for b in range(8)]
+        a1_bank, a3_bank, dh_bank, t3_bank, t1_bank = bank[0:2], bank[2:4], bank[4:6], bank[6], bank[7]
 
         offsets = keep.tile([P, T // 16], U16, name="offsets")
         xw = keep.tile([P, T], I32, name="xw", align_bytes=64)
         dyw = keep.tile([P, 2, T], I32, name="dyw", align_bytes=64)
         xs = keep.tile([P, T], U8, name="xs", align_bytes=64)
         dys = keep.tile([P, T], U8, name="dys", align_bytes=64)
-        w2s = keep.tile([P, 2, H], U8, name="w2s", align_bytes=64)
-        ws = keep.tile([P, 4, H], U8, name="ws", align_bytes=64)
+        w1s = keep.tile([P, H], U8, name="w1s", align_bytes=64)
+        w3s = keep.tile([P, H], U8, name="w3s", align_bytes=64)
+        w2s = keep.tile([P, 2 * E, H], U8, name="w2s", align_bytes=64)
+        w1ts = keep.tile([P, K], U8, name="w1ts", align_bytes=64)
+        w3ts = keep.tile([P, K], U8, name="w3ts", align_bytes=64)
         gcol = keep.tile([P, E], F32, name="gcol")
         ident = keep.tile([P, P], F32, name="ident", align_bytes=64)
-        w1 = keep.tile([P, E, H], I32, name="w1", align_bytes=64)
-        w3 = keep.tile([P, E, H], I32, name="w3", align_bytes=64)
-        w2 = keep.tile([P, 2 * E, H], I32, name="w2", align_bytes=64)
-        w1t = keep.tile([P, E, K], I32, name="w1t", align_bytes=64)
-        w3t = keep.tile([P, E, K], I32, name="w3t", align_bytes=64)
-        xg = keep.tile([P, 4 * C], U32, name="xg", align_bytes=64)
-        dyg = [keep.tile([P, 4 * C], U32, name="dyg%d" % s, align_bytes=64) for s in range(2)]
-        xsg = keep.tile([P, 4 * C], U8, name="xsg", align_bytes=64)
-        dysg = keep.tile([P, 4 * C], U8, name="dysg", align_bytes=64)
-        dx = [keep.tile([P, 4, C], F32, name="dx%d" % e, align_bytes=64) for e in range(E)]
+        w1 = [keep.tile([P, H], I32, name="w1_%d" % e, align_bytes=64) for e in range(E)]
+        w3 = [keep.tile([P, H], I32, name="w3_%d" % e, align_bytes=64) for e in range(E)]
+        w2 = [keep.tile([P, 2, H], I32, name="w2_%d" % e, align_bytes=64) for e in range(E)]
+        w1t = [keep.tile([P, K], I32, name="w1t_%d" % e, align_bytes=64) for e in range(E)]
+        w3t = [keep.tile([P, K], I32, name="w3t_%d" % e, align_bytes=64) for e in range(E)]
+        xg = keep.tile([P, E * C], U32, name="xg", align_bytes=64)
+        dyg = [keep.tile([P, E * C], U32, name="dyg%d" % s, align_bytes=64) for s in range(2)]
+        xsg = keep.tile([P, E * C], U8, name="xsg", align_bytes=64)
+        dysg = keep.tile([P, E * C], U8, name="dysg", align_bytes=64)
+        dx = [[keep.tile([P, 2, C], F32, name="dx%d_%d" % (e, h), align_bytes=64) for h in range(2)] for e in range(E)]
         win = [keep.tile([P, T], F32, name="win%d" % j, align_bytes=64) for j in range(4)]
 
-        def load_words(eng, dst, src, a0, a1):
-            eng.dma_start(dst[:, a0:a1, :], src.rearrange("e s p n d -> p (e s) (n d)").bitcast(I32)[:, a0:a1, :])
+        def words(src):
+            return src.rearrange("s p n d -> p s (n d)").bitcast(I32)
 
-        def load_packed(eng, j, scales):
-            for q in range(4):
-                eng.dma_start(
-                    ws[32 * q : 32 * q + 16, j, :].bitcast(I32),
-                    scales[:, 0, 4 * q : 4 * q + 4, :].bitcast(I32),
-                )
+        def load_words(dst, src):
+            nc.sync.dma_start(dst[:], src[0].rearrange("p n d -> p (n d)").bitcast(I32))
 
-        nc.vector.memset(xs[:].bitcast(I32), 0)
-        nc.vector.memset(ws[:, 0:2, :].rearrange("p a n -> p (a n)").bitcast(I32), 0)
-        nc.vector.memset(w2s[:].rearrange("p a n -> p (a n)").bitcast(I32), 0)
-        nc.vector.memset(dys[:].bitcast(I32), 0)
-        nc.gpsimd.memset(ws[:, 2:4, :].rearrange("p a n -> p (a n)").bitcast(I32), 0)
+        def load_quadrant(eng, dst, planes, q):
+            count = planes.shape[0]
+            eng.dma_start(dst[32 * q : 32 * q + 4 * count, :].bitcast(I32), planes[:, 4 * q : 4 * q + 4, :].bitcast(I32))
+
+        def load_first(e):
+            load_words(w1[e], w1_words[e])
+            load_words(w3[e], w3_words[e])
+            nc.sync.dma_start(w2[e][:], words(w2t_words[e]))
+
+        def load_back(e):
+            load_words(w3t[e], w3t_words[e])
+            load_words(w1t[e], w1t_words[e])
+
+        for plane in (xs, dys, w1s, w3s):
+            nc.vector.memset(plane[:].bitcast(I32), 0)
+        nc.gpsimd.memset(w2s[:].rearrange("p a n -> p (a n)").bitcast(I32), 0)
+        for plane in (w1ts, w3ts):
+            nc.vector.memset(plane[:].bitcast(I32), 0)
 
         nc.sync.dma_start(offsets[:], offs)
-        nc.sync.dma_start(xw[:], x_words[0].rearrange("p n d -> p (n d)").bitcast(I32))
-        nc.gpsimd.dma_start(xs[32 * 3 : 32 * 3 + 4, :].bitcast(I32), x_scales[0, 4 * 3 : 4 * 3 + 4, :].bitcast(I32))
-        nc.gpsimd.dma_start(ws[32 * 2 : 32 * 2 + 16, 0, :].bitcast(I32), w1_scales[:, 0, 4 * 2 : 4 * 2 + 4, :].bitcast(I32))
-        nc.gpsimd.dma_start(ws[32 * 1 : 32 * 1 + 16, 0, :].bitcast(I32), w1_scales[:, 0, 4 * 1 : 4 * 1 + 4, :].bitcast(I32))
-        nc.sync.dma_start(xs[32 * 1 : 32 * 1 + 4, :].bitcast(I32), x_scales[0, 4 * 1 : 4 * 1 + 4, :].bitcast(I32))
-        nc.sync.dma_start(xs[32 * 2 : 32 * 2 + 4, :].bitcast(I32), x_scales[0, 4 * 2 : 4 * 2 + 4, :].bitcast(I32))
-        nc.gpsimd.dma_start(w2s[32 * 3 : 32 * 3 + 16, 0, :].bitcast(I32), w2t_scales.rearrange("e s b n -> (e s) b n")[0:4, 4 * 3 : 4 * 3 + 4, :].bitcast(I32))
-        nc.gpsimd.dma_start(dys[32 * 0 : 32 * 0 + 8, :].bitcast(I32), dy_scales[:, 4 * 0 : 4 * 0 + 4, :].bitcast(I32))
-        nc.sync.dma_start(xs[32 * 0 : 32 * 0 + 4, :].bitcast(I32), x_scales[0, 4 * 0 : 4 * 0 + 4, :].bitcast(I32))
-        nc.gpsimd.dma_start(ws[32 * 3 : 32 * 3 + 16, 1, :].bitcast(I32), w3_scales[:, 0, 4 * 3 : 4 * 3 + 4, :].bitcast(I32))
-        nc.sync.dma_start(ws[32 * 3 : 32 * 3 + 16, 0, :].bitcast(I32), w1_scales[:, 0, 4 * 3 : 4 * 3 + 4, :].bitcast(I32))
-        nc.sync.dma_start(dyw[:], dy_words.rearrange("s p n d -> p s (n d)").bitcast(I32))
-        load_words(nc.sync, w3, w3_words, 0, 1)
-        nc.sync.dma_start(ws[32 * 0 : 32 * 0 + 16, 0, :].bitcast(I32), w1_scales[:, 0, 4 * 0 : 4 * 0 + 4, :].bitcast(I32))
-        nc.sync.dma_start(dys[32 * 1 : 32 * 1 + 8, :].bitcast(I32), dy_scales[:, 4 * 1 : 4 * 1 + 4, :].bitcast(I32))
-        nc.sync.dma_start(ws[32 * 2 : 32 * 2 + 16, 2, :].bitcast(I32), w1t_scales[:, 0, 4 * 2 : 4 * 2 + 4, :].bitcast(I32))
-        nc.sync.dma_start(w2s[32 * 1 : 32 * 1 + 16, 0, :].bitcast(I32), w2t_scales.rearrange("e s b n -> (e s) b n")[0:4, 4 * 1 : 4 * 1 + 4, :].bitcast(I32))
-        nc.sync.dma_start(w2s[32 * 0 : 32 * 0 + 16, 0, :].bitcast(I32), w2t_scales.rearrange("e s b n -> (e s) b n")[0:4, 4 * 0 : 4 * 0 + 4, :].bitcast(I32))
-        load_words(nc.sync, w1, w1_words, 0, 2)
-        nc.sync.dma_start(ws[32 * 2 : 32 * 2 + 16, 1, :].bitcast(I32), w3_scales[:, 0, 4 * 2 : 4 * 2 + 4, :].bitcast(I32))
-        nc.sync.dma_start(dys[32 * 3 : 32 * 3 + 8, :].bitcast(I32), dy_scales[:, 4 * 3 : 4 * 3 + 4, :].bitcast(I32))
-        nc.sync.dma_start(ws[32 * 0 : 32 * 0 + 16, 1, :].bitcast(I32), w3_scales[:, 0, 4 * 0 : 4 * 0 + 4, :].bitcast(I32))
-        make_identity(nc, ident[:])
-        nc.sync.dma_start(w2s[32 * 2 : 32 * 2 + 16, 0, :].bitcast(I32), w2t_scales.rearrange("e s b n -> (e s) b n")[0:4, 4 * 2 : 4 * 2 + 4, :].bitcast(I32))
-        nc.sync.dma_start(dys[32 * 2 : 32 * 2 + 8, :].bitcast(I32), dy_scales[:, 4 * 2 : 4 * 2 + 4, :].bitcast(I32))
-        nc.sync.dma_start(ws[32 * 1 : 32 * 1 + 16, 1, :].bitcast(I32), w3_scales[:, 0, 4 * 1 : 4 * 1 + 4, :].bitcast(I32))
-        load_words(nc.sync, w2, w2t_words, 0, 2)
-        nc.gpsimd.dma_start(ws[32 * 1 : 32 * 1 + 16, 3, :].bitcast(I32), w3t_scales[:, 0, 4 * 1 : 4 * 1 + 4, :].bitcast(I32))
-        nc.gpsimd.dma_start(ws[32 * 0 : 32 * 0 + 16, 3, :].bitcast(I32), w3t_scales[:, 0, 4 * 0 : 4 * 0 + 4, :].bitcast(I32))
-        load_words(nc.sync, w1, w1_words, 2, 3)
-        load_words(nc.sync, w3, w3_words, 1, 2)
-        load_words(nc.sync, w1t, w1t_words, 0, 1)
-        load_words(nc.sync, w3, w3_words, 2, 4)
-        nc.sync.dma_start(ws[32 * 2 : 32 * 2 + 16, 3, :].bitcast(I32), w3t_scales[:, 0, 4 * 2 : 4 * 2 + 4, :].bitcast(I32))
-        nc.sync.dma_start(ws[32 * 1 : 32 * 1 + 16, 2, :].bitcast(I32), w1t_scales[:, 0, 4 * 1 : 4 * 1 + 4, :].bitcast(I32))
-        load_words(nc.sync, w2, w2t_words, 2, 4)
+        load_words(xw, x_words)
+        nc.sync.dma_start(dyw[:], words(dy_words))
+        for q in range(4):
+            load_quadrant(nc.scalar, xs, x_scales, q)
+        load_first(0)
+        for q in range(4):
+            load_quadrant(nc.scalar, dys, dy_scales, q)
+        for dst, src in ((w1s, w1_scales), (w3s, w3_scales)):
+            for q in range(4):
+                load_quadrant(nc.scalar if q % 2 else nc.sync, dst, src[:, 0], q)
         with nc.allow_non_contiguous_dma(reason="one gate value a partition"):
-            nc.scalar.dma_start(
-                gcol[:],
-                gate.rearrange("r c -> (r c)")[0 : E * (T + C)].rearrange("(e x) -> x e", x=T + C)[0:P, :],
-            )
-        load_words(nc.sync, w3t, w3t_words, 0, 1)
-        nc.sync.dma_start(ws[32 * 0 : 32 * 0 + 16, 2, :].bitcast(I32), w1t_scales[:, 0, 4 * 0 : 4 * 0 + 4, :].bitcast(I32))
-        nc.sync.dma_start(w2s[32 * 1 : 32 * 1 + 16, 1, :].bitcast(I32), w2t_scales.rearrange("e s b n -> (e s) b n")[4:8, 4 * 1 : 4 * 1 + 4, :].bitcast(I32))
-        load_words(nc.sync, w2, w2t_words, 4, 6)
-        load_words(nc.sync, w2, w2t_words, 6, 8)
-        nc.sync.dma_start(w2s[32 * 3 : 32 * 3 + 16, 1, :].bitcast(I32), w2t_scales.rearrange("e s b n -> (e s) b n")[4:8, 4 * 3 : 4 * 3 + 4, :].bitcast(I32))
-        load_words(nc.sync, w1, w1_words, 3, 4)
-        load_words(nc.sync, w3t, w3t_words, 1, 2)
-        load_words(nc.sync, w1t, w1t_words, 1, 2)
-        load_words(nc.sync, w1t, w1t_words, 2, 4)
-        nc.gpsimd.dma_start(ws[32 * 3 : 32 * 3 + 16, 3, :].bitcast(I32), w3t_scales[:, 0, 4 * 3 : 4 * 3 + 4, :].bitcast(I32))
-        nc.gpsimd.dma_start(ws[32 * 3 : 32 * 3 + 16, 2, :].bitcast(I32), w1t_scales[:, 0, 4 * 3 : 4 * 3 + 4, :].bitcast(I32))
-        load_words(nc.sync, w3t, w3t_words, 3, 4)
-        nc.gpsimd.dma_start(w2s[32 * 0 : 32 * 0 + 16, 1, :].bitcast(I32), w2t_scales.rearrange("e s b n -> (e s) b n")[4:8, 4 * 0 : 4 * 0 + 4, :].bitcast(I32))
-        load_words(nc.sync, w3t, w3t_words, 2, 3)
-        nc.gpsimd.dma_start(w2s[32 * 2 : 32 * 2 + 16, 1, :].bitcast(I32), w2t_scales.rearrange("e s b n -> (e s) b n")[4:8, 4 * 2 : 4 * 2 + 4, :].bitcast(I32))
+            nc.scalar.dma_start(gcol[:], gate[0].rearrange("(e c) -> c e", e=E))
+        w2_planes = w2t_scales.rearrange("e s (q r) n -> r q (e s) n", r=4)
+        for r in range(4):
+            nc.gpsimd.dma_start(w2s[r:P:32].bitcast(I32), w2_planes[r].bitcast(I32))
+        make_identity(nc, ident[:])
+        for q in range(4):
+            load_quadrant(nc.gpsimd, w3ts, w3t_scales[:, 0], q)
+        for q in (1, 3):
+            load_quadrant(nc.scalar, w1ts, w1t_scales[:, 0], q)
+        load_first(1)
+        for q in (0, 2):
+            load_quadrant(nc.sync, w1ts, w1t_scales[:, 0], q)
+        for e in range(E):
+            load_back(e)
+            if e + 2 < E:
+                load_first(e + 2)
 
-        def ring(e0, e1):
-            return slice(e0 % RING * C, ((e1 - 1) % RING + 1) * C)
+        def slots(e):
+            return slice(e * C, (e + 1) * C)
 
-        def gather_x(e0, e1):
-            lst = offsets[:, e0 * C // 16 : e1 * C // 16]
-            nc.vector.tensor_copy(xg[:, ring(e0, e1)], xw[:].bitcast(U32).indirect(lst))
-            nc.vector.tensor_copy(xsg[:, ring(e0, e1)], xs[:].indirect(lst))
+        def listed(e):
+            return offsets[:, e * C // 16 : (e + 1) * C // 16]
 
-        def gather_dy(e0, e1):
-            lst = offsets[:, e0 * C // 16 : e1 * C // 16]
+        def gather_x(e):
+            nc.vector.tensor_copy(xg[:, slots(e)], xw[:].bitcast(U32).indirect(listed(e)))
+            nc.vector.tensor_copy(xsg[:, slots(e)], xs[:].indirect(listed(e)))
+
+        def gather_dy(e):
             for s in range(2):
-                nc.vector.tensor_copy(dyg[s][:, ring(e0, e1)], dyw[:, s, :].bitcast(U32).indirect(lst))
-            nc.vector.tensor_copy(dysg[:, ring(e0, e1)], dys[:].indirect(lst))
+                nc.vector.tensor_copy(dyg[s][:, slots(e)], dyw[:, s, :].bitcast(U32).indirect(listed(e)))
+            nc.vector.tensor_copy(dysg[:, slots(e)], dys[:].indirect(listed(e)))
 
         def by_byte(sums):
             return sums[:].rearrange("p (m d) -> p d m", d=4)
 
         def first(e):
-            cols = ring(e, e + 1)
-            a1, dh, a3 = bank[A1B[e]], bank[DHB[e]], bank[A3B[e]]
-            nc.tensor.matmul_mx(a1[:], lhsT=xg[:, cols].bitcast(X4), lhsT_scale=xsg[:, cols],
-                                rhs=w1[:, e, :].bitcast(X4), rhs_scale=ws[4 * e : P, 0, :], start=True, stop=True)
-            nc.tensor.matmul_mx(a3[:], lhsT=xg[:, cols].bitcast(X4), lhsT_scale=xsg[:, cols],
-                                rhs=w3[:, e, :].bitcast(X4), rhs_scale=ws[4 * e : P, 1, :], start=True, stop=True)
+            cols = slots(e)
+            for acc, w, ws in ((a1_bank[e % 2], w1, w1s), (a3_bank[e % 2], w3, w3s)):
+                nc.tensor.matmul_mx(acc[:], lhsT=xg[:, cols].bitcast(X4), lhsT_scale=xsg[:, cols],
+                                    rhs=w[e][:].bitcast(X4), rhs_scale=ws[4 * e : P, :], start=True, stop=True)
             for s in range(2):
-                nc.tensor.matmul_mx(dh[:], lhsT=dyg[s][:, cols].bitcast(X4), lhsT_scale=dysg[4 * s : P, cols],
-                                    rhs=w2[:, 2 * e + s, :].bitcast(X4), rhs_scale=w2s[4 * ((2 * e + s) % 4) : P, e // 2, :],
+                nc.tensor.matmul_mx(dh_bank[e % 2][:], lhsT=dyg[s][:, cols].bitcast(X4), lhsT_scale=dysg[4 * s : P, cols],
+                                    rhs=w2[e][:, s, :].bitcast(X4), rhs_scale=w2s[:, 2 * e + s, :],
                                     start=(s == 0), stop=(s == 1))
 
         def products(e):
-            a1, dh, a3 = bank[A1B[e]], bank[DHB[e]], bank[A3B[e]]
+            a1, a3, dh = a1_bank[e % 2], a3_bank[e % 2], dh_bank[e % 2]
             sig = work.tile([P, 4, C], F32, name="sig")
             da3 = work.tile([P, 4, C], F32, name="da3")
             u = work.tile([P, 4, C], F32, name="u")
             nda1 = work.tile([P, 4, C], F32, name="nda1")
             nc.scalar.activation(sig[:], by_byte(a1), ACT.Sigmoid)
-            if PATHS[e] == "P":
-                nsig = work.tile([P, 4, C], F32, name="nsig")
-                na3 = work.tile([P, 4, C], F32, name="na3")
-                nc.scalar.activation(nsig[:], by_byte(a1), ACT.Sigmoid, scale=-1.0)
-                nc.scalar.activation(na3[:], by_byte(a3), ACT.Copy, scale=-1.0)
-                nc.gpsimd.tensor_tensor(u[:], na3[:], nsig[:], MULT)
-            else:
-                nc.vector.scalar_tensor_tensor(u[:], sig[:], 1.0, by_byte(a3), SUB, MULT)
-            if PATHS[e] in "VW":
-                nc.vector.scalar_tensor_tensor(da3[:], by_byte(dh), gcol[:, e : e + 1], sig[:], MULT, MULT)
-            else:
-                dhg = work.tile([P, 4, C], F32, name="dhg")
-                nc.scalar.activation(dhg[:], by_byte(dh), ACT.Copy, scale=gcol[:, e : e + 1])
-                nc.gpsimd.tensor_tensor(da3[:], dhg[:], sig[:], MULT)
-            last = nc.vector if PATHS[e] == "V" else nc.gpsimd
-            last.tensor_tensor(nda1[:], da3[:], u[:], MULT)
+            nc.vector.scalar_tensor_tensor(da3[:], by_byte(dh), gcol[:, e : e + 1], sig[:], MULT, MULT)
+            nc.vector.scalar_tensor_tensor(u[:], sig[:], 1.0, by_byte(a3), SUB, MULT)
+            nc.vector.tensor_tensor(nda1[:], da3[:], u[:], MULT)
             made[e] = (da3, nda1)
 
         def turn(e):
             da3, nda1 = made[e]
             dab = work.tile([P, 2, C, 4], BF16, name="dab", align_bytes=64)
-            for j, (src, turned, sign) in enumerate(((da3, bank[T3B[e]], 1.0), (nda1, bank[T1B[e]], -1.0))):
+            for j, (src, turned, sign) in enumerate(((da3, t3_bank, 1.0), (nda1, t1_bank, -1.0))):
                 for d in range(4):
                     nc.tensor.transpose(turned[:, d * C : (d + 1) * C], src[:, d, :], ident[:])
                 nc.scalar.activation(dab[:, j, :, :], turned[:].rearrange("p (d c) -> p c d", d=4), ACT.Copy, scale=sign)
@@ -199,48 +164,36 @@ def tile_moe_rec_glu_sigmoid_kernel(
 
         def back(e, half):
             daw, das = packed[e]
-            acc = bank[ACCB[e][half]]
+            acc = t1_bank if half else dh_bank[(e + 1) % 2]
             for h in range(2):
                 kt = 2 * half + h
                 kc = slice(kt * P, (kt + 1) * P)
-                for j, (w, plane) in enumerate(((w3t, 3), (w1t, 2))):
+                for j, (w, ws) in enumerate(((w3t, w3ts), (w1t, w1ts))):
                     dc = slice(j * C, (j + 1) * C)
-                    nc.tensor.matmul_mx(acc[:, h * C : (h + 1) * C], lhsT=w[:, e, kc].bitcast(X4),
-                                        lhsT_scale=ws[4 * e : P, plane, kc],
+                    nc.tensor.matmul_mx(acc[:, h * C : (h + 1) * C], lhsT=w[e][:, kc].bitcast(X4),
+                                        lhsT_scale=ws[4 * e : P, kc],
                                         rhs=daw[:, dc].bitcast(X4), rhs_scale=das[:, dc], start=(j == 0), stop=(j == 1))
-            nc.scalar.copy(dx[e][:, 2 * half : 2 * half + 2, :].rearrange("p h c -> p (h c)"), acc[:, 0 : 2 * C])
-
-        made, packed = {}, {}
-        gather_x(0, 0 + 1)
-        gather_dy(0, 0 + 1)
-        first(0)
-        products(0)
-        gather_x(1, 1 + 1)
-        gather_dy(1, 1 + 1)
-        first(1)
-        products(1)
-        gather_x(2, 3 + 1)
-        gather_dy(2, 3 + 1)
-        turn(0)
-        back(0, 0)
-        back(0, 1)
-        first(2)
-        products(2)
-        turn(1)
-        back(1, 0)
-        back(1, 1)
-        first(3)
-        products(3)
-        turn(2)
-        back(2, 0)
-        back(2, 1)
-        turn(3)
-        back(3, 0)
-        back(3, 1)
-
-        for e in range(E):
-            lst = offsets[:, e * C // 16 : (e + 1) * C // 16]
-            for kt in range(4):
-                nc.vector.tensor_copy(win[kt][:].indirect(lst), dx[e][:, kt, :])
+            nc.scalar.copy(dx[e][half][:].rearrange("p h c -> p (h c)"), acc[:, 0 : 2 * C])
+            for h in range(2):
+                kt = 2 * half + h
+                nc.vector.tensor_copy(win[kt][:].indirect(listed(e)), dx[e][half][:, h, :])
                 if e == E - 1:
                     nc.sync.dma_start(out[kt * P : (kt + 1) * P, :], win[kt][:])
+
+        made, packed = {}, {}
+        for e in range(E):
+            gather_x(e)
+            gather_dy(e)
+        first(0)
+        products(0)
+        first(1)
+        products(1)
+        turn(0)
+        for e in range(E):
+            back(e, 0)
+            if e + 1 < E:
+                turn(e + 1)
+            if e + 2 < E:
+                first(e + 2)
+                products(e + 2)
+            back(e, 1)

@@ -18,6 +18,7 @@ MULT = mybir.AluOpType.mult
 SUB = mybir.AluOpType.subtract
 
 P = 128
+ON_VECTOR = 2
 
 
 def tile_moe_rec_glu_sigmoid_kernel(
@@ -30,7 +31,7 @@ def tile_moe_rec_glu_sigmoid_kernel(
         work = ctx.enter_context(tc.tile_pool(name="work", bufs=4))
         psum = ctx.enter_context(tc.psum_pool(name="psum", bufs=1))
         bank = [psum.tile([P, H], F32, name="bank%d" % b) for b in range(8)]
-        a1_bank, a3_bank, dh_bank, t3_bank, t1_bank = bank[0:2], bank[2:4], bank[4:6], bank[6], bank[7]
+        a1_bank, a3_bank, dh_bank, t3_bank, t1_bank, dx_bank = bank[0], bank[1:3], bank[3:5], bank[5], bank[6], bank[7]
 
         offsets = keep.tile([P, T // 16], U16, name="offsets")
         xw = keep.tile([P, T], I32, name="xw", align_bytes=64)
@@ -39,7 +40,7 @@ def tile_moe_rec_glu_sigmoid_kernel(
         dys = keep.tile([P, T], U8, name="dys", align_bytes=64)
         w1s = keep.tile([P, H], U8, name="w1s", align_bytes=64)
         w3s = keep.tile([P, H], U8, name="w3s", align_bytes=64)
-        w2s = keep.tile([P, 2 * E, H], U8, name="w2s", align_bytes=64)
+        w2s = [keep.tile([P, H], U8, name="w2s%d" % j, align_bytes=64) for j in range(2)]
         w1ts = keep.tile([P, K], U8, name="w1ts", align_bytes=64)
         w3ts = keep.tile([P, K], U8, name="w3ts", align_bytes=64)
         gcol = keep.tile([P, E], F32, name="gcol")
@@ -50,10 +51,9 @@ def tile_moe_rec_glu_sigmoid_kernel(
         w1t = [keep.tile([P, K], I32, name="w1t_%d" % e, align_bytes=64) for e in range(E)]
         w3t = [keep.tile([P, K], I32, name="w3t_%d" % e, align_bytes=64) for e in range(E)]
         xg = keep.tile([P, E * C], U32, name="xg", align_bytes=64)
-        dyg = [keep.tile([P, E * C], U32, name="dyg%d" % s, align_bytes=64) for s in range(2)]
+        dyg = [keep.tile([P, 2 * C], U32, name="dyg%d" % s, align_bytes=64) for s in range(2)]
         xsg = keep.tile([P, E * C], U8, name="xsg", align_bytes=64)
-        dysg = keep.tile([P, E * C], U8, name="dysg", align_bytes=64)
-        dx = [[keep.tile([P, 2, C], F32, name="dx%d_%d" % (e, h), align_bytes=64) for h in range(2)] for e in range(E)]
+        dysg = keep.tile([P, 2 * C], U8, name="dysg", align_bytes=64)
         win = [keep.tile([P, T], F32, name="win%d" % j, align_bytes=64) for j in range(4)]
 
         def words(src):
@@ -66,49 +66,47 @@ def tile_moe_rec_glu_sigmoid_kernel(
             count = planes.shape[0]
             eng.dma_start(dst[32 * q : 32 * q + 4 * count, :].bitcast(I32), planes[:, 4 * q : 4 * q + 4, :].bitcast(I32))
 
-        def load_first(e):
-            load_words(w1[e], w1_words[e])
-            load_words(w3[e], w3_words[e])
-            nc.sync.dma_start(w2[e][:], words(w2t_words[e]))
+        def first_loads(e):
+            return [
+                lambda: load_words(w1[e], w1_words[e]),
+                lambda: load_words(w3[e], w3_words[e]),
+                lambda: nc.sync.dma_start(w2[e][:], words(w2t_words[e])),
+            ]
 
-        def load_back(e):
-            load_words(w3t[e], w3t_words[e])
-            load_words(w1t[e], w1t_words[e])
+        def back_loads(e):
+            return [lambda: load_words(w3t[e], w3t_words[e]), lambda: load_words(w1t[e], w1t_words[e])]
 
-        for plane in (xs, dys, w1s, w3s):
+        def quadrant_loads(dst, planes, quadrants=range(4), eng=nc.sync):
+            return [lambda q=q: load_quadrant(eng, dst, planes, q) for q in quadrants]
+
+        def weave(large, small, each):
+            for j, load in enumerate(large):
+                load()
+                for little in small[j * each : (j + 1) * each]:
+                    little()
+            for little in small[len(large) * each :]:
+                little()
+
+        w2_planes = w2t_scales.rearrange("e s b n -> (e s) b n")
+        nc.gpsimd.memset(w1s[:].bitcast(I32), 0)
+        for plane in (xs, dys, w3s, w2s[0], w1ts, w3ts, w2s[1]):
             nc.vector.memset(plane[:].bitcast(I32), 0)
-        nc.gpsimd.memset(w2s[:].rearrange("p a n -> p (a n)").bitcast(I32), 0)
-        for plane in (w1ts, w3ts):
-            nc.vector.memset(plane[:].bitcast(I32), 0)
+        weave([], quadrant_loads(w1s, w1_scales[:, 0], eng=nc.gpsimd) + quadrant_loads(w3s, w3_scales[:, 0], [0, 1], eng=nc.gpsimd), 0)
+        make_identity(nc, ident[:])
+        weave([], quadrant_loads(w3ts, w3t_scales[:, 0], eng=nc.gpsimd) + quadrant_loads(w2s[1], w2_planes[4:8], eng=nc.gpsimd), 0)
 
+        w1_0, w3_0, w2_0 = first_loads(0)
         nc.sync.dma_start(offsets[:], offs)
         load_words(xw, x_words)
+        weave([], quadrant_loads(xs, x_scales), 0)
         nc.sync.dma_start(dyw[:], words(dy_words))
-        for q in range(4):
-            load_quadrant(nc.scalar, xs, x_scales, q)
-        load_first(0)
-        for q in range(4):
-            load_quadrant(nc.scalar, dys, dy_scales, q)
-        for dst, src in ((w1s, w1_scales), (w3s, w3_scales)):
-            for q in range(4):
-                load_quadrant(nc.scalar if q % 2 else nc.sync, dst, src[:, 0], q)
+        weave([w1_0, w2_0], quadrant_loads(dys, dy_scales) + quadrant_loads(w2s[0], w2_planes[0:4]), 4)
+        weave([w3_0], quadrant_loads(w3s, w3_scales[:, 0], [2, 3]), 4)
         with nc.allow_non_contiguous_dma(reason="one gate value a partition"):
-            nc.scalar.dma_start(gcol[:], gate[0].rearrange("(e c) -> c e", e=E))
-        w2_planes = w2t_scales.rearrange("e s (q r) n -> r q (e s) n", r=4)
-        for r in range(4):
-            nc.gpsimd.dma_start(w2s[r:P:32].bitcast(I32), w2_planes[r].bitcast(I32))
-        make_identity(nc, ident[:])
-        for q in range(4):
-            load_quadrant(nc.gpsimd, w3ts, w3t_scales[:, 0], q)
-        for q in (1, 3):
-            load_quadrant(nc.scalar, w1ts, w1t_scales[:, 0], q)
-        load_first(1)
-        for q in (0, 2):
-            load_quadrant(nc.sync, w1ts, w1t_scales[:, 0], q)
-        for e in range(E):
-            load_back(e)
-            if e + 2 < E:
-                load_first(e + 2)
+            nc.sync.dma_start(
+                gcol[:], gate.rearrange("r c -> (r c)")[0 : E * (T + C)].rearrange("(e x) -> x e", x=T + C)[0:P, :])
+        weave(first_loads(1), quadrant_loads(w1ts, w1t_scales[:, 0]), 2)
+        weave(back_loads(0) + first_loads(2) + back_loads(1) + first_loads(3) + back_loads(2) + back_loads(3), [], 0)
 
         def slots(e):
             return slice(e * C, (e + 1) * C)
@@ -122,32 +120,32 @@ def tile_moe_rec_glu_sigmoid_kernel(
 
         def gather_dy(e):
             for s in range(2):
-                nc.vector.tensor_copy(dyg[s][:, slots(e)], dyw[:, s, :].bitcast(U32).indirect(listed(e)))
-            nc.vector.tensor_copy(dysg[:, slots(e)], dys[:].indirect(listed(e)))
+                nc.vector.tensor_copy(dyg[s][:, slots(e % 2)], dyw[:, s, :].bitcast(U32).indirect(listed(e)))
+            nc.vector.tensor_copy(dysg[:, slots(e % 2)], dys[:].indirect(listed(e)))
 
         def by_byte(sums):
             return sums[:].rearrange("p (m d) -> p d m", d=4)
 
         def first(e):
             cols = slots(e)
-            for acc, w, ws in ((a1_bank[e % 2], w1, w1s), (a3_bank[e % 2], w3, w3s)):
+            for acc, w, ws in ((a1_bank, w1, w1s), (a3_bank[e % 2], w3, w3s)):
                 nc.tensor.matmul_mx(acc[:], lhsT=xg[:, cols].bitcast(X4), lhsT_scale=xsg[:, cols],
                                     rhs=w[e][:].bitcast(X4), rhs_scale=ws[4 * e : P, :], start=True, stop=True)
             for s in range(2):
-                nc.tensor.matmul_mx(dh_bank[e % 2][:], lhsT=dyg[s][:, cols].bitcast(X4), lhsT_scale=dysg[4 * s : P, cols],
-                                    rhs=w2[e][:, s, :].bitcast(X4), rhs_scale=w2s[:, 2 * e + s, :],
+                nc.tensor.matmul_mx(dh_bank[e % 2][:], lhsT=dyg[s][:, slots(e % 2)].bitcast(X4), lhsT_scale=dysg[4 * s : P, slots(e % 2)],
+                                    rhs=w2[e][:, s, :].bitcast(X4), rhs_scale=w2s[e // 2][4 * (2 * (e % 2) + s) : P, :],
                                     start=(s == 0), stop=(s == 1))
 
         def products(e):
-            a1, a3, dh = a1_bank[e % 2], a3_bank[e % 2], dh_bank[e % 2]
-            sig = work.tile([P, 4, C], F32, name="sig")
+            a1, a3, dh = a1_bank, a3_bank[e % 2], dh_bank[e % 2]
+            sig = keep.tile([P, 4, C], F32, name="sig%d" % e, tag="after_sig%d" % e)
             da3 = work.tile([P, 4, C], F32, name="da3")
-            u = work.tile([P, 4, C], F32, name="u")
+            u = keep.tile([P, 4, C], F32, name="u%d" % e, tag="before_u%d" % e)
             nda1 = work.tile([P, 4, C], F32, name="nda1")
             nc.scalar.activation(sig[:], by_byte(a1), ACT.Sigmoid)
-            nc.vector.scalar_tensor_tensor(da3[:], by_byte(dh), gcol[:, e : e + 1], sig[:], MULT, MULT)
             nc.vector.scalar_tensor_tensor(u[:], sig[:], 1.0, by_byte(a3), SUB, MULT)
-            nc.vector.tensor_tensor(nda1[:], da3[:], u[:], MULT)
+            nc.vector.scalar_tensor_tensor(da3[:], by_byte(dh), gcol[:, e : e + 1], sig[:], MULT, MULT)
+            (nc.vector if e < ON_VECTOR else nc.gpsimd).tensor_tensor(nda1[:], da3[:], u[:], MULT)
             made[e] = (da3, nda1)
 
         def turn(e):
@@ -164,7 +162,7 @@ def tile_moe_rec_glu_sigmoid_kernel(
 
         def back(e, half):
             daw, das = packed[e]
-            acc = t1_bank if half else dh_bank[(e + 1) % 2]
+            acc = t1_bank if half else dx_bank
             for h in range(2):
                 kt = 2 * half + h
                 kc = slice(kt * P, (kt + 1) * P)
@@ -173,21 +171,28 @@ def tile_moe_rec_glu_sigmoid_kernel(
                     nc.tensor.matmul_mx(acc[:, h * C : (h + 1) * C], lhsT=w[e][:, kc].bitcast(X4),
                                         lhsT_scale=ws[4 * e : P, kc],
                                         rhs=daw[:, dc].bitcast(X4), rhs_scale=das[:, dc], start=(j == 0), stop=(j == 1))
-            nc.scalar.copy(dx[e][half][:].rearrange("p h c -> p (h c)"), acc[:, 0 : 2 * C])
             for h in range(2):
                 kt = 2 * half + h
-                nc.vector.tensor_copy(win[kt][:].indirect(listed(e)), dx[e][half][:, h, :])
+                tag = ("after_sig%d" % (e + 1), "before_u%d" % (e + 2), "after_sig%d" % (e + 2), "last%d" % e)[kt]
+                if kt == 0 and e == 0:
+                    tag = "first"
+                dx = keep.tile([P, C], F32, name="dx%d_%d" % (e, kt), tag=tag)
+                nc.scalar.copy(dx[:], acc[:, h * C : (h + 1) * C])
+                nc.vector.tensor_copy(win[kt][:].indirect(listed(e)), dx[:])
                 if e == E - 1:
                     nc.sync.dma_start(out[kt * P : (kt + 1) * P, :], win[kt][:])
 
         made, packed = {}, {}
         for e in range(E):
             gather_x(e)
-            gather_dy(e)
+        gather_dy(0)
+        gather_dy(1)
         first(0)
+        gather_dy(2)
         products(0)
         first(1)
         products(1)
+        gather_dy(3)
         turn(0)
         for e in range(E):
             back(e, 0)

@@ -15,6 +15,7 @@ U8 = mybir.dt.uint8
 X4 = mybir.dt.float8_e4m3fn_x4
 ACT = mybir.ActivationFunctionType
 MULT = mybir.AluOpType.mult
+ADD = mybir.AluOpType.add
 SUB = mybir.AluOpType.subtract
 
 P = 128
@@ -31,7 +32,7 @@ def tile_moe_rec_glu_sigmoid_kernel(
         work = ctx.enter_context(tc.tile_pool(name="work", bufs=4))
         psum = ctx.enter_context(tc.psum_pool(name="psum", bufs=1))
         bank = [psum.tile([P, H], F32, name="bank%d" % b) for b in range(8)]
-        a1_bank, a3_bank, dh_bank, t3_bank, t1_bank, dx_bank = bank[0], bank[1:3], bank[3:5], bank[5], bank[6], bank[7]
+        a1_bank, a3_bank, dh_bank, t1_bank, dx_bank = bank[0:2], bank[2:4], bank[4:6], bank[6], bank[7]
 
         offsets = keep.tile([P, T // 16], U16, name="offsets")
         xw = keep.tile([P, T], I32, name="xw", align_bytes=64)
@@ -51,9 +52,7 @@ def tile_moe_rec_glu_sigmoid_kernel(
         w1t = [keep.tile([P, K], I32, name="w1t_%d" % e, align_bytes=64) for e in range(E)]
         w3t = [keep.tile([P, K], I32, name="w3t_%d" % e, align_bytes=64) for e in range(E)]
         xg = keep.tile([P, E * C], U32, name="xg", align_bytes=64)
-        dyg = [keep.tile([P, 2 * C], U32, name="dyg%d" % s, align_bytes=64) for s in range(2)]
         xsg = keep.tile([P, E * C], U8, name="xsg", align_bytes=64)
-        dysg = keep.tile([P, 2 * C], U8, name="dysg", align_bytes=64)
         win = [keep.tile([P, T], F32, name="win%d" % j, align_bytes=64) for j in range(4)]
 
         def words(src):
@@ -91,22 +90,26 @@ def tile_moe_rec_glu_sigmoid_kernel(
         nc.gpsimd.memset(w1s[:].bitcast(I32), 0)
         for plane in (xs, dys, w3s, w2s[0], w1ts, w3ts, w2s[1]):
             nc.vector.memset(plane[:].bitcast(I32), 0)
-        weave([], quadrant_loads(w1s, w1_scales[:, 0], eng=nc.gpsimd) + quadrant_loads(w3s, w3_scales[:, 0], [0, 1], eng=nc.gpsimd), 0)
+        weave([], quadrant_loads(w1s, w1_scales[:, 0], eng=nc.gpsimd), 0)
         make_identity(nc, ident[:])
-        weave([], quadrant_loads(w3ts, w3t_scales[:, 0], eng=nc.gpsimd) + quadrant_loads(w2s[1], w2_planes[4:8], eng=nc.gpsimd), 0)
+        weave([], quadrant_loads(w2s[1], w2_planes[4:8], eng=nc.gpsimd), 0)
 
         w1_0, w3_0, w2_0 = first_loads(0)
         nc.sync.dma_start(offsets[:], offs)
         load_words(xw, x_words)
+        w1_1, w3_1, w2_1 = first_loads(1)
         weave([], quadrant_loads(xs, x_scales), 0)
         nc.sync.dma_start(dyw[:], words(dy_words))
-        weave([w1_0, w2_0], quadrant_loads(dys, dy_scales) + quadrant_loads(w2s[0], w2_planes[0:4]), 4)
-        weave([w3_0], quadrant_loads(w3s, w3_scales[:, 0], [2, 3]), 4)
+        weave([w1_0], quadrant_loads(dys, dy_scales), 4)
+        w3_0()
+        weave([w1_1, w2_0], quadrant_loads(w3s, w3_scales[:, 0]) + quadrant_loads(w2s[0], w2_planes[0:4]), 4)
         with nc.allow_non_contiguous_dma(reason="one gate value a partition"):
             nc.sync.dma_start(
                 gcol[:], gate.rearrange("r c -> (r c)")[0 : E * (T + C)].rearrange("(e x) -> x e", x=T + C)[0:P, :])
-        weave(first_loads(1), quadrant_loads(w1ts, w1t_scales[:, 0]), 2)
-        weave(back_loads(0) + first_loads(2) + back_loads(1) + first_loads(3) + back_loads(2) + back_loads(3), [], 0)
+        back_scales = quadrant_loads(w3ts, w3t_scales[:, 0]) + quadrant_loads(w1ts, w1t_scales[:, 0])
+        weave([], back_scales[:4], 0)
+        weave([w3_1], back_scales[4:], 8)
+        weave([w2_1] + back_loads(0) + first_loads(2) + back_loads(1) + first_loads(3) + back_loads(2) + back_loads(3), [], 0)
 
         def slots(e):
             return slice(e * C, (e + 1) * C)
@@ -119,42 +122,65 @@ def tile_moe_rec_glu_sigmoid_kernel(
             nc.vector.tensor_copy(xsg[:, slots(e)], xs[:].indirect(listed(e)))
 
         def gather_dy(e):
+            late = e == E - 1
+            picked = [keep.tile([P, C], U32, name="dyg%d_%d" % (e, s), tag=("u0", "sig0")[s] if late else "dyg%d_%d" % (e, s), align_bytes=64) for s in range(2)]
+            picked.append(keep.tile([P, C], U8, name="dysg%d" % e, tag="dysg0" if late else "dysg%d" % e, align_bytes=64))
             for s in range(2):
-                nc.vector.tensor_copy(dyg[s][:, slots(e % 2)], dyw[:, s, :].bitcast(U32).indirect(listed(e)))
-            nc.vector.tensor_copy(dysg[:, slots(e % 2)], dys[:].indirect(listed(e)))
-
-        def by_byte(sums):
-            return sums[:].rearrange("p (m d) -> p d m", d=4)
+                nc.vector.tensor_copy(picked[s][:], dyw[:, s, :].bitcast(U32).indirect(listed(e)))
+            nc.vector.tensor_copy(picked[2][:], dys[:].indirect(listed(e)))
+            dyg[e] = picked
 
         def first(e):
             cols = slots(e)
-            for acc, w, ws in ((a1_bank, w1, w1s), (a3_bank[e % 2], w3, w3s)):
+            for acc, w, ws in ((a1_bank[e % 2], w1, w1s), (a3_bank[e % 2], w3, w3s)):
                 nc.tensor.matmul_mx(acc[:], lhsT=xg[:, cols].bitcast(X4), lhsT_scale=xsg[:, cols],
                                     rhs=w[e][:].bitcast(X4), rhs_scale=ws[4 * e : P, :], start=True, stop=True)
             for s in range(2):
-                nc.tensor.matmul_mx(dh_bank[e % 2][:], lhsT=dyg[s][:, slots(e % 2)].bitcast(X4), lhsT_scale=dysg[4 * s : P, slots(e % 2)],
+                nc.tensor.matmul_mx(dh_bank[e % 2][:], lhsT=dyg[e][s][:].bitcast(X4), lhsT_scale=dyg[e][2][4 * s : P, :],
                                     rhs=w2[e][:, s, :].bitcast(X4), rhs_scale=w2s[e // 2][4 * (2 * (e % 2) + s) : P, :],
                                     start=(s == 0), stop=(s == 1))
 
+        def by_pair(sums):
+            return sums[:].rearrange("p (m r t) -> p r m t", r=2, t=2)
+
+        def flat(tile):
+            return tile[:].rearrange("p r m t -> p (r m t)")
+
+        def slope(e):
+            a3 = a3_bank[e % 2]
+            sig = keep.tile([P, 2, C, 2], F32, name="sig%d" % e, align_bytes=64)
+            u = keep.tile([P, 2, C, 2], F32, name="u%d" % e, align_bytes=64)
+            nc.scalar.activation(sig[:], by_pair(a1_bank[e % 2]), ACT.Sigmoid)
+            if e < ON_VECTOR:
+                for r in range(2):
+                    nc.vector.scalar_tensor_tensor(u[:, r], sig[:, r], 1.0, by_pair(a3)[:, r], SUB, MULT)
+            else:
+                a3c = keep.tile([P, 2, C, 2], F32, name="a3c%d" % e, align_bytes=64)
+                nc.scalar.copy(a3c[:], by_pair(a3))
+                less = keep.tile([P, H], F32, name="less%d" % e, align_bytes=64)
+                nc.gpsimd.tensor_scalar(less[:], flat(sig), 1.0, -1.0, MULT, ADD)
+                nc.gpsimd.tensor_tensor(flat(u), flat(a3c), less[:], MULT)
+            factors[e] = (sig, u)
+
         def products(e):
-            a1, a3, dh = a1_bank, a3_bank[e % 2], dh_bank[e % 2]
-            sig = keep.tile([P, 4, C], F32, name="sig%d" % e, tag="after_sig%d" % e)
-            da3 = work.tile([P, 4, C], F32, name="da3")
-            u = keep.tile([P, 4, C], F32, name="u%d" % e, tag="before_u%d" % e)
-            nda1 = work.tile([P, 4, C], F32, name="nda1")
-            nc.scalar.activation(sig[:], by_byte(a1), ACT.Sigmoid)
-            nc.vector.scalar_tensor_tensor(u[:], sig[:], 1.0, by_byte(a3), SUB, MULT)
-            nc.vector.scalar_tensor_tensor(da3[:], by_byte(dh), gcol[:, e : e + 1], sig[:], MULT, MULT)
-            (nc.vector if e < ON_VECTOR else nc.gpsimd).tensor_tensor(nda1[:], da3[:], u[:], MULT)
-            made[e] = (da3, nda1)
+            sig, u = factors[e]
+            da3 = keep.tile([P, 2, C, 2], F32, name="da3_%d" % e, align_bytes=64)
+            da1 = keep.tile([P, 2, C, 2], BF16, name="da1_%d" % e, align_bytes=64)
+            for r in range(2):
+                nc.vector.scalar_tensor_tensor(da3[:, r], by_pair(dh_bank[e % 2])[:, r], gcol[:, e : e + 1], sig[:, r], MULT, MULT)
+            nc.vector.scalar_tensor_tensor(flat(da1), flat(da3), -1.0, flat(u), MULT, MULT)
+            made[e] = (da3, da1)
 
         def turn(e):
-            da3, nda1 = made[e]
+            da3, da1 = made[e]
             dab = work.tile([P, 2, C, 4], BF16, name="dab", align_bytes=64)
-            for j, (src, turned, sign) in enumerate(((da3, t3_bank, 1.0), (nda1, t1_bank, -1.0))):
-                for d in range(4):
-                    nc.tensor.transpose(turned[:, d * C : (d + 1) * C], src[:, d, :], ident[:])
-                nc.scalar.activation(dab[:, j, :, :], turned[:].rearrange("p (d c) -> p c d", d=4), ACT.Copy, scale=sign)
+            for d in range(4):
+                nc.tensor.transpose(dx_bank[:, d * C : (d + 1) * C], da3[:, d // 2, :, d % 2], ident[:])
+            nc.scalar.copy(dab[:, 0], dx_bank[:].rearrange("p (d c) -> p c d", d=4))
+            pairs = da1[:].rearrange("p r m t -> p r (m t)").bitcast(F32)
+            for r in range(2):
+                nc.tensor.transpose(t1_bank[:, r * C : (r + 1) * C], pairs[:, r, :], ident[:])
+            nc.scalar.copy(dab[:, 1].bitcast(F32), t1_bank[:, 0 : 2 * C].rearrange("p (r c) -> p c r", r=2))
             daw = work.tile([P, 2 * C], U32, name="daw", align_bytes=64)
             das = work.tile([P, 2 * C], U8, name="das", align_bytes=64)
             nc.vector.quantize_mx(daw[:].bitcast(X4), das[:], dab[:].rearrange("p j c d -> p (j c d)"))
@@ -173,32 +199,32 @@ def tile_moe_rec_glu_sigmoid_kernel(
                                         rhs=daw[:, dc].bitcast(X4), rhs_scale=das[:, dc], start=(j == 0), stop=(j == 1))
             for h in range(2):
                 kt = 2 * half + h
-                tag = ("after_sig%d" % (e + 1), "before_u%d" % (e + 2), "after_sig%d" % (e + 2), "last%d" % e)[kt]
-                if kt == 0 and e == 0:
-                    tag = "first"
-                dx = keep.tile([P, C], F32, name="dx%d_%d" % (e, kt), tag=tag)
+                dx = keep.tile([P, C], F32, name="dx%d_%d" % (e, kt), align_bytes=64)
                 nc.scalar.copy(dx[:], acc[:, h * C : (h + 1) * C])
                 nc.vector.tensor_copy(win[kt][:].indirect(listed(e)), dx[:])
                 if e == E - 1:
                     nc.sync.dma_start(out[kt * P : (kt + 1) * P, :], win[kt][:])
 
-        made, packed = {}, {}
+        dyg, factors, made, packed = {}, {}, {}, {}
         for e in range(E):
             gather_x(e)
-        gather_dy(0)
-        gather_dy(1)
+        for e in range(E - 1):
+            gather_dy(e)
         first(0)
-        gather_dy(2)
+        slope(0)
         products(0)
-        first(1)
-        products(1)
-        gather_dy(3)
+        gather_dy(E - 1)
         turn(0)
+        first(1)
+        slope(1)
+        products(1)
         for e in range(E):
             back(e, 0)
             if e + 1 < E:
                 turn(e + 1)
             if e + 2 < E:
                 first(e + 2)
-                products(e + 2)
+                slope(e + 2)
             back(e, 1)
+            if e + 2 < E:
+                products(e + 2)

@@ -46,8 +46,10 @@ def tile_moe_rec_glu_sigmoid_kernel(
         w3ts = keep.tile([P, K], U8, name="w3ts", align_bytes=64)
         gcol = keep.tile([P, E], F32, name="gcol")
         ident = keep.tile([P, P], F32, name="ident", align_bytes=64)
-        w1 = [keep.tile([P, H], I32, name="w1_%d" % e, align_bytes=64) for e in range(E)]
-        w3 = [keep.tile([P, H], I32, name="w3_%d" % e, align_bytes=64) for e in range(E)]
+        w1_pair = keep.tile([P, 2, H], I32, name="w1_pair", align_bytes=64)
+        w1 = [w1_pair[:, 0, :], w1_pair[:, 1, :]] + [keep.tile([P, H], I32, name="w1_%d" % e, align_bytes=64) for e in range(2, E)]
+        w3_pair = keep.tile([P, 2, H], I32, name="w3_pair", align_bytes=64)
+        w3 = [w3_pair[:, 0, :], w3_pair[:, 1, :]] + [keep.tile([P, H], I32, name="w3_%d" % e, align_bytes=64) for e in range(2, E)]
         w2 = [keep.tile([P, 2, H], I32, name="w2_%d" % e, align_bytes=64) for e in range(E)]
         w1t = [keep.tile([P, K], I32, name="w1t_%d" % e, align_bytes=64) for e in range(E)]
         w3t = [keep.tile([P, K], I32, name="w3t_%d" % e, align_bytes=64) for e in range(E)]
@@ -88,28 +90,29 @@ def tile_moe_rec_glu_sigmoid_kernel(
 
         w2_planes = w2t_scales.rearrange("e s b n -> (e s) b n")
         nc.gpsimd.memset(w1s[:].bitcast(I32), 0)
-        for plane in (xs, dys, w3s, w2s[0], w1ts, w3ts, w2s[1]):
+        for plane in (xs, dys, w3s, w2s[0], w3ts, w1ts, w2s[1]):
             nc.vector.memset(plane[:].bitcast(I32), 0)
+        later_scales = [(w3ts, w3t_scales[:, 0], q) for q in range(4)] + [(w2s[1], w2_planes[4:8], q) for q in range(4)] + [(w1ts, w1t_scales[:, 0], q) for q in range(4)]
         weave([], quadrant_loads(w1s, w1_scales[:, 0], eng=nc.gpsimd), 0)
         make_identity(nc, ident[:])
-        weave([], quadrant_loads(w2s[1], w2_planes[4:8], eng=nc.gpsimd), 0)
-
-        w1_0, w3_0, w2_0 = first_loads(0)
+        for plane in later_scales[:6]:
+            load_quadrant(nc.gpsimd, *plane)
         nc.sync.dma_start(offsets[:], offs)
         load_words(xw, x_words)
-        w1_1, w3_1, w2_1 = first_loads(1)
         weave([], quadrant_loads(xs, x_scales), 0)
         nc.sync.dma_start(dyw[:], words(dy_words))
-        weave([w1_0], quadrant_loads(dys, dy_scales), 4)
-        w3_0()
-        weave([w1_1, w2_0], quadrant_loads(w3s, w3_scales[:, 0]) + quadrant_loads(w2s[0], w2_planes[0:4]), 4)
+        nc.sync.dma_start(w1_pair[:], words(w1_words[0:2, 0]))
+        weave([], quadrant_loads(dys, dy_scales), 0)
+        nc.sync.dma_start(w3_pair[:], words(w3_words[0:2, 0]))
+        weave([], quadrant_loads(w3s, w3_scales[:, 0]), 0)
+        weave(first_loads(0)[2:], quadrant_loads(w2s[0], w2_planes[0:4]), 4)
         with nc.allow_non_contiguous_dma(reason="one gate value a partition"):
             nc.sync.dma_start(
                 gcol[:], gate.rearrange("r c -> (r c)")[0 : E * (T + C)].rearrange("(e x) -> x e", x=T + C)[0:P, :])
-        back_scales = quadrant_loads(w3ts, w3t_scales[:, 0]) + quadrant_loads(w1ts, w1t_scales[:, 0])
-        weave([], back_scales[:4], 0)
-        weave([w3_1], back_scales[4:], 8)
-        weave([w2_1] + back_loads(0) + first_loads(2) + back_loads(1) + first_loads(3) + back_loads(2) + back_loads(3), [], 0)
+        for plane in later_scales[6:]:
+            load_quadrant(nc.sync, *plane)
+        weave(first_loads(1)[2:] + back_loads(0), [], 0)
+        weave(first_loads(2) + back_loads(1) + first_loads(3) + back_loads(2) + back_loads(3), [], 0)
 
         def slots(e):
             return slice(e * C, (e + 1) * C)

@@ -19,7 +19,11 @@ ADD = mybir.AluOpType.add
 SUB = mybir.AluOpType.subtract
 
 P = 128
-ON_VECTOR = 2
+PASSES = N // 512
+ROW_TILES = K // P
+LAST = E - 1
+EARLY = 2
+LATER_ON_GPSIMD = 6
 
 
 def tile_moe_rec_glu_sigmoid_kernel(
@@ -29,90 +33,89 @@ def tile_moe_rec_glu_sigmoid_kernel(
     nc = tc.nc
     with ExitStack() as ctx:
         keep = ctx.enter_context(tc.tile_pool(name="keep", bufs=1))
-        work = ctx.enter_context(tc.tile_pool(name="work", bufs=4))
+        work = ctx.enter_context(tc.tile_pool(name="work", bufs=E))
         psum = ctx.enter_context(tc.psum_pool(name="psum", bufs=1))
         bank = [psum.tile([P, H], F32, name="bank%d" % b) for b in range(8)]
-        a1_bank, a3_bank, dh_bank, t1_bank, dx_bank = bank[0:2], bank[2:4], bank[4:6], bank[6], bank[7]
+        a1_bank, a3_bank, dh_bank, upper_bank, lower_bank = bank[0:2], bank[2:4], bank[4:6], bank[6], bank[7]
+
+        def tile(shape, dtype, name, after=None):
+            return keep.tile(shape, dtype, name=name, tag=after or name, align_bytes=64)
 
         offsets = keep.tile([P, T // 16], U16, name="offsets")
-        xw = keep.tile([P, T], I32, name="xw", align_bytes=64)
-        dyw = keep.tile([P, 2, T], I32, name="dyw", align_bytes=64)
-        xs = keep.tile([P, T], U8, name="xs", align_bytes=64)
-        dys = keep.tile([P, T], U8, name="dys", align_bytes=64)
-        w1s = keep.tile([P, H], U8, name="w1s", align_bytes=64)
-        w3s = keep.tile([P, H], U8, name="w3s", align_bytes=64)
-        w2s = [keep.tile([P, H], U8, name="w2s%d" % j, align_bytes=64) for j in range(2)]
-        w1ts = keep.tile([P, K], U8, name="w1ts", align_bytes=64)
-        w3ts = keep.tile([P, K], U8, name="w3ts", align_bytes=64)
+        xw = tile([P, T], I32, "xw")
+        dyw = tile([P, PASSES, T], I32, "dyw")
+        xs = tile([P, T], U8, "xs")
+        dys = tile([P, T], U8, "dys")
+        w1s = tile([P, H], U8, "w1s")
+        w3s = tile([P, H], U8, "w3s")
+        w2s = [tile([P, H], U8, "w2s%d" % j) for j in range(E * PASSES // 4)]
+        w1ts = tile([P, K], U8, "w1ts")
+        w3ts = tile([P, K], U8, "w3ts")
         gcol = keep.tile([P, E], F32, name="gcol")
-        ident = keep.tile([P, P], F32, name="ident", align_bytes=64)
-        w1_pair = keep.tile([P, 2, H], I32, name="w1_pair", align_bytes=64)
-        w1 = [w1_pair[:, 0, :], w1_pair[:, 1, :]] + [keep.tile([P, H], I32, name="w1_%d" % e, align_bytes=64) for e in range(2, E)]
-        w3_pair = keep.tile([P, 2, H], I32, name="w3_pair", align_bytes=64)
-        w3 = [w3_pair[:, 0, :], w3_pair[:, 1, :]] + [keep.tile([P, H], I32, name="w3_%d" % e, align_bytes=64) for e in range(2, E)]
-        w2 = [keep.tile([P, 2, H], I32, name="w2_%d" % e, align_bytes=64) for e in range(E)]
-        w1t = [keep.tile([P, K], I32, name="w1t_%d" % e, align_bytes=64) for e in range(E)]
-        w3t = [keep.tile([P, K], I32, name="w3t_%d" % e, align_bytes=64) for e in range(E)]
-        xg = keep.tile([P, E * C], U32, name="xg", align_bytes=64)
-        xsg = keep.tile([P, E * C], U8, name="xsg", align_bytes=64)
-        win = [keep.tile([P, T], F32, name="win%d" % j, align_bytes=64) for j in range(4)]
+        ident = tile([P, P], F32, "ident")
+        w1_early = tile([P, EARLY, H], I32, "w1_early")
+        w1 = [w1_early[:, e, :] for e in range(EARLY)] + [tile([P, H], I32, "w1_%d" % e) for e in range(EARLY, E)]
+        w3_early = tile([P, EARLY, H], I32, "w3_early")
+        w3 = [w3_early[:, e, :] for e in range(EARLY)] + [tile([P, H], I32, "w3_%d" % e) for e in range(EARLY, E)]
+        w2 = [tile([P, PASSES, H], I32, "w2_%d" % e) for e in range(E)]
+        w1t = [tile([P, K], I32, "w1t_%d" % e) for e in range(E)]
+        w3t = [tile([P, K], I32, "w3t_%d" % e) for e in range(E)]
+        xg = tile([P, E * C], U32, "xg")
+        xsg = tile([P, E * C], U8, "xsg")
+        rows = [tile([P, T], F32, "rows%d" % kt) for kt in range(ROW_TILES)]
 
-        def words(src):
-            return src.rearrange("s p n d -> p s (n d)").bitcast(I32)
+        def load_pass(dst, src):
+            nc.sync.dma_start(dst[:], src.rearrange("p n d -> p (n d)").bitcast(I32))
 
-        def load_words(dst, src):
-            nc.sync.dma_start(dst[:], src[0].rearrange("p n d -> p (n d)").bitcast(I32))
+        def load_passes(dst, src):
+            nc.sync.dma_start(dst[:], src.rearrange("s p n d -> p s (n d)").bitcast(I32))
 
         def load_quadrant(eng, dst, planes, q):
             count = planes.shape[0]
             eng.dma_start(dst[32 * q : 32 * q + 4 * count, :].bitcast(I32), planes[:, 4 * q : 4 * q + 4, :].bitcast(I32))
 
-        def first_loads(e):
-            return [
-                lambda: load_words(w1[e], w1_words[e]),
-                lambda: load_words(w3[e], w3_words[e]),
-                lambda: nc.sync.dma_start(w2[e][:], words(w2t_words[e])),
-            ]
+        def load_planes(eng, dst, planes):
+            for q in range(4):
+                load_quadrant(eng, dst, planes, q)
 
-        def back_loads(e):
-            return [lambda: load_words(w3t[e], w3t_words[e]), lambda: load_words(w1t[e], w1t_words[e])]
+        def load_back(e):
+            load_pass(w3t[e], w3t_words[e, 0])
+            load_pass(w1t[e], w1t_words[e, 0])
 
-        def quadrant_loads(dst, planes, quadrants=range(4), eng=nc.sync):
-            return [lambda q=q: load_quadrant(eng, dst, planes, q) for q in quadrants]
-
-        def weave(large, small, each):
-            for j, load in enumerate(large):
-                load()
-                for little in small[j * each : (j + 1) * each]:
-                    little()
-            for little in small[len(large) * each :]:
-                little()
+        nc.gpsimd.memset(w1s[:].bitcast(I32), 0)
+        for planes in (xs, dys, w3s, w2s[0], w3ts, w1ts, w2s[1]):
+            nc.vector.memset(planes[:].bitcast(I32), 0)
 
         w2_planes = w2t_scales.rearrange("e s b n -> (e s) b n")
-        nc.gpsimd.memset(w1s[:].bitcast(I32), 0)
-        for plane in (xs, dys, w3s, w2s[0], w3ts, w1ts, w2s[1]):
-            nc.vector.memset(plane[:].bitcast(I32), 0)
-        later_scales = [(w3ts, w3t_scales[:, 0], q) for q in range(4)] + [(w2s[1], w2_planes[4:8], q) for q in range(4)] + [(w1ts, w1t_scales[:, 0], q) for q in range(4)]
-        weave([], quadrant_loads(w1s, w1_scales[:, 0], eng=nc.gpsimd), 0)
+        later = [(dst, planes, q)
+                 for dst, planes in ((w3ts, w3t_scales[:, 0]), (w2s[1], w2_planes[4:8]), (w1ts, w1t_scales[:, 0]))
+                 for q in range(4)]
+        load_planes(nc.gpsimd, w1s, w1_scales[:, 0])
         make_identity(nc, ident[:])
-        for plane in later_scales[:6]:
-            load_quadrant(nc.gpsimd, *plane)
+        for dst, planes, q in later[:LATER_ON_GPSIMD]:
+            load_quadrant(nc.gpsimd, dst, planes, q)
         nc.sync.dma_start(offsets[:], offs)
-        load_words(xw, x_words)
-        weave([], quadrant_loads(xs, x_scales), 0)
-        nc.sync.dma_start(dyw[:], words(dy_words))
-        nc.sync.dma_start(w1_pair[:], words(w1_words[0:2, 0]))
-        weave([], quadrant_loads(dys, dy_scales), 0)
-        nc.sync.dma_start(w3_pair[:], words(w3_words[0:2, 0]))
-        weave([], quadrant_loads(w3s, w3_scales[:, 0]), 0)
-        weave(first_loads(0)[2:], quadrant_loads(w2s[0], w2_planes[0:4]), 4)
+        load_pass(xw, x_words[0])
+        load_planes(nc.sync, xs, x_scales)
+        load_passes(dyw, dy_words)
+        load_passes(w1_early, w1_words[0:EARLY, 0])
+        load_planes(nc.sync, dys, dy_scales)
+        load_passes(w3_early, w3_words[0:EARLY, 0])
+        load_planes(nc.sync, w3s, w3_scales[:, 0])
+        load_passes(w2[0], w2t_words[0])
+        load_planes(nc.sync, w2s[0], w2_planes[0:4])
         with nc.allow_non_contiguous_dma(reason="one gate value a partition"):
             nc.sync.dma_start(
                 gcol[:], gate.rearrange("r c -> (r c)")[0 : E * (T + C)].rearrange("(e x) -> x e", x=T + C)[0:P, :])
-        for plane in later_scales[6:]:
-            load_quadrant(nc.sync, *plane)
-        weave(first_loads(1)[2:] + back_loads(0), [], 0)
-        weave(first_loads(2) + back_loads(1) + first_loads(3) + back_loads(2) + back_loads(3), [], 0)
+        for dst, planes, q in later[LATER_ON_GPSIMD:]:
+            load_quadrant(nc.sync, dst, planes, q)
+        for e in range(1, E):
+            if e >= EARLY:
+                load_pass(w1[e], w1_words[e, 0])
+                load_pass(w3[e], w3_words[e, 0])
+            load_passes(w2[e], w2t_words[e])
+            load_back(e - 1)
+        load_back(LAST)
 
         def slots(e):
             return slice(e * C, (e + 1) * C)
@@ -124,99 +127,105 @@ def tile_moe_rec_glu_sigmoid_kernel(
             nc.vector.tensor_copy(xg[:, slots(e)], xw[:].bitcast(U32).indirect(listed(e)))
             nc.vector.tensor_copy(xsg[:, slots(e)], xs[:].indirect(listed(e)))
 
-        def gather_dy(e):
-            late = e == E - 1
-            picked = [keep.tile([P, C], U32, name="dyg%d_%d" % (e, s), tag=("u0", "sig0")[s] if late else "dyg%d_%d" % (e, s), align_bytes=64) for s in range(2)]
-            picked.append(keep.tile([P, C], U8, name="dysg%d" % e, tag="dysg0" if late else "dysg%d" % e, align_bytes=64))
-            for s in range(2):
+        def gather_dy(e, after=(None, None, None)):
+            picked = [tile([P, C], U32, "dyg%d_%d" % (e, s), after[s]) for s in range(PASSES)]
+            picked_scales = tile([P, C], U8, "dysg%d" % e, after[PASSES])
+            for s in range(PASSES):
                 nc.vector.tensor_copy(picked[s][:], dyw[:, s, :].bitcast(U32).indirect(listed(e)))
-            nc.vector.tensor_copy(picked[2][:], dys[:].indirect(listed(e)))
-            dyg[e] = picked
+            nc.vector.tensor_copy(picked_scales[:], dys[:].indirect(listed(e)))
+            gathered[e] = (picked, picked_scales)
 
         def first(e):
             cols = slots(e)
             for acc, w, ws in ((a1_bank[e % 2], w1, w1s), (a3_bank[e % 2], w3, w3s)):
                 nc.tensor.matmul_mx(acc[:], lhsT=xg[:, cols].bitcast(X4), lhsT_scale=xsg[:, cols],
                                     rhs=w[e][:].bitcast(X4), rhs_scale=ws[4 * e : P, :], start=True, stop=True)
-            for s in range(2):
-                nc.tensor.matmul_mx(dh_bank[e % 2][:], lhsT=dyg[e][s][:].bitcast(X4), lhsT_scale=dyg[e][2][4 * s : P, :],
-                                    rhs=w2[e][:, s, :].bitcast(X4), rhs_scale=w2s[e // 2][4 * (2 * (e % 2) + s) : P, :],
-                                    start=(s == 0), stop=(s == 1))
+            picked, picked_scales = gathered[e]
+            for s in range(PASSES):
+                plane = PASSES * e + s
+                nc.tensor.matmul_mx(dh_bank[e % 2][:], lhsT=picked[s][:].bitcast(X4), lhsT_scale=picked_scales[4 * s : P, :],
+                                    rhs=w2[e][:, s, :].bitcast(X4), rhs_scale=w2s[plane // 4][4 * (plane % 4) : P, :],
+                                    start=(s == 0), stop=(s == PASSES - 1))
 
         def by_pair(sums):
             return sums[:].rearrange("p (m r t) -> p r m t", r=2, t=2)
 
-        def flat(tile):
-            return tile[:].rearrange("p r m t -> p (r m t)")
+        def flat(values):
+            return values[:].rearrange("p r m t -> p (r m t)")
 
         def slope(e):
             a3 = a3_bank[e % 2]
-            sig = keep.tile([P, 2, C, 2], F32, name="sig%d" % e, align_bytes=64)
-            u = keep.tile([P, 2, C, 2], F32, name="u%d" % e, align_bytes=64)
+            sig = tile([P, 2, C, 2], F32, "sig%d" % e)
+            u = tile([P, 2, C, 2], F32, "u%d" % e)
             nc.scalar.activation(sig[:], by_pair(a1_bank[e % 2]), ACT.Sigmoid)
-            if e < ON_VECTOR:
+            if e < EARLY:
                 for r in range(2):
                     nc.vector.scalar_tensor_tensor(u[:, r], sig[:, r], 1.0, by_pair(a3)[:, r], SUB, MULT)
             else:
-                a3c = keep.tile([P, 2, C, 2], F32, name="a3c%d" % e, align_bytes=64)
-                nc.scalar.copy(a3c[:], by_pair(a3))
-                less = keep.tile([P, H], F32, name="less%d" % e, align_bytes=64)
-                nc.gpsimd.tensor_scalar(less[:], flat(sig), 1.0, -1.0, MULT, ADD)
-                nc.gpsimd.tensor_tensor(flat(u), flat(a3c), less[:], MULT)
+                a3_copy = tile([P, 2, C, 2], F32, "a3_copy%d" % e)
+                nc.scalar.copy(a3_copy[:], by_pair(a3))
+                rest = tile([P, H], F32, "rest%d" % e)
+                nc.gpsimd.tensor_scalar(rest[:], flat(sig), -1.0, 1.0, MULT, ADD)
+                nc.gpsimd.tensor_tensor(flat(u), flat(a3_copy), rest[:], MULT)
             factors[e] = (sig, u)
 
         def products(e):
             sig, u = factors[e]
-            da3 = keep.tile([P, 2, C, 2], F32, name="da3_%d" % e, align_bytes=64)
-            da1 = keep.tile([P, 2, C, 2], BF16, name="da1_%d" % e, align_bytes=64)
+            da3 = tile([P, 2, C, 2], F32, "da3_%d" % e)
+            da1 = tile([P, 2, C, 2], BF16, "da1_%d" % e)
             for r in range(2):
-                nc.vector.scalar_tensor_tensor(da3[:, r], by_pair(dh_bank[e % 2])[:, r], gcol[:, e : e + 1], sig[:, r], MULT, MULT)
-            nc.vector.scalar_tensor_tensor(flat(da1), flat(da3), -1.0, flat(u), MULT, MULT)
+                nc.vector.scalar_tensor_tensor(
+                    da3[:, r], by_pair(dh_bank[e % 2])[:, r], gcol[:, e : e + 1], sig[:, r], MULT, MULT)
+            if e < EARLY:
+                nc.vector.scalar_tensor_tensor(flat(da1), flat(da3), -1.0, flat(u), MULT, MULT)
+            else:
+                (nc.gpsimd if e == LAST else nc.vector).tensor_tensor(flat(da1), flat(da3), flat(u), MULT)
             made[e] = (da3, da1)
 
         def turn(e):
             da3, da1 = made[e]
-            dab = work.tile([P, 2, C, 4], BF16, name="dab", align_bytes=64)
+            da3_bank = a1_bank[e % 2] if e == LAST else lower_bank
+            rounded = work.tile([P, 2, C, 4], BF16, name="rounded", align_bytes=64)
             for d in range(4):
-                nc.tensor.transpose(dx_bank[:, d * C : (d + 1) * C], da3[:, d // 2, :, d % 2], ident[:])
-            nc.scalar.copy(dab[:, 0], dx_bank[:].rearrange("p (d c) -> p c d", d=4))
+                nc.tensor.transpose(da3_bank[:, d * C : (d + 1) * C], da3[:, d // 2, :, d % 2], ident[:])
+            nc.scalar.copy(rounded[:, 0], da3_bank[:].rearrange("p (d c) -> p c d", d=4))
             pairs = da1[:].rearrange("p r m t -> p r (m t)").bitcast(F32)
             for r in range(2):
-                nc.tensor.transpose(t1_bank[:, r * C : (r + 1) * C], pairs[:, r, :], ident[:])
-            nc.scalar.copy(dab[:, 1].bitcast(F32), t1_bank[:, 0 : 2 * C].rearrange("p (r c) -> p c r", r=2))
-            daw = work.tile([P, 2 * C], U32, name="daw", align_bytes=64)
-            das = work.tile([P, 2 * C], U8, name="das", align_bytes=64)
-            nc.vector.quantize_mx(daw[:].bitcast(X4), das[:], dab[:].rearrange("p j c d -> p (j c d)"))
-            packed[e] = (daw, das)
+                nc.tensor.transpose(upper_bank[:, r * C : (r + 1) * C], pairs[:, r, :], ident[:])
+            nc.scalar.copy(rounded[:, 1].bitcast(F32), upper_bank[:, 0 : 2 * C].rearrange("p (r c) -> p c r", r=2))
+            da_words = work.tile([P, 2 * C], U32, name="da_words", align_bytes=64)
+            da_scales = work.tile([P, 2 * C], U8, name="da_scales", align_bytes=64)
+            nc.vector.quantize_mx(da_words[:].bitcast(X4), da_scales[:], rounded[:].rearrange("p j c d -> p (j c d)"))
+            packed[e] = (da_words, da_scales)
 
         def back(e, half):
-            daw, das = packed[e]
-            acc = t1_bank if half else dx_bank
+            da_words, da_scales = packed[e]
+            acc = upper_bank if half else lower_bank
             for h in range(2):
                 kt = 2 * half + h
                 kc = slice(kt * P, (kt + 1) * P)
                 for j, (w, ws) in enumerate(((w3t, w3ts), (w1t, w1ts))):
                     dc = slice(j * C, (j + 1) * C)
                     nc.tensor.matmul_mx(acc[:, h * C : (h + 1) * C], lhsT=w[e][:, kc].bitcast(X4),
-                                        lhsT_scale=ws[4 * e : P, kc],
-                                        rhs=daw[:, dc].bitcast(X4), rhs_scale=das[:, dc], start=(j == 0), stop=(j == 1))
+                                        lhsT_scale=ws[4 * e : P, kc], rhs=da_words[:, dc].bitcast(X4),
+                                        rhs_scale=da_scales[:, dc], start=(j == 0), stop=(j == 1))
             for h in range(2):
                 kt = 2 * half + h
-                dx = keep.tile([P, C], F32, name="dx%d_%d" % (e, kt), align_bytes=64)
+                dx = tile([P, C], F32, "dx%d_%d" % (e, kt))
                 nc.scalar.copy(dx[:], acc[:, h * C : (h + 1) * C])
-                nc.vector.tensor_copy(win[kt][:].indirect(listed(e)), dx[:])
-                if e == E - 1:
-                    nc.sync.dma_start(out[kt * P : (kt + 1) * P, :], win[kt][:])
+                nc.vector.tensor_copy(rows[kt][:].indirect(listed(e)), dx[:])
+                if e == LAST:
+                    nc.sync.dma_start(out[kt * P : (kt + 1) * P, :], rows[kt][:])
 
-        dyg, factors, made, packed = {}, {}, {}, {}
+        gathered, factors, made, packed = {}, {}, {}, {}
         for e in range(E):
             gather_x(e)
-        for e in range(E - 1):
+        for e in range(LAST):
             gather_dy(e)
         first(0)
         slope(0)
         products(0)
-        gather_dy(E - 1)
+        gather_dy(LAST, after=("u0", "sig0", "dysg0"))
         turn(0)
         first(1)
         slope(1)

@@ -22,6 +22,16 @@ P = 128
 PASSES = N // 512
 ROW_TILES = K // P
 LAST = E - 1
+U_G = (2, 3)
+U_AFTER = {2: "rounded1"}
+DA3_AFTER = ("da3_0", "rounded0", "da3_2", "da3_3")
+DA1_G = (2, 3)
+DA1_AFTER = {}
+DX_AFTER = {}
+T3_BANK = (6, 6, 6, 6)
+U_POS = ()
+BEFORE = (3, 3, 2, 4)
+PAIR = 2
 EARLY = 2
 LATER_ON_GPSIMD = 6
 
@@ -36,7 +46,9 @@ def tile_moe_rec_glu_sigmoid_kernel(
         work = ctx.enter_context(tc.tile_pool(name="work", bufs=E))
         psum = ctx.enter_context(tc.psum_pool(name="psum", bufs=1))
         bank = [psum.tile([P, H], F32, name="bank%d" % b) for b in range(8)]
-        a1_bank, a3_bank, dh_bank, upper_bank, lower_bank = bank[0:2], bank[2:4], bank[4:6], bank[6], bank[7]
+        a1_bank, a3_bank, dh_bank, spare_bank, da1_bank, dx_bank = bank[0], bank[1], bank[2:4], bank[4], bank[5], bank[6:8]
+        da3_bank = dx_bank[0]
+        dx_at = (da3_bank[:, 0:C], da1_bank[:, 0:C], da1_bank[:, 2 * C : 3 * C], da1_bank[:, 3 * C : 4 * C])
 
         def tile(shape, dtype, name, after=None):
             return keep.tile(shape, dtype, name=name, tag=after or name, align_bytes=64)
@@ -79,21 +91,22 @@ def tile_moe_rec_glu_sigmoid_kernel(
                 load_quadrant(eng, dst, planes, q)
 
         def load_back(e):
-            load_pass(w3t[e], w3t_words[e, 0])
             load_pass(w1t[e], w1t_words[e, 0])
+            load_pass(w3t[e], w3t_words[e, 0])
 
         nc.gpsimd.memset(w1s[:].bitcast(I32), 0)
         for planes in (xs, dys, w3s, w2s[0], w3ts, w1ts, w2s[1]):
             nc.vector.memset(planes[:].bitcast(I32), 0)
 
         w2_planes = w2t_scales.rearrange("e s b n -> (e s) b n")
-        later = [(dst, planes, q)
-                 for dst, planes in ((w3ts, w3t_scales[:, 0]), (w2s[1], w2_planes[4:8]), (w1ts, w1t_scales[:, 0]))
-                 for q in range(4)]
+        def load_gate(eng):
+            with nc.allow_non_contiguous_dma(reason="one gate value a partition"):
+                eng.dma_start(
+                    gcol[:], gate.rearrange("r c -> (r c)")[0 : E * (T + C)].rearrange("(e x) -> x e", x=T + C)[0:P, :])
+
         load_planes(nc.gpsimd, w1s, w1_scales[:, 0])
         make_identity(nc, ident[:])
-        for dst, planes, q in later[:LATER_ON_GPSIMD]:
-            load_quadrant(nc.gpsimd, dst, planes, q)
+        load_planes(nc.gpsimd, w3ts, w3t_scales[:, 0])
         nc.sync.dma_start(offsets[:], offs)
         load_pass(xw, x_words[0])
         load_planes(nc.sync, xs, x_scales)
@@ -104,46 +117,60 @@ def tile_moe_rec_glu_sigmoid_kernel(
         load_planes(nc.sync, w3s, w3_scales[:, 0])
         load_passes(w2[0], w2t_words[0])
         load_planes(nc.sync, w2s[0], w2_planes[0:4])
-        with nc.allow_non_contiguous_dma(reason="one gate value a partition"):
-            nc.sync.dma_start(
-                gcol[:], gate.rearrange("r c -> (r c)")[0 : E * (T + C)].rearrange("(e x) -> x e", x=T + C)[0:P, :])
-        for dst, planes, q in later[LATER_ON_GPSIMD:]:
-            load_quadrant(nc.sync, dst, planes, q)
-        for e in range(1, E):
-            if e >= EARLY:
-                load_pass(w1[e], w1_words[e, 0])
-                load_pass(w3[e], w3_words[e, 0])
-            load_passes(w2[e], w2t_words[e])
-            load_back(e - 1)
-        load_back(LAST)
+        load_gate(nc.sync)
+        load_passes(w2[1], w2t_words[1])
+        load_planes(nc.sync, w1ts, w1t_scales[:, 0])
+        load_pass(w1t[0], w1t_words[0, 0])
+        load_pass(w3t[0], w3t_words[0, 0])
+        load_pass(w1[2], w1_words[2, 0])
+        load_pass(w3[2], w3_words[2, 0])
+        load_planes(nc.sync, w2s[1], w2_planes[4:8])
+        load_passes(w2[2], w2t_words[2])
+        load_pass(w1[3], w1_words[3, 0])
+        load_pass(w1t[1], w1t_words[1, 0])
+        load_pass(w3t[1], w3t_words[1, 0])
+        load_pass(w3[3], w3_words[3, 0])
+        load_passes(w2[3], w2t_words[3])
+        load_pass(w1t[2], w1t_words[2, 0])
+        load_pass(w3t[2], w3t_words[2, 0])
+        load_pass(w1t[3], w1t_words[3, 0])
+        load_pass(w3t[3], w3t_words[3, 0])
 
         def slots(e):
             return slice(e * C, (e + 1) * C)
 
-        def listed(e):
-            return offsets[:, e * C // 16 : (e + 1) * C // 16]
+        def listed(first_expert, experts=1):
+            return offsets[:, first_expert * C // 16 : (first_expert + experts) * C // 16]
 
-        def gather_x(e):
-            nc.vector.tensor_copy(xg[:, slots(e)], xw[:].bitcast(U32).indirect(listed(e)))
-            nc.vector.tensor_copy(xsg[:, slots(e)], xs[:].indirect(listed(e)))
+        def gather_x(g):
+            cols = slice(g * PAIR * C, (g + 1) * PAIR * C)
+            nc.vector.tensor_copy(xg[:, cols], xw[:].bitcast(U32).indirect(listed(g * PAIR, PAIR)))
+            nc.vector.tensor_copy(xsg[:, cols], xs[:].indirect(listed(g * PAIR, PAIR)))
 
-        def gather_dy(e, after=(None, None, None)):
-            picked = [tile([P, C], U32, "dyg%d_%d" % (e, s), after[s]) for s in range(PASSES)]
-            picked_scales = tile([P, C], U8, "dysg%d" % e, after[PASSES])
+        def gather_dy(g, after=(None, None)):
+            picked = tile([P, PASSES, PAIR * C], U32, "dyg%d" % g, after[0])
+            picked_scales = tile([P, PAIR * C], U8, "dysg%d" % g, after[1])
             for s in range(PASSES):
-                nc.vector.tensor_copy(picked[s][:], dyw[:, s, :].bitcast(U32).indirect(listed(e)))
-            nc.vector.tensor_copy(picked_scales[:], dys[:].indirect(listed(e)))
-            gathered[e] = (picked, picked_scales)
+                nc.vector.tensor_copy(picked[:, s, :], dyw[:, s, :].bitcast(U32).indirect(listed(g * PAIR, PAIR)))
+            nc.vector.tensor_copy(picked_scales[:], dys[:].indirect(listed(g * PAIR, PAIR)))
+            gathered[g] = (picked, picked_scales)
+
+        def banks_of(e):
+            return ((a1_bank, a3_bank), (spare_bank, dx_bank[1]), (a1_bank, a3_bank), (spare_bank, a3_bank))[e]
 
         def first(e):
             cols = slots(e)
-            for acc, w, ws in ((a1_bank[e % 2], w1, w1s), (a3_bank[e % 2], w3, w3s)):
+            for acc, w, ws in zip(banks_of(e), (w1, w3), (w1s, w3s)):
                 nc.tensor.matmul_mx(acc[:], lhsT=xg[:, cols].bitcast(X4), lhsT_scale=xsg[:, cols],
                                     rhs=w[e][:].bitcast(X4), rhs_scale=ws[4 * e : P, :], start=True, stop=True)
-            picked, picked_scales = gathered[e]
+
+        def gradient(e):
+            picked, picked_scales = gathered[e // PAIR]
+            own = slots(e % PAIR)
             for s in range(PASSES):
                 plane = PASSES * e + s
-                nc.tensor.matmul_mx(dh_bank[e % 2][:], lhsT=picked[s][:].bitcast(X4), lhsT_scale=picked_scales[4 * s : P, :],
+                nc.tensor.matmul_mx(dh_bank[e % 2][:], lhsT=picked[:, s, own].bitcast(X4),
+                                    lhsT_scale=picked_scales[4 * s : P, own],
                                     rhs=w2[e][:, s, :].bitcast(X4), rhs_scale=w2s[plane // 4][4 * (plane % 4) : P, :],
                                     start=(s == 0), stop=(s == PASSES - 1))
 
@@ -153,90 +180,118 @@ def tile_moe_rec_glu_sigmoid_kernel(
         def flat(values):
             return values[:].rearrange("p r m t -> p (r m t)")
 
-        def slope(e):
-            a3 = a3_bank[e % 2]
+        def sigmoid(e):
             sig = tile([P, 2, C, 2], F32, "sig%d" % e)
-            u = tile([P, 2, C, 2], F32, "u%d" % e)
-            nc.scalar.activation(sig[:], by_pair(a1_bank[e % 2]), ACT.Sigmoid)
-            if e < EARLY:
+            nc.scalar.activation(sig[:], by_pair(banks_of(e)[0]), ACT.Sigmoid)
+            sigs[e] = sig
+
+        def slope(e):
+            a1, a3 = banks_of(e)
+            if e in U_POS:
+                rest = tile([P, 2, C, 2], F32, "rest%d" % e)
+                nc.scalar.activation(rest[:], by_pair(a1), ACT.Sigmoid, scale=-1.0)
+                u = tile([P, 2, C, 2], F32, "u%d" % e, U_AFTER.get(e))
+                nc.vector.tensor_tensor(u[:], by_pair(a3), rest[:], MULT)
+            elif e not in U_G:
+                u = tile([P, 2, C, 2], F32, "u%d" % e, U_AFTER.get(e))
                 for r in range(2):
-                    nc.vector.scalar_tensor_tensor(u[:, r], sig[:, r], 1.0, by_pair(a3)[:, r], SUB, MULT)
+                    nc.vector.scalar_tensor_tensor(u[:, r], sigs[e][:, r], 1.0, by_pair(a3)[:, r], SUB, MULT)
             else:
+                rest = tile([P, 2, C, 2], F32, "rest%d" % e)
+                nc.scalar.activation(rest[:], by_pair(a1), ACT.Sigmoid, scale=-1.0)
                 a3_copy = tile([P, 2, C, 2], F32, "a3_copy%d" % e)
                 nc.scalar.copy(a3_copy[:], by_pair(a3))
-                rest = tile([P, H], F32, "rest%d" % e)
-                nc.gpsimd.tensor_scalar(rest[:], flat(sig), -1.0, 1.0, MULT, ADD)
-                nc.gpsimd.tensor_tensor(flat(u), flat(a3_copy), rest[:], MULT)
-            factors[e] = (sig, u)
+                u = tile([P, 2, C, 2], F32, "u%d" % e, U_AFTER.get(e))
+                nc.gpsimd.tensor_tensor(flat(u), flat(a3_copy), flat(rest), MULT)
+            factors[e] = u
 
-        def products(e):
-            sig, u = factors[e]
-            da3 = tile([P, 2, C, 2], F32, "da3_%d" % e)
-            da1 = tile([P, 2, C, 2], BF16, "da1_%d" % e)
+        def da3_tag(e):
+            return DA3_AFTER[e]
+
+        def product3(e):
+            sig = sigs[e]
+            da3 = tile([P, 2, C, 2], F32, "da3_%d" % e, da3_tag(e))
             for r in range(2):
                 nc.vector.scalar_tensor_tensor(
                     da3[:, r], by_pair(dh_bank[e % 2])[:, r], gcol[:, e : e + 1], sig[:, r], MULT, MULT)
-            if e < EARLY:
+            da3s[e] = da3
+
+        def product1(e):
+            da3, u = da3s[e], factors[e]
+            da1 = tile([P, 2, C, 2], BF16, "da1_%d" % e, DA1_AFTER.get(e))
+            if e not in U_G and e not in U_POS:
                 nc.vector.scalar_tensor_tensor(flat(da1), flat(da3), -1.0, flat(u), MULT, MULT)
             else:
-                (nc.gpsimd if e == LAST else nc.vector).tensor_tensor(flat(da1), flat(da3), flat(u), MULT)
+                (nc.gpsimd if e in DA1_G else nc.vector).tensor_tensor(flat(da1), flat(da3), flat(u), MULT)
             made[e] = (da3, da1)
 
         def turn(e):
             da3, da1 = made[e]
-            da3_bank = a1_bank[e % 2] if e == LAST else lower_bank
-            rounded = work.tile([P, 2, C, 4], BF16, name="rounded", align_bytes=64)
+            da3_bank = bank[T3_BANK[e]]
+            rounded = tile([P, 2, C, 4], BF16, "rounded%d" % e)
             for d in range(4):
                 nc.tensor.transpose(da3_bank[:, d * C : (d + 1) * C], da3[:, d // 2, :, d % 2], ident[:])
             nc.scalar.copy(rounded[:, 0], da3_bank[:].rearrange("p (d c) -> p c d", d=4))
             pairs = da1[:].rearrange("p r m t -> p r (m t)").bitcast(F32)
             for r in range(2):
-                nc.tensor.transpose(upper_bank[:, r * C : (r + 1) * C], pairs[:, r, :], ident[:])
-            nc.scalar.copy(rounded[:, 1].bitcast(F32), upper_bank[:, 0 : 2 * C].rearrange("p (r c) -> p c r", r=2))
+                nc.tensor.transpose(da1_bank[:, r * C : (r + 1) * C], pairs[:, r, :], ident[:])
+            nc.scalar.copy(rounded[:, 1].bitcast(F32), da1_bank[:, 0 : 2 * C].rearrange("p (r c) -> p c r", r=2))
             da_words = work.tile([P, 2 * C], U32, name="da_words", align_bytes=64)
             da_scales = work.tile([P, 2 * C], U8, name="da_scales", align_bytes=64)
             nc.vector.quantize_mx(da_words[:].bitcast(X4), da_scales[:], rounded[:].rearrange("p j c d -> p (j c d)"))
             packed[e] = (da_words, da_scales)
 
-        def back(e, half):
+        def back(e):
             da_words, da_scales = packed[e]
-            acc = upper_bank if half else lower_bank
-            for h in range(2):
-                kt = 2 * half + h
+            for kt in range(ROW_TILES):
                 kc = slice(kt * P, (kt + 1) * P)
                 for j, (w, ws) in enumerate(((w3t, w3ts), (w1t, w1ts))):
                     dc = slice(j * C, (j + 1) * C)
-                    nc.tensor.matmul_mx(acc[:, h * C : (h + 1) * C], lhsT=w[e][:, kc].bitcast(X4),
+                    nc.tensor.matmul_mx(dx_at[kt], lhsT=w[e][:, kc].bitcast(X4),
                                         lhsT_scale=ws[4 * e : P, kc], rhs=da_words[:, dc].bitcast(X4),
                                         rhs_scale=da_scales[:, dc], start=(j == 0), stop=(j == 1))
-            for h in range(2):
-                kt = 2 * half + h
-                dx = tile([P, C], F32, "dx%d_%d" % (e, kt))
-                nc.scalar.copy(dx[:], acc[:, h * C : (h + 1) * C])
+
+        def scatter(e, kts):
+            for kt in kts:
+                after = DX_AFTER.get((e, kt))
+                dx = tile([P, C], F32, "dx%d_%d" % (e, kt), after)
+                nc.scalar.copy(dx[:], dx_at[kt])
                 nc.vector.tensor_copy(rows[kt][:].indirect(listed(e)), dx[:])
                 if e == LAST:
                     nc.sync.dma_start(out[kt * P : (kt + 1) * P, :], rows[kt][:])
 
-        gathered, factors, made, packed = {}, {}, {}, {}
-        for e in range(E):
-            gather_x(e)
-        for e in range(LAST):
-            gather_dy(e)
+        gathered, sigs, factors, da3s, made, packed = {}, {}, {}, {}, {}, {}
+        gather_x(0)
+        gather_dy(0)
+        gather_x(1)
+        gather_dy(1)
         first(0)
+        gradient(0)
+        sigmoid(0)
         slope(0)
-        products(0)
-        gather_dy(LAST, after=("u0", "sig0", "dysg0"))
-        turn(0)
+        product3(0)
+        product1(0)
         first(1)
+        sigmoid(1)
         slope(1)
-        products(1)
+        turn(0)
+        gradient(1)
+        back(0)
+        product3(1)
+        product1(1)
         for e in range(E):
-            back(e, 0)
+            before = BEFORE[e]
+            scatter(e, range(before))
             if e + 1 < E:
                 turn(e + 1)
             if e + 2 < E:
                 first(e + 2)
+                gradient(e + 2)
+                sigmoid(e + 2)
                 slope(e + 2)
-            back(e, 1)
             if e + 2 < E:
-                products(e + 2)
+                product3(e + 2)
+                product1(e + 2)
+            scatter(e, range(before, ROW_TILES))
+            if e + 1 < E:
+                back(e + 1)

@@ -22,15 +22,19 @@ P = 128
 PASSES = N // 512
 ROW_TILES = K // P
 LAST = E - 1
-U_G = (2, 3)
+U_G = (2,)
 U_AFTER = {2: "rounded1"}
 DA3_AFTER = ("da3_0", "rounded0", "da3_2", "da3_3")
-DA1_G = (2, 3)
+DA1_G = (2,)
 DA1_AFTER = {}
 DX_AFTER = {}
 T3_BANK = (6, 6, 6, 6)
 U_POS = ()
 BEFORE = (3, 3, 2, 4)
+REST_G = ()
+FIRST_EARLY = ()
+X_LATE = ()
+P3_FIRST = False
 PAIR = 2
 EARLY = 2
 LATER_ON_GPSIMD = 6
@@ -64,6 +68,7 @@ def tile_moe_rec_glu_sigmoid_kernel(
         w1ts = tile([P, K], U8, "w1ts")
         w3ts = tile([P, K], U8, "w3ts")
         gcol = keep.tile([P, E], F32, name="gcol")
+        grows = tile([P, P], F32, "grows")
         ident = tile([P, P], F32, "ident")
         w1_early = tile([P, EARLY, H], I32, "w1_early")
         w1 = [w1_early[:, e, :] for e in range(EARLY)] + [tile([P, H], I32, "w1_%d" % e) for e in range(EARLY, E)]
@@ -72,15 +77,18 @@ def tile_moe_rec_glu_sigmoid_kernel(
         w2 = [tile([P, PASSES, H], I32, "w2_%d" % e) for e in range(E)]
         w1t = [tile([P, K], I32, "w1t_%d" % e) for e in range(E)]
         w3t = [tile([P, K], I32, "w3t_%d" % e) for e in range(E)]
-        xg = tile([P, E * C], U32, "xg")
-        xsg = tile([P, E * C], U8, "xsg")
+
+        def load_half(dst, src, h):
+            half = slice(h * K // 2, (h + 1) * K // 2)
+            nc.sync.dma_start(dst[:, half], src.rearrange("p n d -> p (n d)").bitcast(I32)[:, half])
+
         rows = [tile([P, T], F32, "rows%d" % kt) for kt in range(ROW_TILES)]
 
-        def load_pass(dst, src):
-            nc.sync.dma_start(dst[:], src.rearrange("p n d -> p (n d)").bitcast(I32))
+        def load_pass(dst, src, eng=nc.sync):
+            eng.dma_start(dst[:], src.rearrange("p n d -> p (n d)").bitcast(I32))
 
-        def load_passes(dst, src):
-            nc.sync.dma_start(dst[:], src.rearrange("s p n d -> p s (n d)").bitcast(I32))
+        def load_passes(dst, src, eng=nc.sync):
+            eng.dma_start(dst[:], src.rearrange("s p n d -> p s (n d)").bitcast(I32))
 
         def load_quadrant(eng, dst, planes, q):
             count = planes.shape[0]
@@ -97,12 +105,11 @@ def tile_moe_rec_glu_sigmoid_kernel(
         nc.gpsimd.memset(w1s[:].bitcast(I32), 0)
         for planes in (xs, dys, w3s, w2s[0], w3ts, w1ts, w2s[1]):
             nc.vector.memset(planes[:].bitcast(I32), 0)
+        nc.vector.memset(grows[:], 0.0)
 
         w2_planes = w2t_scales.rearrange("e s b n -> (e s) b n")
         def load_gate(eng):
-            with nc.allow_non_contiguous_dma(reason="one gate value a partition"):
-                eng.dma_start(
-                    gcol[:], gate.rearrange("r c -> (r c)")[0 : E * (T + C)].rearrange("(e x) -> x e", x=T + C)[0:P, :])
+            eng.dma_start(grows[0:E, :], gate[0].rearrange("(e c) -> e c", e=E))
 
         load_planes(nc.gpsimd, w1s, w1_scales[:, 0])
         make_identity(nc, ident[:])
@@ -114,25 +121,30 @@ def tile_moe_rec_glu_sigmoid_kernel(
         load_passes(w1_early, w1_words[0:EARLY, 0])
         load_planes(nc.sync, dys, dy_scales)
         load_passes(w3_early, w3_words[0:EARLY, 0])
+        load_gate(nc.sync)
         load_planes(nc.sync, w3s, w3_scales[:, 0])
         load_passes(w2[0], w2t_words[0])
         load_planes(nc.sync, w2s[0], w2_planes[0:4])
-        load_gate(nc.sync)
+        load_quadrant(nc.sync, w1ts, w1t_scales[:, 0], 0)
         load_passes(w2[1], w2t_words[1])
-        load_planes(nc.sync, w1ts, w1t_scales[:, 0])
+        load_quadrant(nc.sync, w1ts, w1t_scales[:, 0], 1)
+        load_quadrant(nc.sync, w1ts, w1t_scales[:, 0], 2)
+        load_quadrant(nc.sync, w1ts, w1t_scales[:, 0], 3)
         load_pass(w1t[0], w1t_words[0, 0])
         load_pass(w3t[0], w3t_words[0, 0])
         load_pass(w1[2], w1_words[2, 0])
         load_pass(w3[2], w3_words[2, 0])
         load_planes(nc.sync, w2s[1], w2_planes[4:8])
         load_passes(w2[2], w2t_words[2])
-        load_pass(w1[3], w1_words[3, 0])
         load_pass(w1t[1], w1t_words[1, 0])
         load_pass(w3t[1], w3t_words[1, 0])
+        load_pass(w1[3], w1_words[3, 0])
         load_pass(w3[3], w3_words[3, 0])
         load_passes(w2[3], w2t_words[3])
-        load_pass(w1t[2], w1t_words[2, 0])
-        load_pass(w3t[2], w3t_words[2, 0])
+        load_half(w1t[2], w1t_words[2, 0], 0)
+        load_half(w3t[2], w3t_words[2, 0], 0)
+        load_half(w1t[2], w1t_words[2, 0], 1)
+        load_half(w3t[2], w3t_words[2, 0], 1)
         load_pass(w1t[3], w1t_words[3, 0])
         load_pass(w3t[3], w3t_words[3, 0])
 
@@ -142,10 +154,12 @@ def tile_moe_rec_glu_sigmoid_kernel(
         def listed(first_expert, experts=1):
             return offsets[:, first_expert * C // 16 : (first_expert + experts) * C // 16]
 
-        def gather_x(g):
-            cols = slice(g * PAIR * C, (g + 1) * PAIR * C)
-            nc.vector.tensor_copy(xg[:, cols], xw[:].bitcast(U32).indirect(listed(g * PAIR, PAIR)))
-            nc.vector.tensor_copy(xsg[:, cols], xs[:].indirect(listed(g * PAIR, PAIR)))
+        def gather_x(g, after=(None, None)):
+            xg = tile([P, PAIR * C], U32, "xg%d" % g, after[0])
+            xsg = tile([P, PAIR * C], U8, "xsg%d" % g, after[1])
+            nc.vector.tensor_copy(xg[:], xw[:].bitcast(U32).indirect(listed(g * PAIR, PAIR)))
+            nc.vector.tensor_copy(xsg[:], xs[:].indirect(listed(g * PAIR, PAIR)))
+            tokens[g] = (xg, xsg)
 
         def gather_dy(g, after=(None, None)):
             picked = tile([P, PASSES, PAIR * C], U32, "dyg%d" % g, after[0])
@@ -159,7 +173,8 @@ def tile_moe_rec_glu_sigmoid_kernel(
             return ((a1_bank, a3_bank), (spare_bank, dx_bank[1]), (a1_bank, a3_bank), (spare_bank, a3_bank))[e]
 
         def first(e):
-            cols = slots(e)
+            cols = slots(e % PAIR)
+            xg, xsg = tokens[e // PAIR]
             for acc, w, ws in zip(banks_of(e), (w1, w3), (w1s, w3s)):
                 nc.tensor.matmul_mx(acc[:], lhsT=xg[:, cols].bitcast(X4), lhsT_scale=xsg[:, cols],
                                     rhs=w[e][:].bitcast(X4), rhs_scale=ws[4 * e : P, :], start=True, stop=True)
@@ -198,11 +213,20 @@ def tile_moe_rec_glu_sigmoid_kernel(
                     nc.vector.scalar_tensor_tensor(u[:, r], sigs[e][:, r], 1.0, by_pair(a3)[:, r], SUB, MULT)
             else:
                 rest = tile([P, 2, C, 2], F32, "rest%d" % e)
-                nc.scalar.activation(rest[:], by_pair(a1), ACT.Sigmoid, scale=-1.0)
+                if e in REST_G:
+                    nc.gpsimd.tensor_scalar(flat(rest), flat(sigs[e]), -1.0, 1.0, MULT, ADD)
+                else:
+                    nc.scalar.activation(rest[:], by_pair(a1), ACT.Sigmoid, scale=-1.0)
                 a3_copy = tile([P, 2, C, 2], F32, "a3_copy%d" % e)
                 nc.scalar.copy(a3_copy[:], by_pair(a3))
-                u = tile([P, 2, C, 2], F32, "u%d" % e, U_AFTER.get(e))
-                nc.gpsimd.tensor_tensor(flat(u), flat(a3_copy), flat(rest), MULT)
+                parts[e] = (a3_copy, rest)
+                return
+            factors[e] = u
+
+        def slope_product(e):
+            a3_copy, rest = parts[e]
+            u = tile([P, 2, C, 2], F32, "u%d" % e, U_AFTER.get(e))
+            nc.gpsimd.tensor_tensor(flat(u), flat(a3_copy), flat(rest), MULT)
             factors[e] = u
 
         def da3_tag(e):
@@ -241,9 +265,9 @@ def tile_moe_rec_glu_sigmoid_kernel(
             nc.vector.quantize_mx(da_words[:].bitcast(X4), da_scales[:], rounded[:].rearrange("p j c d -> p (j c d)"))
             packed[e] = (da_words, da_scales)
 
-        def back(e):
+        def back(e, kts):
             da_words, da_scales = packed[e]
-            for kt in range(ROW_TILES):
+            for kt in kts:
                 kc = slice(kt * P, (kt + 1) * P)
                 for j, (w, ws) in enumerate(((w3t, w3ts), (w1t, w1ts))):
                     dc = slice(j * C, (j + 1) * C)
@@ -251,47 +275,66 @@ def tile_moe_rec_glu_sigmoid_kernel(
                                         lhsT_scale=ws[4 * e : P, kc], rhs=da_words[:, dc].bitcast(X4),
                                         rhs_scale=da_scales[:, dc], start=(j == 0), stop=(j == 1))
 
-        def scatter(e, kts):
+        def drain(e, kts):
             for kt in kts:
                 after = DX_AFTER.get((e, kt))
                 dx = tile([P, C], F32, "dx%d_%d" % (e, kt), after)
                 nc.scalar.copy(dx[:], dx_at[kt])
+                sums[e, kt] = dx
+
+        def scatter(e, kts):
+            for kt in kts:
+                dx = sums[e, kt]
                 nc.vector.tensor_copy(rows[kt][:].indirect(listed(e)), dx[:])
                 if e == LAST:
                     nc.sync.dma_start(out[kt * P : (kt + 1) * P, :], rows[kt][:])
 
-        gathered, sigs, factors, da3s, made, packed = {}, {}, {}, {}, {}, {}
+        gathered, sigs, factors, da3s, made, packed, sums, parts, tokens = {}, {}, {}, {}, {}, {}, {}, {}, {}
+        nc.tensor.transpose(da1_bank[:, 0:P], grows[:], ident[:])
+        nc.scalar.copy(gcol[:], da1_bank[:, 0:E])
         gather_x(0)
         gather_dy(0)
-        gather_x(1)
+        if not X_LATE:
+            gather_x(1)
         gather_dy(1)
         first(0)
         gradient(0)
         sigmoid(0)
+        if P3_FIRST:
+            product3(0)
         slope(0)
-        product3(0)
+        if not P3_FIRST:
+            product3(0)
         product1(0)
         first(1)
         sigmoid(1)
         slope(1)
         turn(0)
+        if X_LATE:
+            gather_x(1, X_LATE)
         gradient(1)
-        back(0)
+        back(0, [0, 1])
         product3(1)
         product1(1)
         for e in range(E):
             before = BEFORE[e]
-            scatter(e, range(before))
+            drain(e, [0, 1])
+            scatter(e, [0, 1])
+            back(e, [2, 3])
+            drain(e, range(2, before))
+            scatter(e, range(2, before))
             if e + 1 < E:
                 turn(e + 1)
+            drain(e, range(before, ROW_TILES))
             if e + 2 < E:
                 first(e + 2)
-                gradient(e + 2)
                 sigmoid(e + 2)
                 slope(e + 2)
-            if e + 2 < E:
+                if e + 2 in U_G:
+                    slope_product(e + 2)
+                gradient(e + 2)
                 product3(e + 2)
                 product1(e + 2)
             scatter(e, range(before, ROW_TILES))
             if e + 1 < E:
-                back(e + 1)
+                back(e + 1, [0, 1])

@@ -23,18 +23,21 @@ PASSES = N // 512
 ROW_TILES = K // P
 LAST = E - 1
 U_G = (2,)
-U_AFTER = {2: "rounded1"}
+U_AFTER = {1: "u0", 2: "rounded1"}
 DA3_AFTER = ("da3_0", "rounded0", "da3_2", "da3_3")
-DA1_G = (2,)
+DA1_G = (1, 2)
 DA1_AFTER = {}
 DX_AFTER = {}
 T3_BANK = (6, 6, 6, 6)
-U_POS = ()
+U_POS = (1,)
 BEFORE = (3, 3, 2, 4)
 REST_G = ()
 FIRST_EARLY = ()
 X_LATE = ()
 P3_FIRST = False
+NATURAL = ()
+LATE_B = ()
+LATE_C = ()
 PAIR = 2
 EARLY = 2
 LATER_ON_GPSIMD = 6
@@ -111,25 +114,34 @@ def tile_moe_rec_glu_sigmoid_kernel(
         def load_gate(eng):
             eng.dma_start(grows[0:E, :], gate[0].rearrange("(e c) -> e c", e=E))
 
-        load_planes(nc.gpsimd, w1s, w1_scales[:, 0])
+        load_quadrant(nc.gpsimd, w1s, w1_scales[:, 0], 0)
+        load_quadrant(nc.gpsimd, w1s, w1_scales[:, 0], 1)
+        load_quadrant(nc.gpsimd, w2s[0], w2_planes[0:4], 0)
+        load_quadrant(nc.gpsimd, w2s[0], w2_planes[0:4], 1)
         make_identity(nc, ident[:])
-        load_planes(nc.gpsimd, w3ts, w3t_scales[:, 0])
+        load_quadrant(nc.gpsimd, w3ts, w3t_scales[:, 0], 0)
+        load_quadrant(nc.gpsimd, w3ts, w3t_scales[:, 0], 1)
+        load_quadrant(nc.gpsimd, w3ts, w3t_scales[:, 0], 2)
         nc.sync.dma_start(offsets[:], offs)
         load_pass(xw, x_words[0])
         load_planes(nc.sync, xs, x_scales)
         load_passes(dyw, dy_words)
         load_passes(w1_early, w1_words[0:EARLY, 0])
+        load_quadrant(nc.sync, w1s, w1_scales[:, 0], 2)
+        load_quadrant(nc.sync, w1s, w1_scales[:, 0], 3)
         load_planes(nc.sync, dys, dy_scales)
         load_passes(w3_early, w3_words[0:EARLY, 0])
         load_gate(nc.sync)
         load_planes(nc.sync, w3s, w3_scales[:, 0])
         load_passes(w2[0], w2t_words[0])
-        load_planes(nc.sync, w2s[0], w2_planes[0:4])
+        load_quadrant(nc.sync, w2s[0], w2_planes[0:4], 2)
+        load_quadrant(nc.sync, w2s[0], w2_planes[0:4], 3)
         load_quadrant(nc.sync, w1ts, w1t_scales[:, 0], 0)
         load_passes(w2[1], w2t_words[1])
         load_quadrant(nc.sync, w1ts, w1t_scales[:, 0], 1)
         load_quadrant(nc.sync, w1ts, w1t_scales[:, 0], 2)
         load_quadrant(nc.sync, w1ts, w1t_scales[:, 0], 3)
+        load_quadrant(nc.sync, w3ts, w3t_scales[:, 0], 3)
         load_pass(w1t[0], w1t_words[0, 0])
         load_pass(w3t[0], w3t_words[0, 0])
         load_pass(w1[2], w1_words[2, 0])
@@ -161,13 +173,15 @@ def tile_moe_rec_glu_sigmoid_kernel(
             nc.vector.tensor_copy(xsg[:], xs[:].indirect(listed(g * PAIR, PAIR)))
             tokens[g] = (xg, xsg)
 
-        def gather_dy(g, after=(None, None)):
-            picked = tile([P, PASSES, PAIR * C], U32, "dyg%d" % g, after[0])
-            picked_scales = tile([P, PAIR * C], U8, "dysg%d" % g, after[1])
-            for s in range(PASSES):
-                nc.vector.tensor_copy(picked[:, s, :], dyw[:, s, :].bitcast(U32).indirect(listed(g * PAIR, PAIR)))
-            nc.vector.tensor_copy(picked_scales[:], dys[:].indirect(listed(g * PAIR, PAIR)))
-            gathered[g] = (picked, picked_scales)
+        def gather_dy(g, parts_=(0, 1, 2), after=None):
+            for s in parts_:
+                if s < PASSES:
+                    got = tile([P, PAIR * C], U32, "dyg%d_%d" % (g, s), after)
+                    nc.vector.tensor_copy(got[:], dyw[:, s, :].bitcast(U32).indirect(listed(g * PAIR, PAIR)))
+                else:
+                    got = tile([P, PAIR * C], U8, "dysg%d" % g, after)
+                    nc.vector.tensor_copy(got[:], dys[:].indirect(listed(g * PAIR, PAIR)))
+                gathered[g, s] = got
 
         def banks_of(e):
             return ((a1_bank, a3_bank), (spare_bank, dx_bank[1]), (a1_bank, a3_bank), (spare_bank, a3_bank))[e]
@@ -180,16 +194,19 @@ def tile_moe_rec_glu_sigmoid_kernel(
                                     rhs=w[e][:].bitcast(X4), rhs_scale=ws[4 * e : P, :], start=True, stop=True)
 
         def gradient(e):
-            picked, picked_scales = gathered[e // PAIR]
+            picked = [gathered[e // PAIR, s] for s in range(PASSES)]
+            picked_scales = gathered[e // PAIR, PASSES]
             own = slots(e % PAIR)
             for s in range(PASSES):
                 plane = PASSES * e + s
-                nc.tensor.matmul_mx(dh_bank[e % 2][:], lhsT=picked[:, s, own].bitcast(X4),
+                nc.tensor.matmul_mx(dh_bank[e % 2][:], lhsT=picked[s][:, own].bitcast(X4),
                                     lhsT_scale=picked_scales[4 * s : P, own],
                                     rhs=w2[e][:, s, :].bitcast(X4), rhs_scale=w2s[plane // 4][4 * (plane % 4) : P, :],
                                     start=(s == 0), stop=(s == PASSES - 1))
 
-        def by_pair(sums):
+        def by_pair(sums, e):
+            if e in NATURAL:
+                return sums[:].rearrange("p (r m t) -> p r m t", r=2, t=2)
             return sums[:].rearrange("p (m r t) -> p r m t", r=2, t=2)
 
         def flat(values):
@@ -197,28 +214,31 @@ def tile_moe_rec_glu_sigmoid_kernel(
 
         def sigmoid(e):
             sig = tile([P, 2, C, 2], F32, "sig%d" % e)
-            nc.scalar.activation(sig[:], by_pair(banks_of(e)[0]), ACT.Sigmoid)
+            nc.scalar.activation(sig[:], by_pair(banks_of(e)[0], e), ACT.Sigmoid)
             sigs[e] = sig
 
         def slope(e):
             a1, a3 = banks_of(e)
             if e in U_POS:
                 rest = tile([P, 2, C, 2], F32, "rest%d" % e)
-                nc.scalar.activation(rest[:], by_pair(a1), ACT.Sigmoid, scale=-1.0)
+                nc.scalar.activation(rest[:], by_pair(a1, e), ACT.Sigmoid, scale=-1.0)
                 u = tile([P, 2, C, 2], F32, "u%d" % e, U_AFTER.get(e))
-                nc.vector.tensor_tensor(u[:], by_pair(a3), rest[:], MULT)
+                nc.vector.tensor_tensor(u[:], by_pair(a3, e), rest[:], MULT)
             elif e not in U_G:
                 u = tile([P, 2, C, 2], F32, "u%d" % e, U_AFTER.get(e))
-                for r in range(2):
-                    nc.vector.scalar_tensor_tensor(u[:, r], sigs[e][:, r], 1.0, by_pair(a3)[:, r], SUB, MULT)
+                if e in NATURAL:
+                    nc.vector.scalar_tensor_tensor(flat(u), flat(sigs[e]), 1.0, a3[:], SUB, MULT)
+                else:
+                    for r in range(2):
+                        nc.vector.scalar_tensor_tensor(u[:, r], sigs[e][:, r], 1.0, by_pair(a3, e)[:, r], SUB, MULT)
             else:
                 rest = tile([P, 2, C, 2], F32, "rest%d" % e)
                 if e in REST_G:
                     nc.gpsimd.tensor_scalar(flat(rest), flat(sigs[e]), -1.0, 1.0, MULT, ADD)
                 else:
-                    nc.scalar.activation(rest[:], by_pair(a1), ACT.Sigmoid, scale=-1.0)
+                    nc.scalar.activation(rest[:], by_pair(a1, e), ACT.Sigmoid, scale=-1.0)
                 a3_copy = tile([P, 2, C, 2], F32, "a3_copy%d" % e)
-                nc.scalar.copy(a3_copy[:], by_pair(a3))
+                nc.scalar.copy(a3_copy[:], by_pair(a3, e))
                 parts[e] = (a3_copy, rest)
                 return
             factors[e] = u
@@ -235,9 +255,12 @@ def tile_moe_rec_glu_sigmoid_kernel(
         def product3(e):
             sig = sigs[e]
             da3 = tile([P, 2, C, 2], F32, "da3_%d" % e, da3_tag(e))
-            for r in range(2):
-                nc.vector.scalar_tensor_tensor(
-                    da3[:, r], by_pair(dh_bank[e % 2])[:, r], gcol[:, e : e + 1], sig[:, r], MULT, MULT)
+            if e in NATURAL:
+                nc.vector.scalar_tensor_tensor(flat(da3), dh_bank[e % 2][:], gcol[:, e : e + 1], flat(sig), MULT, MULT)
+            else:
+                for r in range(2):
+                    nc.vector.scalar_tensor_tensor(
+                        da3[:, r], by_pair(dh_bank[e % 2], e)[:, r], gcol[:, e : e + 1], sig[:, r], MULT, MULT)
             da3s[e] = da3
 
         def product1(e):
@@ -254,9 +277,11 @@ def tile_moe_rec_glu_sigmoid_kernel(
             da3_bank = bank[T3_BANK[e]]
             rounded = tile([P, 2, C, 4], BF16, "rounded%d" % e)
             for d in range(4):
-                nc.tensor.transpose(da3_bank[:, d * C : (d + 1) * C], da3[:, d // 2, :, d % 2], ident[:])
+                nc.tensor.transpose(da3_bank[:, d * C : (d + 1) * C], flat(da3)[:, d::4] if e in NATURAL else da3[:, d // 2, :, d % 2], ident[:])
             nc.scalar.copy(rounded[:, 0], da3_bank[:].rearrange("p (d c) -> p c d", d=4))
             pairs = da1[:].rearrange("p r m t -> p r (m t)").bitcast(F32)
+            if e in NATURAL:
+                pairs = flat(da1).bitcast(F32).rearrange("p (m r) -> p r m", r=2)
             for r in range(2):
                 nc.tensor.transpose(da1_bank[:, r * C : (r + 1) * C], pairs[:, r, :], ident[:])
             nc.scalar.copy(rounded[:, 1].bitcast(F32), da1_bank[:, 0 : 2 * C].rearrange("p (r c) -> p c r", r=2))
@@ -296,7 +321,7 @@ def tile_moe_rec_glu_sigmoid_kernel(
         gather_dy(0)
         if not X_LATE:
             gather_x(1)
-        gather_dy(1)
+        gather_dy(1, [s for s in range(3) if s not in LATE_B and s not in LATE_C])
         first(0)
         gradient(0)
         sigmoid(0)
@@ -312,10 +337,14 @@ def tile_moe_rec_glu_sigmoid_kernel(
         turn(0)
         if X_LATE:
             gather_x(1, X_LATE)
+        for s in LATE_B:
+            gather_dy(1, [s], "da3_0")
         gradient(1)
         back(0, [0, 1])
         product3(1)
         product1(1)
+        for s in LATE_C:
+            gather_dy(1, [s], "sig1")
         for e in range(E):
             before = BEFORE[e]
             drain(e, [0, 1])
@@ -323,13 +352,18 @@ def tile_moe_rec_glu_sigmoid_kernel(
             back(e, [2, 3])
             drain(e, range(2, before))
             scatter(e, range(2, before))
+            if e in FIRST_EARLY:
+                first(e + 2)
+                sigmoid(e + 2)
+                slope(e + 2)
             if e + 1 < E:
                 turn(e + 1)
             drain(e, range(before, ROW_TILES))
             if e + 2 < E:
-                first(e + 2)
-                sigmoid(e + 2)
-                slope(e + 2)
+                if e not in FIRST_EARLY:
+                    first(e + 2)
+                    sigmoid(e + 2)
+                    slope(e + 2)
                 if e + 2 in U_G:
                     slope_product(e + 2)
                 gradient(e + 2)

@@ -15,32 +15,16 @@ U8 = mybir.dt.uint8
 X4 = mybir.dt.float8_e4m3fn_x4
 ACT = mybir.ActivationFunctionType
 MULT = mybir.AluOpType.mult
-ADD = mybir.AluOpType.add
 SUB = mybir.AluOpType.subtract
 
 P = 128
 PASSES = N // 512
 ROW_TILES = K // P
+QUADRANTS = 4
 LAST = E - 1
-U_G = (2,)
-U_AFTER = {1: "u0", 2: "rounded1"}
-DA3_AFTER = ("da3_0", "rounded0", "da3_2", "da3_3")
-DA1_G = (1, 2)
-DA1_AFTER = {}
-DX_AFTER = {}
-T3_BANK = (6, 6, 6, 6)
-U_POS = (1,)
-BEFORE = (3, 3, 2, 4)
-REST_G = ()
-FIRST_EARLY = ()
-X_LATE = ()
-P3_FIRST = False
-NATURAL = ()
-LATE_B = ()
-LATE_C = ()
 PAIR = 2
-EARLY = 2
-LATER_ON_GPSIMD = 6
+W1S_ON_GPSIMD, W2S_ON_GPSIMD, W3TS_ON_GPSIMD = 3, 2, 2
+W1TS_FIRST = 2
 
 
 def tile_moe_rec_glu_sigmoid_kernel(
@@ -53,8 +37,9 @@ def tile_moe_rec_glu_sigmoid_kernel(
         work = ctx.enter_context(tc.tile_pool(name="work", bufs=E))
         psum = ctx.enter_context(tc.psum_pool(name="psum", bufs=1))
         bank = [psum.tile([P, H], F32, name="bank%d" % b) for b in range(8)]
-        a1_bank, a3_bank, dh_bank, spare_bank, da1_bank, dx_bank = bank[0], bank[1], bank[2:4], bank[4], bank[5], bank[6:8]
-        da3_bank = dx_bank[0]
+        a1_bank, dh_bank = (bank[0], bank[4]), (bank[2], bank[3])
+        a3_bank = (bank[1], bank[7], bank[1], bank[1])
+        da3_bank, da1_bank = bank[6], bank[5]
         dx_at = (da3_bank[:, 0:C], da1_bank[:, 0:C], da1_bank[:, 2 * C : 3 * C], da1_bank[:, 3 * C : 4 * C])
 
         def tile(shape, dtype, name, after=None):
@@ -67,39 +52,32 @@ def tile_moe_rec_glu_sigmoid_kernel(
         dys = tile([P, T], U8, "dys")
         w1s = tile([P, H], U8, "w1s")
         w3s = tile([P, H], U8, "w3s")
-        w2s = [tile([P, H], U8, "w2s%d" % j) for j in range(E * PASSES // 4)]
+        w2s = [tile([P, H], U8, "w2s%d" % g) for g in range(E // PAIR)]
         w1ts = tile([P, K], U8, "w1ts")
         w3ts = tile([P, K], U8, "w3ts")
-        gcol = keep.tile([P, E], F32, name="gcol")
-        grows = tile([P, P], F32, "grows")
+        gate_by_slot = keep.tile([P, E], F32, name="gate_by_slot")
+        gate_rows = tile([P, P], F32, "gate_rows")
         ident = tile([P, P], F32, "ident")
-        w1_early = tile([P, EARLY, H], I32, "w1_early")
-        w1 = [w1_early[:, e, :] for e in range(EARLY)] + [tile([P, H], I32, "w1_%d" % e) for e in range(EARLY, E)]
-        w3_early = tile([P, EARLY, H], I32, "w3_early")
-        w3 = [w3_early[:, e, :] for e in range(EARLY)] + [tile([P, H], I32, "w3_%d" % e) for e in range(EARLY, E)]
+        w1_pair = tile([P, PAIR, H], I32, "w1_pair")
+        w1 = [w1_pair[:, e, :] for e in range(PAIR)] + [tile([P, H], I32, "w1_%d" % e) for e in range(PAIR, E)]
+        w3_pair = tile([P, PAIR, H], I32, "w3_pair")
+        w3 = [w3_pair[:, e, :] for e in range(PAIR)] + [tile([P, H], I32, "w3_%d" % e) for e in range(PAIR, E)]
         w2 = [tile([P, PASSES, H], I32, "w2_%d" % e) for e in range(E)]
         w1t = [tile([P, K], I32, "w1t_%d" % e) for e in range(E)]
         w3t = [tile([P, K], I32, "w3t_%d" % e) for e in range(E)]
-
-        def load_half(dst, src, h):
-            half = slice(h * K // 2, (h + 1) * K // 2)
-            nc.sync.dma_start(dst[:, half], src.rearrange("p n d -> p (n d)").bitcast(I32)[:, half])
-
         rows = [tile([P, T], F32, "rows%d" % kt) for kt in range(ROW_TILES)]
 
-        def load_pass(dst, src, eng=nc.sync):
-            eng.dma_start(dst[:], src.rearrange("p n d -> p (n d)").bitcast(I32))
+        def load_pass(dst, src):
+            nc.sync.dma_start(dst[:], src.rearrange("p n d -> p (n d)").bitcast(I32))
 
-        def load_passes(dst, src, eng=nc.sync):
-            eng.dma_start(dst[:], src.rearrange("s p n d -> p s (n d)").bitcast(I32))
+        def load_passes(dst, src):
+            nc.sync.dma_start(dst[:], src.rearrange("s p n d -> p s (n d)").bitcast(I32))
 
-        def load_quadrant(eng, dst, planes, q):
+        def load_planes(eng, dst, planes, first=0, end=QUADRANTS):
             count = planes.shape[0]
-            eng.dma_start(dst[32 * q : 32 * q + 4 * count, :].bitcast(I32), planes[:, 4 * q : 4 * q + 4, :].bitcast(I32))
-
-        def load_planes(eng, dst, planes):
-            for q in range(4):
-                load_quadrant(eng, dst, planes, q)
+            for q in range(first, end):
+                eng.dma_start(dst[32 * q : 32 * q + 4 * count, :].bitcast(I32),
+                              planes[:, 4 * q : 4 * q + 4, :].bitcast(I32))
 
         def load_back(e):
             load_pass(w1t[e], w1t_words[e, 0])
@@ -108,57 +86,41 @@ def tile_moe_rec_glu_sigmoid_kernel(
         nc.gpsimd.memset(w1s[:].bitcast(I32), 0)
         for planes in (xs, dys, w3s, w2s[0], w3ts, w1ts, w2s[1]):
             nc.vector.memset(planes[:].bitcast(I32), 0)
-        nc.vector.memset(grows[:], 0.0)
+        nc.vector.memset(gate_rows[:], 0.0)
 
-        w2_planes = w2t_scales.rearrange("e s b n -> (e s) b n")
-        def load_gate(eng):
-            eng.dma_start(grows[0:E, :], gate[0].rearrange("(e c) -> e c", e=E))
-
-        load_quadrant(nc.gpsimd, w1s, w1_scales[:, 0], 0)
-        load_quadrant(nc.gpsimd, w1s, w1_scales[:, 0], 1)
-        load_quadrant(nc.gpsimd, w2s[0], w2_planes[0:4], 0)
-        load_quadrant(nc.gpsimd, w2s[0], w2_planes[0:4], 1)
+        w2_planes = w2t_scales.rearrange("(g e) s b n -> g (e s) b n", e=PAIR)
+        load_planes(nc.gpsimd, w1s, w1_scales[:, 0], end=W1S_ON_GPSIMD)
+        load_planes(nc.gpsimd, w2s[0], w2_planes[0], end=W2S_ON_GPSIMD)
         make_identity(nc, ident[:])
-        load_quadrant(nc.gpsimd, w3ts, w3t_scales[:, 0], 0)
-        load_quadrant(nc.gpsimd, w3ts, w3t_scales[:, 0], 1)
-        load_quadrant(nc.gpsimd, w3ts, w3t_scales[:, 0], 2)
+        load_planes(nc.gpsimd, w3ts, w3t_scales[:, 0], end=W3TS_ON_GPSIMD)
+
         nc.sync.dma_start(offsets[:], offs)
         load_pass(xw, x_words[0])
         load_planes(nc.sync, xs, x_scales)
         load_passes(dyw, dy_words)
-        load_passes(w1_early, w1_words[0:EARLY, 0])
-        load_quadrant(nc.sync, w1s, w1_scales[:, 0], 2)
-        load_quadrant(nc.sync, w1s, w1_scales[:, 0], 3)
+        load_passes(w1_pair, w1_words[0:PAIR, 0])
+        load_planes(nc.sync, w1s, w1_scales[:, 0], first=W1S_ON_GPSIMD)
         load_planes(nc.sync, dys, dy_scales)
-        load_passes(w3_early, w3_words[0:EARLY, 0])
-        load_gate(nc.sync)
+        load_passes(w3_pair, w3_words[0:PAIR, 0])
+        nc.sync.dma_start(gate_rows[0:E, :], gate[0].rearrange("(e c) -> e c", e=E))
         load_planes(nc.sync, w3s, w3_scales[:, 0])
         load_passes(w2[0], w2t_words[0])
-        load_quadrant(nc.sync, w2s[0], w2_planes[0:4], 2)
-        load_quadrant(nc.sync, w2s[0], w2_planes[0:4], 3)
-        load_quadrant(nc.sync, w1ts, w1t_scales[:, 0], 0)
+        load_planes(nc.sync, w2s[0], w2_planes[0], first=W2S_ON_GPSIMD)
+        load_planes(nc.sync, w1ts, w1t_scales[:, 0], end=W1TS_FIRST)
         load_passes(w2[1], w2t_words[1])
-        load_quadrant(nc.sync, w1ts, w1t_scales[:, 0], 1)
-        load_quadrant(nc.sync, w1ts, w1t_scales[:, 0], 2)
-        load_quadrant(nc.sync, w1ts, w1t_scales[:, 0], 3)
-        load_quadrant(nc.sync, w3ts, w3t_scales[:, 0], 3)
-        load_pass(w1t[0], w1t_words[0, 0])
-        load_pass(w3t[0], w3t_words[0, 0])
+        load_planes(nc.sync, w1ts, w1t_scales[:, 0], first=W1TS_FIRST)
+        load_planes(nc.sync, w3ts, w3t_scales[:, 0], first=W3TS_ON_GPSIMD)
+        load_back(0)
         load_pass(w1[2], w1_words[2, 0])
         load_pass(w3[2], w3_words[2, 0])
-        load_planes(nc.sync, w2s[1], w2_planes[4:8])
+        load_planes(nc.sync, w2s[1], w2_planes[1])
         load_passes(w2[2], w2t_words[2])
-        load_pass(w1t[1], w1t_words[1, 0])
-        load_pass(w3t[1], w3t_words[1, 0])
         load_pass(w1[3], w1_words[3, 0])
+        load_back(1)
         load_pass(w3[3], w3_words[3, 0])
         load_passes(w2[3], w2t_words[3])
-        load_half(w1t[2], w1t_words[2, 0], 0)
-        load_half(w3t[2], w3t_words[2, 0], 0)
-        load_half(w1t[2], w1t_words[2, 0], 1)
-        load_half(w3t[2], w3t_words[2, 0], 1)
-        load_pass(w1t[3], w1t_words[3, 0])
-        load_pass(w3t[3], w3t_words[3, 0])
+        load_back(2)
+        load_back(3)
 
         def slots(e):
             return slice(e * C, (e + 1) * C)
@@ -166,209 +128,155 @@ def tile_moe_rec_glu_sigmoid_kernel(
         def listed(first_expert, experts=1):
             return offsets[:, first_expert * C // 16 : (first_expert + experts) * C // 16]
 
-        def gather_x(g, after=(None, None)):
-            xg = tile([P, PAIR * C], U32, "xg%d" % g, after[0])
-            xsg = tile([P, PAIR * C], U8, "xsg%d" % g, after[1])
-            nc.vector.tensor_copy(xg[:], xw[:].bitcast(U32).indirect(listed(g * PAIR, PAIR)))
-            nc.vector.tensor_copy(xsg[:], xs[:].indirect(listed(g * PAIR, PAIR)))
-            tokens[g] = (xg, xsg)
+        def gather(window, dtype, name, g):
+            picked = tile([P, PAIR * C], dtype, name)
+            nc.vector.tensor_copy(picked[:], window.indirect(listed(g * PAIR, PAIR)))
+            return picked
 
-        def gather_dy(g, parts_=(0, 1, 2), after=None):
-            for s in parts_:
-                if s < PASSES:
-                    got = tile([P, PAIR * C], U32, "dyg%d_%d" % (g, s), after)
-                    nc.vector.tensor_copy(got[:], dyw[:, s, :].bitcast(U32).indirect(listed(g * PAIR, PAIR)))
-                else:
-                    got = tile([P, PAIR * C], U8, "dysg%d" % g, after)
-                    nc.vector.tensor_copy(got[:], dys[:].indirect(listed(g * PAIR, PAIR)))
-                gathered[g, s] = got
+        def gather_pair(g):
+            xg = gather(xw[:].bitcast(U32), U32, "xg%d" % g, g)
+            xsg = gather(xs[:], U8, "xsg%d" % g, g)
+            dyg = [gather(dyw[:, s, :].bitcast(U32), U32, "dyg%d_%d" % (g, s), g) for s in range(PASSES)]
+            dysg = gather(dys[:], U8, "dysg%d" % g, g)
+            return xg, xsg, dyg, dysg
 
-        def banks_of(e):
-            return ((a1_bank, a3_bank), (spare_bank, dx_bank[1]), (a1_bank, a3_bank), (spare_bank, a3_bank))[e]
-
-        def first(e):
-            cols = slots(e % PAIR)
-            xg, xsg = tokens[e // PAIR]
-            for acc, w, ws in zip(banks_of(e), (w1, w3), (w1s, w3s)):
-                nc.tensor.matmul_mx(acc[:], lhsT=xg[:, cols].bitcast(X4), lhsT_scale=xsg[:, cols],
+        def recompute(e):
+            xg, xsg = gathered[e // PAIR][0:2]
+            own = slots(e % PAIR)
+            for acc, w, ws in ((a1_bank[e % 2], w1, w1s), (a3_bank[e], w3, w3s)):
+                nc.tensor.matmul_mx(acc[:], lhsT=xg[:, own].bitcast(X4), lhsT_scale=xsg[:, own],
                                     rhs=w[e][:].bitcast(X4), rhs_scale=ws[4 * e : P, :], start=True, stop=True)
 
         def gradient(e):
-            picked = [gathered[e // PAIR, s] for s in range(PASSES)]
-            picked_scales = gathered[e // PAIR, PASSES]
+            dyg, dysg = gathered[e // PAIR][2:4]
             own = slots(e % PAIR)
             for s in range(PASSES):
-                plane = PASSES * e + s
-                nc.tensor.matmul_mx(dh_bank[e % 2][:], lhsT=picked[s][:, own].bitcast(X4),
-                                    lhsT_scale=picked_scales[4 * s : P, own],
-                                    rhs=w2[e][:, s, :].bitcast(X4), rhs_scale=w2s[plane // 4][4 * (plane % 4) : P, :],
+                plane = PASSES * (e % PAIR) + s
+                nc.tensor.matmul_mx(dh_bank[e % 2][:], lhsT=dyg[s][:, own].bitcast(X4), lhsT_scale=dysg[4 * s : P, own],
+                                    rhs=w2[e][:, s, :].bitcast(X4), rhs_scale=w2s[e // PAIR][4 * plane : P, :],
                                     start=(s == 0), stop=(s == PASSES - 1))
 
-        def by_pair(sums, e):
-            if e in NATURAL:
-                return sums[:].rearrange("p (r m t) -> p r m t", r=2, t=2)
+        def by_pair(sums):
             return sums[:].rearrange("p (m r t) -> p r m t", r=2, t=2)
 
         def flat(values):
             return values[:].rearrange("p r m t -> p (r m t)")
 
-        def sigmoid(e):
-            sig = tile([P, 2, C, 2], F32, "sig%d" % e)
-            nc.scalar.activation(sig[:], by_pair(banks_of(e)[0], e), ACT.Sigmoid)
-            sigs[e] = sig
+        def values(name, e, dtype=F32, after=None):
+            return tile([P, 2, C, 2], dtype, "%s%d" % (name, e), after)
 
-        def slope(e):
-            a1, a3 = banks_of(e)
-            if e in U_POS:
-                rest = tile([P, 2, C, 2], F32, "rest%d" % e)
-                nc.scalar.activation(rest[:], by_pair(a1, e), ACT.Sigmoid, scale=-1.0)
-                u = tile([P, 2, C, 2], F32, "u%d" % e, U_AFTER.get(e))
-                nc.vector.tensor_tensor(u[:], by_pair(a3, e), rest[:], MULT)
-            elif e not in U_G:
-                u = tile([P, 2, C, 2], F32, "u%d" % e, U_AFTER.get(e))
-                if e in NATURAL:
-                    nc.vector.scalar_tensor_tensor(flat(u), flat(sigs[e]), 1.0, a3[:], SUB, MULT)
-                else:
-                    for r in range(2):
-                        nc.vector.scalar_tensor_tensor(u[:, r], sigs[e][:, r], 1.0, by_pair(a3, e)[:, r], SUB, MULT)
-            else:
-                rest = tile([P, 2, C, 2], F32, "rest%d" % e)
-                if e in REST_G:
-                    nc.gpsimd.tensor_scalar(flat(rest), flat(sigs[e]), -1.0, 1.0, MULT, ADD)
-                else:
-                    nc.scalar.activation(rest[:], by_pair(a1, e), ACT.Sigmoid, scale=-1.0)
-                a3_copy = tile([P, 2, C, 2], F32, "a3_copy%d" % e)
-                nc.scalar.copy(a3_copy[:], by_pair(a3, e))
-                parts[e] = (a3_copy, rest)
-                return
-            factors[e] = u
+        def sigmoid(e, name="sig", scale=1.0):
+            sig = values(name, e)
+            nc.scalar.activation(sig[:], by_pair(a1_bank[e % 2]), ACT.Sigmoid, scale=scale)
+            return sig
 
-        def slope_product(e):
-            a3_copy, rest = parts[e]
-            u = tile([P, 2, C, 2], F32, "u%d" % e, U_AFTER.get(e))
-            nc.gpsimd.tensor_tensor(flat(u), flat(a3_copy), flat(rest), MULT)
-            factors[e] = u
+        def minus_u(e, sig):
+            u = values("u", e)
+            for r in range(2):
+                nc.vector.scalar_tensor_tensor(u[:, r], sig[:, r], 1.0, by_pair(a3_bank[e])[:, r], SUB, MULT)
+            return u
 
-        def da3_tag(e):
-            return DA3_AFTER[e]
+        def make_da3(e, sig, after=None):
+            da3 = values("da3_", e, after=after)
+            for r in range(2):
+                nc.vector.scalar_tensor_tensor(
+                    da3[:, r], by_pair(dh_bank[e % 2])[:, r], gate_by_slot[:, e : e + 1], sig[:, r], MULT, MULT)
+            return da3
 
-        def product3(e):
-            sig = sigs[e]
-            da3 = tile([P, 2, C, 2], F32, "da3_%d" % e, da3_tag(e))
-            if e in NATURAL:
-                nc.vector.scalar_tensor_tensor(flat(da3), dh_bank[e % 2][:], gcol[:, e : e + 1], flat(sig), MULT, MULT)
-            else:
-                for r in range(2):
-                    nc.vector.scalar_tensor_tensor(
-                        da3[:, r], by_pair(dh_bank[e % 2], e)[:, r], gcol[:, e : e + 1], sig[:, r], MULT, MULT)
-            da3s[e] = da3
+        def da1_on_vector(e, da3, negative_u):
+            da1 = values("da1_", e, BF16)
+            nc.vector.scalar_tensor_tensor(flat(da1), flat(da3), -1.0, flat(negative_u), MULT, MULT)
+            return da1
 
-        def product1(e):
-            da3, u = da3s[e], factors[e]
-            da1 = tile([P, 2, C, 2], BF16, "da1_%d" % e, DA1_AFTER.get(e))
-            if e not in U_G and e not in U_POS:
-                nc.vector.scalar_tensor_tensor(flat(da1), flat(da3), -1.0, flat(u), MULT, MULT)
-            else:
-                (nc.gpsimd if e in DA1_G else nc.vector).tensor_tensor(flat(da1), flat(da3), flat(u), MULT)
-            made[e] = (da3, da1)
+        def da1_on_gpsimd(e, da3, u):
+            da1 = values("da1_", e, BF16)
+            nc.gpsimd.tensor_tensor(flat(da1), flat(da3), flat(u), MULT)
+            return da1
 
-        def turn(e):
-            da3, da1 = made[e]
-            da3_bank = bank[T3_BANK[e]]
+        def turn(e, da3, da1):
             rounded = tile([P, 2, C, 4], BF16, "rounded%d" % e)
             for d in range(4):
-                nc.tensor.transpose(da3_bank[:, d * C : (d + 1) * C], flat(da3)[:, d::4] if e in NATURAL else da3[:, d // 2, :, d % 2], ident[:])
+                nc.tensor.transpose(da3_bank[:, d * C : (d + 1) * C], da3[:, d // 2, :, d % 2], ident[:])
             nc.scalar.copy(rounded[:, 0], da3_bank[:].rearrange("p (d c) -> p c d", d=4))
             pairs = da1[:].rearrange("p r m t -> p r (m t)").bitcast(F32)
-            if e in NATURAL:
-                pairs = flat(da1).bitcast(F32).rearrange("p (m r) -> p r m", r=2)
             for r in range(2):
                 nc.tensor.transpose(da1_bank[:, r * C : (r + 1) * C], pairs[:, r, :], ident[:])
             nc.scalar.copy(rounded[:, 1].bitcast(F32), da1_bank[:, 0 : 2 * C].rearrange("p (r c) -> p c r", r=2))
             da_words = work.tile([P, 2 * C], U32, name="da_words", align_bytes=64)
             da_scales = work.tile([P, 2 * C], U8, name="da_scales", align_bytes=64)
             nc.vector.quantize_mx(da_words[:].bitcast(X4), da_scales[:], rounded[:].rearrange("p j c d -> p (j c d)"))
-            packed[e] = (da_words, da_scales)
+            return da_words, da_scales
 
-        def back(e, kts):
-            da_words, da_scales = packed[e]
-            for kt in kts:
+        def back(e, packed, row_tiles):
+            da_words, da_scales = packed
+            for kt in row_tiles:
                 kc = slice(kt * P, (kt + 1) * P)
                 for j, (w, ws) in enumerate(((w3t, w3ts), (w1t, w1ts))):
                     dc = slice(j * C, (j + 1) * C)
-                    nc.tensor.matmul_mx(dx_at[kt], lhsT=w[e][:, kc].bitcast(X4),
-                                        lhsT_scale=ws[4 * e : P, kc], rhs=da_words[:, dc].bitcast(X4),
-                                        rhs_scale=da_scales[:, dc], start=(j == 0), stop=(j == 1))
+                    nc.tensor.matmul_mx(dx_at[kt], lhsT=w[e][:, kc].bitcast(X4), lhsT_scale=ws[4 * e : P, kc],
+                                        rhs=da_words[:, dc].bitcast(X4), rhs_scale=da_scales[:, dc],
+                                        start=(j == 0), stop=(j == 1))
 
-        def drain(e, kts):
-            for kt in kts:
-                after = DX_AFTER.get((e, kt))
-                dx = tile([P, C], F32, "dx%d_%d" % (e, kt), after)
-                nc.scalar.copy(dx[:], dx_at[kt])
-                sums[e, kt] = dx
+        def drain(e, row_tiles):
+            for kt in row_tiles:
+                dx[kt] = tile([P, C], F32, "dx%d_%d" % (e, kt))
+                nc.scalar.copy(dx[kt][:], dx_at[kt])
 
-        def scatter(e, kts):
-            for kt in kts:
-                dx = sums[e, kt]
-                nc.vector.tensor_copy(rows[kt][:].indirect(listed(e)), dx[:])
+        def scatter(e, row_tiles):
+            for kt in row_tiles:
+                nc.vector.tensor_copy(rows[kt][:].indirect(listed(e)), dx[kt][:])
                 if e == LAST:
                     nc.sync.dma_start(out[kt * P : (kt + 1) * P, :], rows[kt][:])
 
-        gathered, sigs, factors, da3s, made, packed, sums, parts, tokens = {}, {}, {}, {}, {}, {}, {}, {}, {}
-        nc.tensor.transpose(da1_bank[:, 0:P], grows[:], ident[:])
-        nc.scalar.copy(gcol[:], da1_bank[:, 0:E])
-        gather_x(0)
-        gather_dy(0)
-        if not X_LATE:
-            gather_x(1)
-        gather_dy(1, [s for s in range(3) if s not in LATE_B and s not in LATE_C])
-        first(0)
+        def products(e):
+            recompute(e)
+            sig = sigmoid(e)
+            if e == LAST:
+                u = minus_u(e, sig)
+                gradient(e)
+                da3 = make_da3(e, sig)
+                return da3, da1_on_vector(e, da3, u)
+            rest = sigmoid(e, "rest", -1.0)
+            a3 = values("a3_copy", e)
+            nc.scalar.copy(a3[:], by_pair(a3_bank[e]))
+            u = values("u", e, after="rounded%d" % (e - 1))
+            nc.gpsimd.tensor_tensor(flat(u), flat(a3), flat(rest), MULT)
+            gradient(e)
+            da3 = make_da3(e, sig)
+            return da3, da1_on_gpsimd(e, da3, u)
+
+        nc.tensor.transpose(da1_bank[:, 0:P], gate_rows[:], ident[:])
+        nc.scalar.copy(gate_by_slot[:], da1_bank[:, 0:E])
+        gathered = [gather_pair(g) for g in range(E // PAIR)]
+
+        recompute(0)
         gradient(0)
-        sigmoid(0)
-        if P3_FIRST:
-            product3(0)
-        slope(0)
-        if not P3_FIRST:
-            product3(0)
-        product1(0)
-        first(1)
-        sigmoid(1)
-        slope(1)
-        turn(0)
-        if X_LATE:
-            gather_x(1, X_LATE)
-        for s in LATE_B:
-            gather_dy(1, [s], "da3_0")
+        sig0 = sigmoid(0)
+        u0 = minus_u(0, sig0)
+        da3_0 = make_da3(0, sig0)
+        da1_0 = da1_on_vector(0, da3_0, u0)
+        recompute(1)
+        sig1 = sigmoid(1)
+        rest1 = sigmoid(1, "rest", -1.0)
+        u1 = values("u", 1, after="u0")
+        nc.vector.tensor_tensor(u1[:], by_pair(a3_bank[1]), rest1[:], MULT)
+        packed = turn(0, da3_0, da1_0)
         gradient(1)
-        back(0, [0, 1])
-        product3(1)
-        product1(1)
-        for s in LATE_C:
-            gather_dy(1, [s], "sig1")
+        back(0, packed, range(ROW_TILES))
+        da3_1 = make_da3(1, sig1, after="rounded0")
+        made = {1: (da3_1, da1_on_gpsimd(1, da3_1, u1))}
+
+        dx = [None] * ROW_TILES
         for e in range(E):
-            before = BEFORE[e]
-            drain(e, [0, 1])
-            scatter(e, [0, 1])
-            back(e, [2, 3])
-            drain(e, range(2, before))
-            scatter(e, range(2, before))
-            if e in FIRST_EARLY:
-                first(e + 2)
-                sigmoid(e + 2)
-                slope(e + 2)
-            if e + 1 < E:
-                turn(e + 1)
-            drain(e, range(before, ROW_TILES))
-            if e + 2 < E:
-                if e not in FIRST_EARLY:
-                    first(e + 2)
-                    sigmoid(e + 2)
-                    slope(e + 2)
-                if e + 2 in U_G:
-                    slope_product(e + 2)
-                gradient(e + 2)
-                product3(e + 2)
-                product1(e + 2)
-            scatter(e, range(before, ROW_TILES))
-            if e + 1 < E:
-                back(e + 1, [0, 1])
+            held = 1 if e + 2 < E else 2 if e < LAST else 0
+            early, late = range(ROW_TILES - held), range(ROW_TILES - held, ROW_TILES)
+            for pair_of_tiles in (early[0:2], early[2:]):
+                drain(e, pair_of_tiles)
+                scatter(e, pair_of_tiles)
+            if e < LAST:
+                packed = turn(e + 1, *made[e + 1])
+                drain(e, late)
+                if e + 2 < E:
+                    made[e + 2] = products(e + 2)
+                scatter(e, late)
+                back(e + 1, packed, range(ROW_TILES))

@@ -23,6 +23,7 @@ ROW_TILES = K // P
 QUADRANTS = 4
 LAST = E - 1
 PAIR = 2
+LOW_ROWS = 2
 W1S_ON_GPSIMD, W2S_ON_GPSIMD, W3TS_ON_GPSIMD = 3, 2, 2
 W1TS_FIRST = 2
 
@@ -34,16 +35,22 @@ def tile_moe_rec_glu_sigmoid_kernel(
     nc = tc.nc
     with ExitStack() as ctx:
         keep = ctx.enter_context(tc.tile_pool(name="keep", bufs=1))
-        work = ctx.enter_context(tc.tile_pool(name="work", bufs=E))
         psum = ctx.enter_context(tc.psum_pool(name="psum", bufs=1))
         bank = [psum.tile([P, H], F32, name="bank%d" % b) for b in range(8)]
-        a1_bank, dh_bank = (bank[0], bank[4]), (bank[2], bank[3])
-        a3_bank = (bank[1], bank[7], bank[1], bank[1])
-        da3_bank, da1_bank = bank[6], bank[5]
-        dx_at = (da3_bank[:, 0:C], da1_bank[:, 0:C], da1_bank[:, 2 * C : 3 * C], da1_bank[:, 3 * C : 4 * C])
+        dh_bank, low_bank, shared = bank[3], bank[4:6], bank[6:8]
+        a1_bank = (bank[0], bank[1], shared[0], shared[1])
+        a3_bank = (bank[2], low_bank[1], bank[2], bank[0])
+        last_bank = (low_bank[LAST % 2], bank[1], bank[2], bank[0])
 
-        def tile(shape, dtype, name, after=None):
-            return keep.tile(shape, dtype, name=name, tag=after or name, align_bytes=64)
+        def dx_at(e, first, count=1):
+            if e == LAST:
+                return last_bank[first][:, 0:C]
+            if first < LOW_ROWS:
+                return low_bank[e % 2][:, first * C : (first + count) * C]
+            return shared[first - LOW_ROWS][:, 2 * C : 3 * C]
+
+        def tile(shape, dtype, name):
+            return keep.tile(shape, dtype, name=name, tag=name, align_bytes=64)
 
         offsets = keep.tile([P, T // 16], U16, name="offsets")
         xw = tile([P, T], I32, "xw")
@@ -55,13 +62,13 @@ def tile_moe_rec_glu_sigmoid_kernel(
         w2s = [tile([P, H], U8, "w2s%d" % g) for g in range(E // PAIR)]
         w1ts = tile([P, K], U8, "w1ts")
         w3ts = tile([P, K], U8, "w3ts")
-        gate_by_slot = keep.tile([P, E], F32, name="gate_by_slot")
+        gates = keep.tile([P, 2, E], F32, name="gates")
         gate_rows = tile([P, P], F32, "gate_rows")
         ident = tile([P, P], F32, "ident")
-        w1_pair = tile([P, PAIR, H], I32, "w1_pair")
-        w1 = [w1_pair[:, e, :] for e in range(PAIR)] + [tile([P, H], I32, "w1_%d" % e) for e in range(PAIR, E)]
-        w3_pair = tile([P, PAIR, H], I32, "w3_pair")
-        w3 = [w3_pair[:, e, :] for e in range(PAIR)] + [tile([P, H], I32, "w3_%d" % e) for e in range(PAIR, E)]
+        w1_pair = [tile([P, PAIR, H], I32, "w1_pair%d" % g) for g in range(E // PAIR)]
+        w3_pair = [tile([P, PAIR, H], I32, "w3_pair%d" % g) for g in range(E // PAIR)]
+        w1 = [w1_pair[e // PAIR][:, e % PAIR, :] for e in range(E)]
+        w3 = [w3_pair[e // PAIR][:, e % PAIR, :] for e in range(E)]
         w2 = [tile([P, PASSES, H], I32, "w2_%d" % e) for e in range(E)]
         w1t = [tile([P, K], I32, "w1t_%d" % e) for e in range(E)]
         w3t = [tile([P, K], I32, "w3t_%d" % e) for e in range(E)]
@@ -98,26 +105,26 @@ def tile_moe_rec_glu_sigmoid_kernel(
         load_pass(xw, x_words[0])
         load_planes(nc.sync, xs, x_scales)
         load_passes(dyw, dy_words)
-        load_passes(w1_pair, w1_words[0:PAIR, 0])
+        load_passes(w1_pair[0], w1_words[0:PAIR, 0])
         load_planes(nc.sync, w1s, w1_scales[:, 0], first=W1S_ON_GPSIMD)
         load_planes(nc.sync, dys, dy_scales)
-        load_passes(w3_pair, w3_words[0:PAIR, 0])
+        load_passes(w3_pair[0], w3_words[0:PAIR, 0])
         nc.sync.dma_start(gate_rows[0:E, :], gate[0].rearrange("(e c) -> e c", e=E))
         load_planes(nc.sync, w3s, w3_scales[:, 0])
         load_passes(w2[0], w2t_words[0])
         load_planes(nc.sync, w2s[0], w2_planes[0], first=W2S_ON_GPSIMD)
+        load_passes(w1_pair[1], w1_words[PAIR:E, 0])
         load_planes(nc.sync, w1ts, w1t_scales[:, 0], end=W1TS_FIRST)
         load_passes(w2[1], w2t_words[1])
         load_planes(nc.sync, w1ts, w1t_scales[:, 0], first=W1TS_FIRST)
+        load_pass(w1t[0], w1t_words[0, 0])
         load_planes(nc.sync, w3ts, w3t_scales[:, 0], first=W3TS_ON_GPSIMD)
-        load_back(0)
-        load_pass(w1[2], w1_words[2, 0])
         load_pass(w3[2], w3_words[2, 0])
+        load_pass(w3t[0], w3t_words[0, 0])
         load_planes(nc.sync, w2s[1], w2_planes[1])
         load_passes(w2[2], w2t_words[2])
-        load_pass(w1[3], w1_words[3, 0])
-        load_back(1)
         load_pass(w3[3], w3_words[3, 0])
+        load_back(1)
         load_passes(w2[3], w2t_words[3])
         load_back(2)
         load_back(3)
@@ -133,150 +140,142 @@ def tile_moe_rec_glu_sigmoid_kernel(
             nc.vector.tensor_copy(picked[:], window.indirect(listed(g * PAIR, PAIR)))
             return picked
 
+        tokens, grads = {}, {}
+
         def gather_pair(g):
-            xg = gather(xw[:].bitcast(U32), U32, "xg%d" % g, g)
-            xsg = gather(xs[:], U8, "xsg%d" % g, g)
+            tokens[g] = gather(xw[:].bitcast(U32), U32, "xg%d" % g, g), gather(xs[:], U8, "xsg%d" % g, g)
             dyg = [gather(dyw[:, s, :].bitcast(U32), U32, "dyg%d_%d" % (g, s), g) for s in range(PASSES)]
-            dysg = gather(dys[:], U8, "dysg%d" % g, g)
-            return xg, xsg, dyg, dysg
+            grads[g] = dyg, gather(dys[:], U8, "dysg%d" % g, g)
 
-        def recompute(e):
-            xg, xsg = gathered[e // PAIR][0:2]
+        def first_product(e, acc, w, ws):
+            xg, xsg = tokens[e // PAIR]
             own = slots(e % PAIR)
-            for acc, w, ws in ((a1_bank[e % 2], w1, w1s), (a3_bank[e], w3, w3s)):
-                nc.tensor.matmul_mx(acc[:], lhsT=xg[:, own].bitcast(X4), lhsT_scale=xsg[:, own],
-                                    rhs=w[e][:].bitcast(X4), rhs_scale=ws[4 * e : P, :], start=True, stop=True)
+            nc.tensor.matmul_mx(acc[:], lhsT=xg[:, own].bitcast(X4), lhsT_scale=xsg[:, own],
+                                rhs=w[e][:].bitcast(X4), rhs_scale=ws[4 * e : P, :], start=True, stop=True)
 
-        def gradient(e):
-            dyg, dysg = gathered[e // PAIR][2:4]
+        def make_dh(e):
+            dyg, dysg = grads[e // PAIR]
             own = slots(e % PAIR)
             for s in range(PASSES):
                 plane = PASSES * (e % PAIR) + s
-                nc.tensor.matmul_mx(dh_bank[e % 2][:], lhsT=dyg[s][:, own].bitcast(X4), lhsT_scale=dysg[4 * s : P, own],
+                nc.tensor.matmul_mx(dh_bank[:], lhsT=dyg[s][:, own].bitcast(X4), lhsT_scale=dysg[4 * s : P, own],
                                     rhs=w2[e][:, s, :].bitcast(X4), rhs_scale=w2s[e // PAIR][4 * plane : P, :],
                                     start=(s == 0), stop=(s == PASSES - 1))
 
         def by_pair(sums):
             return sums[:].rearrange("p (m r t) -> p r m t", r=2, t=2)
 
-        def flat(values):
-            return values[:].rearrange("p r m t -> p (r m t)")
+        def values(name, e):
+            return tile([P, 2, C, 2], F32, "%s%d" % (name, e))
 
-        def values(name, e, dtype=F32, after=None):
-            return tile([P, 2, C, 2], dtype, "%s%d" % (name, e), after)
+        sig, square, v, da, dx = {}, {}, {}, {}, {}
 
-        def sigmoid(e, name="sig", scale=1.0):
-            sig = values(name, e)
-            nc.scalar.activation(sig[:], by_pair(a1_bank[e % 2]), ACT.Sigmoid, scale=scale)
-            return sig
+        def sigmoid(e):
+            first_product(e, a1_bank[e], w1, w1s)
+            sig[e] = values("sig", e)
+            nc.scalar.activation(sig[e][:], by_pair(a1_bank[e]), ACT.Sigmoid)
+            square[e] = values("square", e)
+            flat = "p r m t -> p (r m t)"
+            nc.scalar.activation(square[e][:].rearrange(flat), sig[e][:].rearrange(flat), ACT.Square, bias=-0.5)
 
-        def minus_u(e, sig):
-            u = values("u", e)
+        def slope(e):
+            first_product(e, a3_bank[e], w3, w3s)
+            v[e] = values("v", e)
             for r in range(2):
-                nc.vector.scalar_tensor_tensor(u[:, r], sig[:, r], 1.0, by_pair(a3_bank[e])[:, r], SUB, MULT)
-            return u
+                nc.vector.scalar_tensor_tensor(v[e][:, r], square[e][:, r], 0.25, by_pair(a3_bank[e])[:, r], SUB, MULT)
 
-        def make_da3(e, sig, after=None):
-            da3 = values("da3_", e, after=after)
-            for r in range(2):
-                nc.vector.scalar_tensor_tensor(
-                    da3[:, r], by_pair(dh_bank[e % 2])[:, r], gate_by_slot[:, e : e + 1], sig[:, r], MULT, MULT)
-            return da3
+        def make_da(e):
+            da[e] = tile([P, 2, 2, C, 2], BF16, "da%d" % e)
+            for j, factor in enumerate((sig[e], v[e])):
+                for r in range(2):
+                    nc.vector.scalar_tensor_tensor(da[e][:, j, r], by_pair(dh_bank)[:, r],
+                                                   gates[:, j, e : e + 1], factor[:, r], MULT, MULT)
 
-        def da1_on_vector(e, da3, negative_u):
-            da1 = values("da1_", e, BF16)
-            nc.vector.scalar_tensor_tensor(flat(da1), flat(da3), -1.0, flat(negative_u), MULT, MULT)
-            return da1
+        def turn(e):
+            pairs = da[e][:].rearrange("p j r m t -> p (j r) (m t)").bitcast(F32)
+            for q in range(4):
+                nc.tensor.transpose(shared[q // 2][:, (q % 2) * C : (q % 2 + 1) * C], pairs[:, q, :], ident[:])
 
-        def da1_on_gpsimd(e, da3, u):
-            da1 = values("da1_", e, BF16)
-            nc.gpsimd.tensor_tensor(flat(da1), flat(da3), flat(u), MULT)
-            return da1
+        rounded, packed = {}, {}
 
-        def turn(e, da3, da1):
-            rounded = tile([P, 2, C, 4], BF16, "rounded%d" % e)
-            for d in range(4):
-                nc.tensor.transpose(da3_bank[:, d * C : (d + 1) * C], da3[:, d // 2, :, d % 2], ident[:])
-            nc.scalar.copy(rounded[:, 0], da3_bank[:].rearrange("p (d c) -> p c d", d=4))
-            pairs = da1[:].rearrange("p r m t -> p r (m t)").bitcast(F32)
-            for r in range(2):
-                nc.tensor.transpose(da1_bank[:, r * C : (r + 1) * C], pairs[:, r, :], ident[:])
-            nc.scalar.copy(rounded[:, 1].bitcast(F32), da1_bank[:, 0 : 2 * C].rearrange("p (r c) -> p c r", r=2))
-            da_words = work.tile([P, 2 * C], U32, name="da_words", align_bytes=64)
-            da_scales = work.tile([P, 2 * C], U8, name="da_scales", align_bytes=64)
-            nc.vector.quantize_mx(da_words[:].bitcast(X4), da_scales[:], rounded[:].rearrange("p j c d -> p (j c d)"))
-            return da_words, da_scales
+        def copy_da(e):
+            rounded[e] = tile([P, 2, C, 4], BF16, "rounded%d" % e)
+            for j in range(2):
+                nc.vector.tensor_copy(rounded[e][:, j].bitcast(F32),
+                                      shared[j][:, 0 : 2 * C].rearrange("p (r c) -> p c r", r=2))
 
-        def back(e, packed, row_tiles):
-            da_words, da_scales = packed
+        def quantise(e):
+            da_words = tile([P, 2 * C], U32, "da_words%d" % e)
+            da_scales = tile([P, 2 * C], U8, "da_scales%d" % e)
+            nc.vector.quantize_mx(da_words[:].bitcast(X4), da_scales[:],
+                                  rounded[e][:].rearrange("p j c d -> p (j c d)"))
+            packed[e] = da_words, da_scales
+
+        def back(e, row_tiles):
+            da_words, da_scales = packed[e]
             for kt in row_tiles:
                 kc = slice(kt * P, (kt + 1) * P)
                 for j, (w, ws) in enumerate(((w3t, w3ts), (w1t, w1ts))):
                     dc = slice(j * C, (j + 1) * C)
-                    nc.tensor.matmul_mx(dx_at[kt], lhsT=w[e][:, kc].bitcast(X4), lhsT_scale=ws[4 * e : P, kc],
+                    nc.tensor.matmul_mx(dx_at(e, kt), lhsT=w[e][:, kc].bitcast(X4), lhsT_scale=ws[4 * e : P, kc],
                                         rhs=da_words[:, dc].bitcast(X4), rhs_scale=da_scales[:, dc],
                                         start=(j == 0), stop=(j == 1))
 
-        def drain(e, row_tiles):
-            for kt in row_tiles:
-                dx[kt] = tile([P, C], F32, "dx%d_%d" % (e, kt))
-                nc.scalar.copy(dx[kt][:], dx_at[kt])
+        def drain(e, first, count, on_vector):
+            sums = tile([P, count * C], F32, "dx%d_%d" % (e, first))
+            if on_vector:
+                nc.vector.tensor_copy(sums[:], dx_at(e, first, count))
+            else:
+                nc.scalar.copy(sums[:], dx_at(e, first, count))
+            for n in range(count):
+                dx[e, first + n] = sums[:, n * C : (n + 1) * C]
 
-        def scatter(e, row_tiles):
-            for kt in row_tiles:
-                nc.vector.tensor_copy(rows[kt][:].indirect(listed(e)), dx[kt][:])
-                if e == LAST:
-                    nc.sync.dma_start(out[kt * P : (kt + 1) * P, :], rows[kt][:])
-
-        def products(e):
-            recompute(e)
-            sig = sigmoid(e)
+        def scatter(e, kt, on_vector):
+            if on_vector:
+                nc.vector.tensor_copy(rows[kt][:].indirect(listed(e)), dx[e, kt])
+            else:
+                nc.scalar.activation(rows[kt][:].indirect(listed(e)), dx[e, kt], ACT.Copy)
             if e == LAST:
-                u = minus_u(e, sig)
-                gradient(e)
-                da3 = make_da3(e, sig)
-                return da3, da1_on_vector(e, da3, u)
-            rest = sigmoid(e, "rest", -1.0)
-            a3 = values("a3_copy", e)
-            nc.scalar.copy(a3[:], by_pair(a3_bank[e]))
-            u = values("u", e, after="rounded%d" % (e - 1))
-            nc.gpsimd.tensor_tensor(flat(u), flat(a3), flat(rest), MULT)
-            gradient(e)
-            da3 = make_da3(e, sig)
-            return da3, da1_on_gpsimd(e, da3, u)
+                nc.sync.dma_start(out[kt * P : (kt + 1) * P, :], rows[kt][:])
 
-        nc.tensor.transpose(da1_bank[:, 0:P], gate_rows[:], ident[:])
-        nc.scalar.copy(gate_by_slot[:], da1_bank[:, 0:E])
-        gathered = [gather_pair(g) for g in range(E // PAIR)]
+        nc.tensor.transpose(low_bank[0][:, 0:P], gate_rows[:], ident[:])
+        nc.scalar.copy(gates[:, 0, :], low_bank[0][:, 0:E])
+        nc.scalar.mul(gates[:, 1, :], low_bank[0][:, 0:E], -1.0)
+        for g in range(E // PAIR):
+            gather_pair(g)
 
-        recompute(0)
-        gradient(0)
-        sig0 = sigmoid(0)
-        u0 = minus_u(0, sig0)
-        da3_0 = make_da3(0, sig0)
-        da1_0 = da1_on_vector(0, da3_0, u0)
-        recompute(1)
-        sig1 = sigmoid(1)
-        rest1 = sigmoid(1, "rest", -1.0)
-        u1 = values("u", 1, after="u0")
-        nc.vector.tensor_tensor(u1[:], by_pair(a3_bank[1]), rest1[:], MULT)
-        packed = turn(0, da3_0, da1_0)
-        gradient(1)
-        back(0, packed, range(ROW_TILES))
-        da3_1 = make_da3(1, sig1, after="rounded0")
-        made = {1: (da3_1, da1_on_gpsimd(1, da3_1, u1))}
-
-        dx = [None] * ROW_TILES
+        for e in range(PAIR):
+            sigmoid(e)
+            slope(e)
+        make_dh(0)
+        for e in range(PAIR, E):
+            sigmoid(e)
         for e in range(E):
-            held = 1 if e + 2 < E else 2 if e < LAST else 0
-            early, late = range(ROW_TILES - held), range(ROW_TILES - held, ROW_TILES)
-            for pair_of_tiles in (early[0:2], early[2:]):
-                drain(e, pair_of_tiles)
-                scatter(e, pair_of_tiles)
-            if e < LAST:
-                packed = turn(e + 1, *made[e + 1])
-                drain(e, late)
-                if e + 2 < E:
-                    made[e + 2] = products(e + 2)
-                scatter(e, late)
-                back(e + 1, packed, range(ROW_TILES))
+            before = e - 1
+            if e > 0:
+                make_dh(e)
+            make_da(e)
+            if 0 < e < LAST:
+                slope(e + 1)
+            if e > 0:
+                back(before, range(ROW_TILES))
+                if before == 0:
+                    for kt in range(LOW_ROWS):
+                        drain(before, kt, 1, False)
+                else:
+                    drain(before, 0, LOW_ROWS, e == LAST)
+            turn(e)
+            copy_da(e)
+            if e > 0:
+                for kt in range(LOW_ROWS, ROW_TILES):
+                    drain(before, kt, 1, True)
+            quantise(e)
+            if e > 0:
+                for kt in range(ROW_TILES):
+                    scatter(before, kt, e == LAST and kt >= LOW_ROWS)
+        in_turn = (2, 0, 3, 1)
+        back(LAST, in_turn)
+        for kt in in_turn:
+            drain(LAST, kt, 1, kt >= LOW_ROWS)
+        for kt in in_turn:
+            scatter(LAST, kt, kt >= LOW_ROWS)

from contextlib import ExitStack

import concourse.mybir as mybir
from concourse.masks import make_identity

K, T, E, C, H, N = 512, 512, 4, 128, 512, 1024
FLOPS = 1610612736

F32 = mybir.dt.float32
BF16 = mybir.dt.bfloat16
I32 = mybir.dt.int32
U32 = mybir.dt.uint32
U16 = mybir.dt.uint16
U8 = mybir.dt.uint8
X4 = mybir.dt.float8_e4m3fn_x4
ACT = mybir.ActivationFunctionType
MULT = mybir.AluOpType.mult
SUB = mybir.AluOpType.subtract

P = 128
PASSES = N // 512
ROW_TILES = K // P
QUADRANTS = 4
LAST = E - 1
PAIR = 2
LOW_ROWS = 2
W1S_ON_GPSIMD, W2S_ON_GPSIMD, W3TS_ON_GPSIMD = 3, 2, 2
W1TS_FIRST = 2


def tile_moe_rec_glu_sigmoid_kernel(
    tc, x_words, x_scales, dy_words, dy_scales, w1_words, w1_scales, w3_words, w3_scales,
    w2t_words, w2t_scales, w1t_words, w1t_scales, w3t_words, w3t_scales, gate, offs, out,
):
    nc = tc.nc
    with ExitStack() as ctx:
        keep = ctx.enter_context(tc.tile_pool(name="keep", bufs=1))
        psum = ctx.enter_context(tc.psum_pool(name="psum", bufs=1))
        bank = [psum.tile([P, H], F32, name="bank%d" % b) for b in range(8)]
        dh_bank, low_bank, shared = bank[3], bank[4:6], bank[6:8]
        a1_bank = (bank[0], bank[1], shared[0], shared[1])
        a3_bank = (bank[2], low_bank[1], bank[2], bank[0])
        last_bank = (low_bank[LAST % 2], bank[1], bank[2], bank[0])

        def dx_at(e, first, count=1):
            if e == LAST:
                return last_bank[first][:, 0:C]
            if first < LOW_ROWS:
                return low_bank[e % 2][:, first * C : (first + count) * C]
            return shared[first - LOW_ROWS][:, 2 * C : 3 * C]

        def tile(shape, dtype, name):
            return keep.tile(shape, dtype, name=name, tag=name, align_bytes=64)

        offsets = keep.tile([P, T // 16], U16, name="offsets")
        xw = tile([P, T], I32, "xw")
        dyw = tile([P, PASSES, T], I32, "dyw")
        xs = tile([P, T], U8, "xs")
        dys = tile([P, T], U8, "dys")
        w1s = tile([P, H], U8, "w1s")
        w3s = tile([P, H], U8, "w3s")
        w2s = [tile([P, H], U8, "w2s%d" % g) for g in range(E // PAIR)]
        w1ts = tile([P, K], U8, "w1ts")
        w3ts = tile([P, K], U8, "w3ts")
        gates = keep.tile([P, 2, E], F32, name="gates")
        gate_rows = tile([P, P], F32, "gate_rows")
        ident = tile([P, P], F32, "ident")
        w1_pair = [tile([P, PAIR, H], I32, "w1_pair%d" % g) for g in range(E // PAIR)]
        w3_pair = [tile([P, PAIR, H], I32, "w3_pair%d" % g) for g in range(E // PAIR)]
        w1 = [w1_pair[e // PAIR][:, e % PAIR, :] for e in range(E)]
        w3 = [w3_pair[e // PAIR][:, e % PAIR, :] for e in range(E)]
        w2 = [tile([P, PASSES, H], I32, "w2_%d" % e) for e in range(E)]
        w1t = [tile([P, K], I32, "w1t_%d" % e) for e in range(E)]
        w3t = [tile([P, K], I32, "w3t_%d" % e) for e in range(E)]
        rows = [tile([P, T], F32, "rows%d" % kt) for kt in range(ROW_TILES)]

        def load_pass(dst, src):
            nc.sync.dma_start(dst[:], src.rearrange("p n d -> p (n d)").bitcast(I32))

        def load_passes(dst, src):
            nc.sync.dma_start(dst[:], src.rearrange("s p n d -> p s (n d)").bitcast(I32))

        def load_planes(eng, dst, planes, first=0, end=QUADRANTS):
            count = planes.shape[0]
            for q in range(first, end):
                eng.dma_start(dst[32 * q : 32 * q + 4 * count, :].bitcast(I32),
                              planes[:, 4 * q : 4 * q + 4, :].bitcast(I32))

        def load_back(e):
            load_pass(w1t[e], w1t_words[e, 0])
            load_pass(w3t[e], w3t_words[e, 0])

        nc.gpsimd.memset(w1s[:].bitcast(I32), 0)
        for planes in (xs, dys, w3s, w2s[0], w3ts, w1ts, w2s[1]):
            nc.vector.memset(planes[:].bitcast(I32), 0)
        nc.vector.memset(gate_rows[:], 0.0)

        w2_planes = w2t_scales.rearrange("(g e) s b n -> g (e s) b n", e=PAIR)
        load_planes(nc.gpsimd, w1s, w1_scales[:, 0], end=W1S_ON_GPSIMD)
        load_planes(nc.gpsimd, w2s[0], w2_planes[0], end=W2S_ON_GPSIMD)
        make_identity(nc, ident[:])
        load_planes(nc.gpsimd, w3ts, w3t_scales[:, 0], end=W3TS_ON_GPSIMD)

        nc.sync.dma_start(offsets[:], offs)
        load_pass(xw, x_words[0])
        load_planes(nc.sync, xs, x_scales)
        load_passes(dyw, dy_words)
        load_passes(w1_pair[0], w1_words[0:PAIR, 0])
        load_planes(nc.sync, w1s, w1_scales[:, 0], first=W1S_ON_GPSIMD)
        load_planes(nc.sync, dys, dy_scales)
        load_passes(w3_pair[0], w3_words[0:PAIR, 0])
        nc.sync.dma_start(gate_rows[0:E, :], gate[0].rearrange("(e c) -> e c", e=E))
        load_planes(nc.sync, w3s, w3_scales[:, 0])
        load_passes(w2[0], w2t_words[0])
        load_planes(nc.sync, w2s[0], w2_planes[0], first=W2S_ON_GPSIMD)
        load_passes(w1_pair[1], w1_words[PAIR:E, 0])
        load_planes(nc.sync, w1ts, w1t_scales[:, 0], end=W1TS_FIRST)
        load_passes(w2[1], w2t_words[1])
        load_planes(nc.sync, w1ts, w1t_scales[:, 0], first=W1TS_FIRST)
        load_pass(w1t[0], w1t_words[0, 0])
        load_planes(nc.sync, w3ts, w3t_scales[:, 0], first=W3TS_ON_GPSIMD)
        load_pass(w3[2], w3_words[2, 0])
        load_pass(w3t[0], w3t_words[0, 0])
        load_planes(nc.sync, w2s[1], w2_planes[1])
        load_passes(w2[2], w2t_words[2])
        load_pass(w3[3], w3_words[3, 0])
        load_back(1)
        load_passes(w2[3], w2t_words[3])
        load_back(2)
        load_back(3)

        def slots(e):
            return slice(e * C, (e + 1) * C)

        def listed(first_expert, experts=1):
            return offsets[:, first_expert * C // 16 : (first_expert + experts) * C // 16]

        def gather(window, dtype, name, g):
            picked = tile([P, PAIR * C], dtype, name)
            nc.vector.tensor_copy(picked[:], window.indirect(listed(g * PAIR, PAIR)))
            return picked

        tokens, grads = {}, {}

        def gather_pair(g):
            tokens[g] = gather(xw[:].bitcast(U32), U32, "xg%d" % g, g), gather(xs[:], U8, "xsg%d" % g, g)
            dyg = [gather(dyw[:, s, :].bitcast(U32), U32, "dyg%d_%d" % (g, s), g) for s in range(PASSES)]
            grads[g] = dyg, gather(dys[:], U8, "dysg%d" % g, g)

        def first_product(e, acc, w, ws):
            xg, xsg = tokens[e // PAIR]
            own = slots(e % PAIR)
            nc.tensor.matmul_mx(acc[:], lhsT=xg[:, own].bitcast(X4), lhsT_scale=xsg[:, own],
                                rhs=w[e][:].bitcast(X4), rhs_scale=ws[4 * e : P, :], start=True, stop=True)

        def make_dh(e):
            dyg, dysg = grads[e // PAIR]
            own = slots(e % PAIR)
            for s in range(PASSES):
                plane = PASSES * (e % PAIR) + s
                nc.tensor.matmul_mx(dh_bank[:], lhsT=dyg[s][:, own].bitcast(X4), lhsT_scale=dysg[4 * s : P, own],
                                    rhs=w2[e][:, s, :].bitcast(X4), rhs_scale=w2s[e // PAIR][4 * plane : P, :],
                                    start=(s == 0), stop=(s == PASSES - 1))

        def by_pair(sums):
            return sums[:].rearrange("p (m r t) -> p r m t", r=2, t=2)

        def values(name, e):
            return tile([P, 2, C, 2], F32, "%s%d" % (name, e))

        sig, square, v, da, dx = {}, {}, {}, {}, {}

        def sigmoid(e):
            first_product(e, a1_bank[e], w1, w1s)
            sig[e] = values("sig", e)
            nc.scalar.activation(sig[e][:], by_pair(a1_bank[e]), ACT.Sigmoid)
            square[e] = values("square", e)
            flat = "p r m t -> p (r m t)"
            nc.scalar.activation(square[e][:].rearrange(flat), sig[e][:].rearrange(flat), ACT.Square, bias=-0.5)

        def slope(e):
            first_product(e, a3_bank[e], w3, w3s)
            v[e] = values("v", e)
            for r in range(2):
                nc.vector.scalar_tensor_tensor(v[e][:, r], square[e][:, r], 0.25, by_pair(a3_bank[e])[:, r], SUB, MULT)

        def make_da(e):
            da[e] = tile([P, 2, 2, C, 2], BF16, "da%d" % e)
            for j, factor in enumerate((sig[e], v[e])):
                for r in range(2):
                    nc.vector.scalar_tensor_tensor(da[e][:, j, r], by_pair(dh_bank)[:, r],
                                                   gates[:, j, e : e + 1], factor[:, r], MULT, MULT)

        def turn(e):
            pairs = da[e][:].rearrange("p j r m t -> p (j r) (m t)").bitcast(F32)
            for q in range(4):
                nc.tensor.transpose(shared[q // 2][:, (q % 2) * C : (q % 2 + 1) * C], pairs[:, q, :], ident[:])

        rounded, packed = {}, {}

        def copy_da(e):
            rounded[e] = tile([P, 2, C, 4], BF16, "rounded%d" % e)
            for j in range(2):
                nc.vector.tensor_copy(rounded[e][:, j].bitcast(F32),
                                      shared[j][:, 0 : 2 * C].rearrange("p (r c) -> p c r", r=2))

        def quantise(e):
            da_words = tile([P, 2 * C], U32, "da_words%d" % e)
            da_scales = tile([P, 2 * C], U8, "da_scales%d" % e)
            nc.vector.quantize_mx(da_words[:].bitcast(X4), da_scales[:],
                                  rounded[e][:].rearrange("p j c d -> p (j c d)"))
            packed[e] = da_words, da_scales

        def back(e, row_tiles):
            da_words, da_scales = packed[e]
            for kt in row_tiles:
                kc = slice(kt * P, (kt + 1) * P)
                for j, (w, ws) in enumerate(((w3t, w3ts), (w1t, w1ts))):
                    dc = slice(j * C, (j + 1) * C)
                    nc.tensor.matmul_mx(dx_at(e, kt), lhsT=w[e][:, kc].bitcast(X4), lhsT_scale=ws[4 * e : P, kc],
                                        rhs=da_words[:, dc].bitcast(X4), rhs_scale=da_scales[:, dc],
                                        start=(j == 0), stop=(j == 1))

        def drain(e, first, count, on_vector):
            sums = tile([P, count * C], F32, "dx%d_%d" % (e, first))
            if on_vector:
                nc.vector.tensor_copy(sums[:], dx_at(e, first, count))
            else:
                nc.scalar.copy(sums[:], dx_at(e, first, count))
            for n in range(count):
                dx[e, first + n] = sums[:, n * C : (n + 1) * C]

        def scatter(e, kt, on_vector):
            if on_vector:
                nc.vector.tensor_copy(rows[kt][:].indirect(listed(e)), dx[e, kt])
            else:
                nc.scalar.activation(rows[kt][:].indirect(listed(e)), dx[e, kt], ACT.Copy)
            if e == LAST:
                nc.sync.dma_start(out[kt * P : (kt + 1) * P, :], rows[kt][:])

        nc.tensor.transpose(low_bank[0][:, 0:P], gate_rows[:], ident[:])
        nc.scalar.copy(gates[:, 0, :], low_bank[0][:, 0:E])
        nc.scalar.mul(gates[:, 1, :], low_bank[0][:, 0:E], -1.0)
        for g in range(E // PAIR):
            gather_pair(g)

        for e in range(PAIR):
            sigmoid(e)
            slope(e)
        make_dh(0)
        for e in range(PAIR, E):
            sigmoid(e)
        for e in range(E):
            before = e - 1
            if e > 0:
                make_dh(e)
            make_da(e)
            if 0 < e < LAST:
                slope(e + 1)
            if e > 0:
                back(before, range(ROW_TILES))
                if before == 0:
                    for kt in range(LOW_ROWS):
                        drain(before, kt, 1, False)
                else:
                    drain(before, 0, LOW_ROWS, e == LAST)
            turn(e)
            copy_da(e)
            if e > 0:
                for kt in range(LOW_ROWS, ROW_TILES):
                    drain(before, kt, 1, True)
            quantise(e)
            if e > 0:
                for kt in range(ROW_TILES):
                    scatter(before, kt, e == LAST and kt >= LOW_ROWS)
        in_turn = (2, 0, 3, 1)
        back(LAST, in_turn)
        for kt in in_turn:
            drain(LAST, kt, 1, kt >= LOW_ROWS)
        for kt in in_turn:
            scatter(LAST, kt, kt >= LOW_ROWS)
